import numpy as np
import ml_dtypes


def mxq(x, axis, fmt="e4m3"):
    dtype, down = {"e4m3": (ml_dtypes.float8_e4m3fn, 7), "e5m2": (ml_dtypes.float8_e5m2, 14)}[fmt]
    v = np.moveaxis(np.asarray(x, np.float32).astype(ml_dtypes.bfloat16).astype(np.float64), axis, -1)
    blocks = v.reshape(v.shape[:-1] + (-1, 32))
    amax = np.abs(blocks).max(-1, keepdims=True)
    byte = np.maximum(np.where(amax > 0, np.frexp(amax)[1] - 1 + 127, 0) - down, 1)
    scale = np.exp2(byte - 127.0)
    codes = (blocks / scale).astype(np.float32).astype(dtype).astype(np.float64)
    return np.moveaxis((codes * scale).reshape(v.shape), -1, axis)


WIDE = False


def mx_kscale(k):
    if not WIDE:
        return np.ones(k)
    levels = np.array([24, -24, 12, -12, 0])
    if k % 512:
        return np.exp2(np.random.permutation(np.resize(levels, k // 32))).repeat(32)
    a = np.empty((k // 512, 16))
    for p in range(k // 512):
        a[p, :8] = np.random.permutation(np.resize(levels, 8))
        for g in range(8):
            far = levels[np.abs(levels - a[p, g]) >= 10]
            a[p, g + 8] = far[np.random.randint(len(far))]
    return np.exp2(a.ravel()).repeat(32)


def f64(x):
    return np.asarray(x).astype(np.float64)


def striped(idx):
    return np.tile(idx.reshape(-1, 16).T, (8, 1)).astype(np.uint16)


def unstriped(offs):
    return offs[:16].T.reshape(-1).astype(np.int64)


E2M1 = np.array([0.0, 0.5, 1.0, 1.5, 2.0, 3.0, 4.0, 6.0, -0.0, -0.5, -1.0, -1.5, -2.0, -3.0, -4.0, -6.0])


def pack_weight(w, fmt):
    k, n = w.shape
    w = f64(np.asarray(w, np.float32).astype(ml_dtypes.bfloat16)).reshape(k // 32, 32, n)
    amax = np.abs(w).max(1)
    if fmt == "e4m3":
        byte = np.frexp(amax)[1] - 1 + 127 - 7
    else:
        mant, ex = np.frexp(amax / 6.0)
        byte = np.where(mant > 0.5, ex, ex - 1) + 127
    byte = np.clip(np.where(amax > 0, byte, 1), 1, 254)
    scaled = (w * np.exp2(127.0 - byte)[:, None, :]).reshape(k, n).astype(np.float32)
    by_word = np.ascontiguousarray(scaled.reshape(k // 512, 128, 4, n).transpose(0, 1, 3, 2))
    if fmt == "e4m3":
        words = by_word.astype(ml_dtypes.float8_e4m3fn).view(np.uint8)
    else:
        c = by_word.astype(ml_dtypes.float4_e2m1fn).view(np.uint8) & 0xF
        words = (c[..., 0::2] | (c[..., 1::2] << 4)).reshape(k // 512, 128, 2 * n)
    return np.ascontiguousarray(words), np.ascontiguousarray(byte.astype(np.uint8).reshape(k // 512, 16, n))


def unpack_weight(words, scales, fmt):
    g, _, n = scales.shape
    words = np.ascontiguousarray(words).reshape(g, 128, n, -1)
    if fmt == "e4m3":
        vals = words.view(ml_dtypes.float8_e4m3fn).astype(np.float64)
    else:
        nib = np.empty((g, 128, n, 4), np.uint8)
        nib[..., 0::2] = words & 0xF
        nib[..., 1::2] = words >> 4
        vals = E2M1[nib]
    vals = vals * np.repeat(np.exp2(scales.astype(np.float64) - 127.0), 8, axis=1)[..., None]
    return vals.transpose(0, 1, 3, 2).reshape(g * 512, n)


def pack_table4(v):
    words, scales = pack_weight(v, "e2m1")
    g, t = words.shape[0] // 2, v.shape[1]
    return np.ascontiguousarray(words.reshape(g, 2, 128, t, 2).transpose(0, 2, 3, 1, 4).reshape(g, 128, t, 4)), scales


def unpack_table4(words, scales):
    g, _, t, _ = words.shape
    return unpack_weight(words.reshape(g, 128, t, 2, 2).transpose(0, 3, 1, 2, 4).reshape(2 * g, 128, 2 * t), scales, "e2m1")


K, R, T, M, J = 1024, 1024, 2048, 512, 1024


def setup_inputs():
    n = np.random.standard_normal
    s = mx_kscale(K)[:, None]
    u = mx_kscale(R)[:, None]
    p_tab = pack_table4(n((K, T)) * s)
    p_wb = pack_weight(n((K, R)) / np.sqrt(K) / s, "e2m1")
    return {
        "tab_words": p_tab[0],
        "tab_scales": p_tab[1],
        "wa": (n((K, R)) / np.sqrt(K) / s).astype(np.float32),
        "wb_words": p_wb[0],
        "wb_scales": p_wb[1],
        "sa": (np.random.uniform(0.5, 2.0, R) * u[:, 0]).astype(np.float32),
        "sb": (np.random.uniform(0.5, 2.0, R) / u[:, 0]).astype(np.float32),
        "offs": striped(np.random.permutation(T)[:M]),
        "offs2": striped(np.random.permutation(T)[:J]),
    }


def reference(tab_words, tab_scales, wa, wb_words, wb_scales, sa, sb, offs, offs2):
    idx = unstriped(offs)
    idx2 = unstriped(offs2)
    tab_ = unpack_table4(tab_words, tab_scales)[:, idx]
    tabb_ = unpack_table4(tab_words, tab_scales)[:, idx2]
    wa_ = mxq(f64(wa), 0, "e4m3")
    wb_ = unpack_weight(wb_words, wb_scales, "e2m1")
    za = wa_.T @ tab_
    zb = wb_.T @ tabb_
    ha = f64(sa)[:, None] * np.tanh(za)
    hb = f64(sb)[:, None] * np.tanh(zb)
    ha_ = mxq(ha, 0, "e4m3")
    hb_ = mxq(hb, 0, "e4m3")
    y = ha_.T @ hb_
    return np.exp(y * 0.015625)

@@ -1,0 +1,240 @@
+from contextlib import ExitStack
+
+import concourse.mybir as mybir
+from concourse.masks import make_identity
+
+K, R, T, M, J = 1024, 1024, 2048, 512, 1024
+FLOPS = 2 * K * R * (M + J) + 2 * R * M * J
+
+F32 = mybir.dt.float32
+BF16 = mybir.dt.bfloat16
+I32 = mybir.dt.int32
+U32 = mybir.dt.uint32
+U16 = mybir.dt.uint16
+U8 = mybir.dt.uint8
+FP8X4 = mybir.dt.float8_e4m3fn_x4
+FP4X4 = mybir.dt.float4_e2m1fn_x4
+ACT = mybir.ActivationFunctionType
+MULT = mybir.AluOpType.mult
+
+P = 128
+PACK = 4
+PASSES = 2
+CHUNK = 128
+HALF = 512
+B_FIRST = 5
+
+
+def tile_list_biaff_tanh_exp_kernel(
+    tc, tab_words, tab_scales, wa, wb_words, wb_scales, sa, sb, offs, offs2, out
+):
+    nc = tc.nc
+    with ExitStack() as ctx:
+        keep = ctx.enter_context(tc.tile_pool(name="keep", bufs=1))
+        ring = ctx.enter_context(tc.tile_pool(name="ring", bufs=3))
+        psum = ctx.enter_context(tc.psum_pool(name="psum", bufs=1))
+
+        list_b = keep.tile([P, J // 16], U16)
+        list_a = keep.tile([P, M // 16], U16)
+        tab_s = keep.tile([P, T], U8, align_bytes=64, tag="early")
+        wb_raw_s = keep.tile([P, PASSES, R], U8, align_bytes=64)
+        gain_raw = keep.tile([2, R], F32, align_bytes=64, tag="then_wb")
+        gain_rows = keep.tile([P, 2, PACK, P], F32)
+        ident = keep.tile([P, P], F32)
+        warm = keep.tile([P, 8], F32, align_bytes=64, tag="then_tab")
+        s0_first = keep.tile([P, HALF], U8, align_bytes=64)
+        s1_first = keep.tile([P, HALF], U8, align_bytes=64)
+        s0_rest = keep.tile([P, 2 * HALF], U8, align_bytes=64)
+        s1_rest = keep.tile([P, 2 * HALF], U8, align_bytes=64)
+
+        nc.vector.memset(tab_s[:].bitcast(I32), 0)
+        nc.vector.memset(warm[:], 0.0)
+        nc.gpsimd.memset(gain_rows[:], 0.0)
+        make_identity(nc, ident[:])
+        nc.gpsimd.memset(wb_raw_s[:].bitcast(I32), 0)
+        nc.vector.memset(s1_first[:].bitcast(I32), 0)
+        nc.vector.memset(s1_rest[:].bitcast(I32), 0)
+        nc.scalar.activation(warm[:], warm[:], ACT.Exp)
+
+        nc.sync.dma_start(list_b[:], offs2)
+        nc.sync.dma_start(list_a[:], offs)
+        for row, vec in enumerate((sa, sb)):
+            nc.sync.dma_start(gain_raw[row : row + 1, :], vec.rearrange("(o r) -> o r", o=1))
+        for q in range(4):
+            nc.sync.dma_start(tab_s[32 * q : 32 * q + 8, :].bitcast(I32), tab_scales[:, 4 * q : 4 * q + 4, :].bitcast(I32))
+        tab_w = keep.tile([P, T], I32, align_bytes=64, tag="then_tab")
+        nc.sync.dma_start(tab_w[:], tab_words[0].rearrange("p t b -> p (t b)").bitcast(I32))
+        for q in range(4):
+            nc.sync.dma_start(
+                wb_raw_s[32 * q : 32 * q + 4, :, :].bitcast(I32),
+                wb_scales[:, 4 * q : 4 * q + 4, :].rearrange("a r n -> r a n").bitcast(I32),
+            )
+        nc.scalar.copy(
+            gain_rows[0:2].rearrange("v g t (q i) -> v g t q i", i=4),
+            gain_raw[:].rearrange("v (g q t i) -> v g t q i", g=2, t=PACK, i=4),
+        )
+        wb_raw_w = keep.tile([P, PASSES, R // 2], I32, align_bytes=64, tag="then_wb")
+        nc.sync.dma_start(wb_raw_w[:], wb_words.rearrange("a p b -> p a b").bitcast(I32))
+
+        nc.vector.tensor_copy(s0_first[:], tab_s[:].indirect(list_b[:, 0:32]))
+        nc.scalar.dma_start(s1_first[0:112, :].bitcast(I32), s0_first[4:116, :].bitcast(I32))
+        nc.vector.tensor_copy(s0_rest[:, 0:HALF], tab_s[:].indirect(list_b[:, 32:64]))
+        nc.vector.tensor_copy(s0_rest[:, HALF:], tab_s[:].indirect(list_a[:]))
+        nc.scalar.dma_start(s1_rest[0:112, :].bitcast(I32), s0_rest[4:116, :].bitcast(I32))
+
+        wa_all = keep.tile([P, 2, PASSES, PACK, HALF], F32, align_bytes=64, tag="early")
+        wa_raw = {}
+        for g in range(2):
+            for a in range(PASSES):
+                nc.sync.dma_start(
+                    wa_all[:, g, a, :, :],
+                    wa[512 * a : 512 * (a + 1), HALF * g : HALF * (g + 1)].rearrange("(p j) c -> p j c", j=PACK),
+                )
+                wa_raw[a, g] = wa_all[:, g, a, :, :]
+
+        wb_w = keep.tile([P, PASSES, PACK, 512], U8, align_bytes=64)
+        wb_s = keep.tile([P, PASSES, PACK, 256], U8, align_bytes=64)
+
+        def permute_wb():
+            nc.vector.tensor_copy(
+                wb_w[:].bitcast(I32).rearrange("p a t (q w) -> p a t q w", w=2),
+                wb_raw_w[:].rearrange("p a (q t w) -> p a t q w", t=PACK, w=2),
+            )
+            nc.vector.tensor_copy(
+                wb_s[:].bitcast(I32),
+                wb_raw_s[:].bitcast(I32).rearrange("p a (q t) -> p a t q", t=PACK),
+            )
+
+        gain = keep.tile([P, 2, 2, PACK], F32)
+        for g in range(2):
+            gain_ps = psum.tile([P, PACK, P], F32, tag="y", bufs=3, name="gain_ps")
+            for t in range(PACK):
+                nc.tensor.transpose(gain_ps[:, t, :], gain_rows[:, g, t, :], ident[:])
+            nc.scalar.copy(gain[:, :, g, :], gain_ps[:, :, 0:2].rearrange("p t v -> p v t"))
+
+        def gather_words(offsets, n, name, tag="then_wb"):
+            both = keep.tile([P, n], U32, name=name + "_both", align_bytes=64, tag=tag)
+            nc.vector.tensor_copy(both[:], tab_w[:].bitcast(U32).indirect(offsets))
+            parted = keep.tile([P, PASSES, 2 * n], U8, name=name + "_parted", align_bytes=64)
+            nc.vector.tensor_copy(parted[:].bitcast(U16), both[:].bitcast(U16).rearrange("p (n d) -> p d n", d=PASSES))
+            return parted
+
+        wa_codes, wa_scales = {}, {}
+
+        def quantize_wa(a, g, on_scalar):
+            grouped = ring.tile([P, PACK * HALF], BF16, name="wa_grouped", tag="act", bufs=4, align_bytes=64)
+            dst = grouped[:].rearrange("p (t q i j) -> p t q j i", t=PACK, i=4, j=PACK)
+            src = wa_raw[a, g].rearrange("p j (q t i) -> p t q j i", t=PACK, i=4)
+            if on_scalar:
+                nc.scalar.copy(dst, src)
+            else:
+                nc.vector.tensor_copy(dst, src)
+            codes = keep.tile([P, HALF], U32, name="wa_codes_%d%d" % (a, g), align_bytes=64)
+            scales = keep.tile([P, HALF], U8, name="wa_scales_%d%d" % (a, g), align_bytes=64)
+            nc.vector.quantize_mx(out=codes[:].bitcast(FP8X4), scales=scales[:], in_=grouped[:])
+            wa_codes[a, g], wa_scales[a, g] = codes, scales
+
+        def wa_tile(a, g, t):
+            cols = slice(P * t, P * (t + 1))
+            return wa_codes[a, g][:, cols].bitcast(FP8X4), wa_scales[a, g][:, cols]
+
+        def wb_tile(a, g, t):
+            return wb_w[:, a, t, 256 * g : 256 * (g + 1)].bitcast(FP4X4), wb_s[:, a, t, P * g : P * (g + 1)]
+
+        def hidden(weight_tile, words, word_col, planes, plane_col, gain_col, name):
+            act = ring.tile([P, 2, CHUNK, PACK], F32, name="act", tag="act", bufs=4, align_bytes=64)
+            for g in range(2):
+                z = psum.tile([P, PACK, CHUNK], F32, tag="z", bufs=5, name="z")
+                for t in range(PACK):
+                    for a in range(PASSES):
+                        codes, scales = weight_tile(a, g, t)
+                        nc.tensor.matmul_mx(
+                            out=z[:, t, :],
+                            lhsT=codes,
+                            lhsT_scale=scales,
+                            rhs=words[:, a, 2 * word_col : 2 * (word_col + CHUNK)].bitcast(FP4X4),
+                            rhs_scale=planes[a][:, plane_col : plane_col + CHUNK],
+                            start=(a == 0),
+                            stop=(a == PASSES - 1),
+                        )
+                nc.scalar.activation(act[:, g, :, :], z[:].rearrange("p t n -> p n t"), ACT.Tanh)
+            scaled = ring.tile([P, 2, CHUNK, PACK], BF16, name="scaled", align_bytes=64)
+            factor = gain[:, gain_col, :, :].unsqueeze(2).to_broadcast([P, 2, CHUNK, PACK])
+            nc.vector.tensor_tensor(scaled[:], act[:], factor, MULT)
+            codes = keep.tile([P, 2 * CHUNK], U32, name=name + "_codes", align_bytes=64)
+            scales = keep.tile([P, 2 * CHUNK], U8, name=name + "_scales", align_bytes=64)
+            nc.vector.quantize_mx(
+                out=codes[:].bitcast(FP8X4), scales=scales[:], in_=scaled[:].rearrange("p g n t -> p (g n t)")
+            )
+            return codes, scales
+
+        b_words = {}
+        hb, ha = {}, {}
+
+        def hidden_b(c):
+            words, col = b_words[c]
+            planes = (s0_first, s1_first) if c < 4 else (s0_rest, s1_rest)
+            hb[c] = hidden(wb_tile, words, col, planes, CHUNK * (c % 4), 1, "hb%d" % c)
+
+        def scores(pairs, dst):
+            y = psum.tile([P, 4, CHUNK], F32, tag="y", bufs=3, name="y")
+            for i, (m, c) in enumerate(pairs):
+                for g in range(2):
+                    cols = slice(CHUNK * g, CHUNK * (g + 1))
+                    nc.tensor.matmul_mx(
+                        out=y[:, i, :],
+                        lhsT=ha[m][0][:, cols].bitcast(FP8X4),
+                        lhsT_scale=ha[m][1][:, cols],
+                        rhs=hb[c][0][:, cols].bitcast(FP8X4),
+                        rhs_scale=hb[c][1][:, cols],
+                        start=(g == 0),
+                        stop=(g == 1),
+                    )
+            result = ring.tile([P, 4, CHUNK], F32, name="result", bufs=4)
+            nc.scalar.activation(result[:], y[:], ACT.Exp, scale=0.015625)
+            nc.sync.dma_start(dst, result[:])
+
+        def scores_row(m):
+            dst = out[P * m : P * (m + 1), 0:HALF].rearrange("p (c n) -> p c n", n=CHUNK)
+            scores([(m, c) for c in range(4)], dst)
+
+        def scores_column(c):
+            dst = out[:, CHUNK * c : CHUNK * (c + 1)].rearrange("(m p) n -> p m n", p=P)
+            scores([(m, c) for m in range(4)], dst)
+
+        def hidden_a(m):
+            ha[m] = hidden(wa_tile, a_words, CHUNK * m, (s0_rest, s1_rest), HALF + CHUNK * m, 0, "ha%d" % m)
+
+        def gather_b(c0, n_chunks, tag="then_wb"):
+            words = gather_words(list_b[:, 8 * c0 : 8 * (c0 + n_chunks)], CHUNK * n_chunks, "vb%d" % c0, tag)
+            for i in range(n_chunks):
+                b_words[c0 + i] = (words, CHUNK * i)
+
+        gather_b(0, 2, "first")
+        permute_wb()
+        gather_b(2, 2)
+        hidden_b(0)
+        gather_b(4, 2)
+        hidden_b(1)
+        hidden_b(2)
+        hidden_b(3)
+        quantize_wa(0, 0, True)
+        quantize_wa(1, 0, False)
+        a_words = gather_words(list_a[:], M, "va")
+        hidden_b(4)
+        quantize_wa(0, 1, True)
+        quantize_wa(1, 1, True)
+        gather_b(6, 2)
+        hidden_b(5)
+        hidden_a(0)
+        hidden_a(1)
+        hidden_a(2)
+        scores_row(0)
+        hidden_a(3)
+        scores_row(1)
+        hidden_b(6)
+        scores_row(2)
+        hidden_b(7)
+        scores_row(3)
+        for c in range(4, 8):
+            scores_column(c)

@@ -1,7 +1,6 @@
 from contextlib import ExitStack
 
 import concourse.mybir as mybir
-from concourse.masks import make_identity
 
 K, R, T, M, J = 1024, 1024, 2048, 512, 1024
 FLOPS = 2 * K * R * (M + J) + 2 * R * M * J
@@ -36,24 +35,32 @@ def tile_list_biaff_tanh_exp_kernel(
 
         list_b = keep.tile([P, J // 16], U16)
         list_a = keep.tile([P, M // 16], U16)
-        tab_s = keep.tile([P, T], U8, align_bytes=64, tag="early")
-        wb_raw_s = keep.tile([P, PASSES, R], U8, align_bytes=64)
-        gain_raw = keep.tile([2, R], F32, align_bytes=64, tag="then_wb")
+        tab_s = keep.tile([P, T], U8, align_bytes=64)
+        gain_raw = keep.tile([2, R], F32)
         gain_rows = keep.tile([P, 2, PACK, P], F32)
         ident = keep.tile([P, P], F32)
-        warm = keep.tile([P, 8], F32, align_bytes=64, tag="then_tab")
-        s0_first = keep.tile([P, HALF], U8, align_bytes=64)
-        s1_first = keep.tile([P, HALF], U8, align_bytes=64)
-        s0_rest = keep.tile([P, 2 * HALF], U8, align_bytes=64)
-        s1_rest = keep.tile([P, 2 * HALF], U8, align_bytes=64)
+        zeros = keep.tile([P, P], F32, align_bytes=64, tag="then_tab")
+        warm = keep.tile([P, 8], F32, align_bytes=64, tag="then_wb")
+        early0 = keep.tile([P, HALF], U8, align_bytes=64)
+        early1 = keep.tile([P, HALF], U8, align_bytes=64)
+        late0 = keep.tile([P, HALF + M], U8, align_bytes=64)
+        late1 = keep.tile([P, HALF + M], U8, align_bytes=64)
 
         nc.vector.memset(tab_s[:].bitcast(I32), 0)
+        nc.vector.memset(zeros[:], 0.0)
         nc.vector.memset(warm[:], 0.0)
+        nc.vector.memset(early1[:].bitcast(I32), 0)
+        nc.vector.memset(late1[:].bitcast(I32), 0)
+        nc.gpsimd.affine_select(
+            out=ident[:],
+            in_=zeros[:],
+            compare_op=mybir.AluOpType.not_equal,
+            fill=1.0,
+            base=0,
+            pattern=[[-1, P]],
+            channel_multiplier=1,
+        )
         nc.gpsimd.memset(gain_rows[:], 0.0)
-        make_identity(nc, ident[:])
-        nc.gpsimd.memset(wb_raw_s[:].bitcast(I32), 0)
-        nc.vector.memset(s1_first[:].bitcast(I32), 0)
-        nc.vector.memset(s1_rest[:].bitcast(I32), 0)
         nc.scalar.activation(warm[:], warm[:], ACT.Exp)
 
         nc.sync.dma_start(list_b[:], offs2)
@@ -64,33 +71,47 @@ def tile_list_biaff_tanh_exp_kernel(
             nc.sync.dma_start(tab_s[32 * q : 32 * q + 8, :].bitcast(I32), tab_scales[:, 4 * q : 4 * q + 4, :].bitcast(I32))
         tab_w = keep.tile([P, T], I32, align_bytes=64, tag="then_tab")
         nc.sync.dma_start(tab_w[:], tab_words[0].rearrange("p t b -> p (t b)").bitcast(I32))
+        wb_raw = keep.tile([P, R + R // 2], I32, align_bytes=64, tag="then_wb")
+        wb_raw_w = wb_raw[:, 0:R].rearrange("p (a w) -> p a w", a=PASSES)
+        wb_raw_s = wb_raw[:, R:].rearrange("p (a w) -> p a w", a=PASSES)
+        nc.vector.memset(wb_raw[:, R:], 0)
+        nc.sync.dma_start(wb_raw_w, wb_words.rearrange("a p b -> p a b").bitcast(I32))
         for q in range(4):
             nc.sync.dma_start(
-                wb_raw_s[32 * q : 32 * q + 4, :, :].bitcast(I32),
+                wb_raw_s[32 * q : 32 * q + 4, :, :],
                 wb_scales[:, 4 * q : 4 * q + 4, :].rearrange("a r n -> r a n").bitcast(I32),
             )
         nc.scalar.copy(
             gain_rows[0:2].rearrange("v g t (q i) -> v g t q i", i=4),
             gain_raw[:].rearrange("v (g q t i) -> v g t q i", g=2, t=PACK, i=4),
         )
-        wb_raw_w = keep.tile([P, PASSES, R // 2], I32, align_bytes=64, tag="then_wb")
-        nc.sync.dma_start(wb_raw_w[:], wb_words.rearrange("a p b -> p a b").bitcast(I32))
 
-        nc.vector.tensor_copy(s0_first[:], tab_s[:].indirect(list_b[:, 0:32]))
-        nc.scalar.dma_start(s1_first[0:112, :].bitcast(I32), s0_first[4:116, :].bitcast(I32))
-        nc.vector.tensor_copy(s0_rest[:, 0:HALF], tab_s[:].indirect(list_b[:, 32:64]))
-        nc.vector.tensor_copy(s0_rest[:, HALF:], tab_s[:].indirect(list_a[:]))
-        nc.scalar.dma_start(s1_rest[0:112, :].bitcast(I32), s0_rest[4:116, :].bitcast(I32))
+        def lift_second_pass(plane0, plane1):
+            nc.scalar.dma_start(plane1[0:112, :].bitcast(I32), plane0[4:116, :].bitcast(I32))
 
-        wa_all = keep.tile([P, 2, PASSES, PACK, HALF], F32, align_bytes=64, tag="early")
+        nc.vector.tensor_copy(early0[:], tab_s[:].indirect(list_b[:, 0:32]))
+        lift_second_pass(early0, early1)
+        nc.vector.tensor_copy(late0[:, 0:HALF], tab_s[:].indirect(list_b[:, 32:64]))
+        nc.vector.tensor_copy(late0[:, HALF:], tab_s[:].indirect(list_a[:]))
+        lift_second_pass(late0, late1)
+
+        def entry_scales(side, c, a):
+            if side == "b" and c < 4:
+                return (early0, early1)[a][:, CHUNK * c : CHUNK * (c + 1)]
+            first = CHUNK * (c - 4) if side == "b" else HALF + CHUNK * c
+            return (late0, late1)[a][:, first : first + CHUNK]
+
         wa_raw = {}
-        for g in range(2):
-            for a in range(PASSES):
-                nc.sync.dma_start(
-                    wa_all[:, g, a, :, :],
-                    wa[512 * a : 512 * (a + 1), HALF * g : HALF * (g + 1)].rearrange("(p j) c -> p j c", j=PACK),
-                )
-                wa_raw[a, g] = wa_all[:, g, a, :, :]
+
+        def load_wa():
+            wa_all = keep.tile([P, 2, PASSES, PACK, HALF], F32, align_bytes=64, tag="then_wa")
+            for g in range(2):
+                for a in range(PASSES):
+                    nc.sync.dma_start(
+                        wa_all[:, g, a, :, :],
+                        wa[512 * a : 512 * (a + 1), HALF * g : HALF * (g + 1)].rearrange("(p j) c -> p j c", j=PACK),
+                    )
+                    wa_raw[a, g] = wa_all[:, g, a, :, :]
 
         wb_w = keep.tile([P, PASSES, PACK, 512], U8, align_bytes=64)
         wb_s = keep.tile([P, PASSES, PACK, 256], U8, align_bytes=64)
@@ -98,11 +119,11 @@ def tile_list_biaff_tanh_exp_kernel(
         def permute_wb():
             nc.vector.tensor_copy(
                 wb_w[:].bitcast(I32).rearrange("p a t (q w) -> p a t q w", w=2),
-                wb_raw_w[:].rearrange("p a (q t w) -> p a t q w", t=PACK, w=2),
+                wb_raw_w.rearrange("p a (q t w) -> p a t q w", t=PACK, w=2),
             )
             nc.vector.tensor_copy(
                 wb_s[:].bitcast(I32),
-                wb_raw_s[:].bitcast(I32).rearrange("p a (q t) -> p a t q", t=PACK),
+                wb_raw_s.rearrange("p a (q t) -> p a t q", t=PACK),
             )
 
         gain = keep.tile([P, 2, 2, PACK], F32)
@@ -112,26 +133,32 @@ def tile_list_biaff_tanh_exp_kernel(
                 nc.tensor.transpose(gain_ps[:, t, :], gain_rows[:, g, t, :], ident[:])
             nc.scalar.copy(gain[:, :, g, :], gain_ps[:, :, 0:2].rearrange("p t v -> p v t"))
 
-        def gather_words(offsets, n, name, tag="then_wb"):
-            both = keep.tile([P, n], U32, name=name + "_both", align_bytes=64, tag=tag)
-            nc.vector.tensor_copy(both[:], tab_w[:].bitcast(U32).indirect(offsets))
-            parted = keep.tile([P, PASSES, 2 * n], U8, name=name + "_parted", align_bytes=64)
-            nc.vector.tensor_copy(parted[:].bitcast(U16), both[:].bitcast(U16).rearrange("p (n d) -> p d n", d=PASSES))
-            return parted
+        def gather_words(both, offsets):
+            nc.vector.tensor_copy(both, tab_w[:].bitcast(U32).indirect(offsets))
 
-        wa_codes, wa_scales = {}, {}
+        words = {}
 
-        def quantize_wa(a, g, on_scalar):
-            grouped = ring.tile([P, PACK * HALF], BF16, name="wa_grouped", tag="act", bufs=4, align_bytes=64)
-            dst = grouped[:].rearrange("p (t q i j) -> p t q j i", t=PACK, i=4, j=PACK)
-            src = wa_raw[a, g].rearrange("p j (q t i) -> p t q j i", t=PACK, i=4)
-            if on_scalar:
-                nc.scalar.copy(dst, src)
-            else:
-                nc.vector.tensor_copy(dst, src)
+        def part_words(both, side, c0):
+            n = both.shape[1]
+            parted = keep.tile([P, PASSES, 2 * n], U8, name="v%s%d" % (side, c0), align_bytes=64)
+            nc.vector.tensor_copy(parted[:].bitcast(U16), both.bitcast(U16).rearrange("p (n d) -> p d n", d=PASSES))
+            for i in range(n // CHUNK):
+                words[side, c0 + i] = (parted, CHUNK * i)
+
+        wa_grouped, wa_codes, wa_scales = {}, {}, {}
+
+        def round_wa(a, g, copy, tag, bufs):
+            grouped = ring.tile([P, PACK * HALF], BF16, name="wa_grouped", tag=tag, bufs=bufs, align_bytes=64)
+            copy(
+                grouped[:].rearrange("p (t q i j) -> p t q j i", t=PACK, i=4, j=PACK),
+                wa_raw[a, g].rearrange("p j (q t i) -> p t q j i", t=PACK, i=4),
+            )
+            wa_grouped[a, g] = grouped
+
+        def quantize_wa(a, g):
             codes = keep.tile([P, HALF], U32, name="wa_codes_%d%d" % (a, g), align_bytes=64)
             scales = keep.tile([P, HALF], U8, name="wa_scales_%d%d" % (a, g), align_bytes=64)
-            nc.vector.quantize_mx(out=codes[:].bitcast(FP8X4), scales=scales[:], in_=grouped[:])
+            nc.vector.quantize_mx(out=codes[:].bitcast(FP8X4), scales=scales[:], in_=wa_grouped[a, g][:])
             wa_codes[a, g], wa_scales[a, g] = codes, scales
 
         def wa_tile(a, g, t):
@@ -141,100 +168,135 @@ def tile_list_biaff_tanh_exp_kernel(
         def wb_tile(a, g, t):
             return wb_w[:, a, t, 256 * g : 256 * (g + 1)].bitcast(FP4X4), wb_s[:, a, t, P * g : P * (g + 1)]
 
-        def hidden(weight_tile, words, word_col, planes, plane_col, gain_col, name):
-            act = ring.tile([P, 2, CHUNK, PACK], F32, name="act", tag="act", bufs=4, align_bytes=64)
+        weights = {"a": wa_tile, "b": wb_tile}
+        acts = {}
+
+        def first_layer(side, c):
+            parted, col = words[side, c]
+            act = ring.tile([P, 2, CHUNK, PACK], F32, name="act", tag="act", bufs=5, align_bytes=64)
             for g in range(2):
                 z = psum.tile([P, PACK, CHUNK], F32, tag="z", bufs=5, name="z")
                 for t in range(PACK):
                     for a in range(PASSES):
-                        codes, scales = weight_tile(a, g, t)
+                        codes, scales = weights[side](a, g, t)
                         nc.tensor.matmul_mx(
                             out=z[:, t, :],
                             lhsT=codes,
                             lhsT_scale=scales,
-                            rhs=words[:, a, 2 * word_col : 2 * (word_col + CHUNK)].bitcast(FP4X4),
-                            rhs_scale=planes[a][:, plane_col : plane_col + CHUNK],
+                            rhs=parted[:, a, 2 * col : 2 * (col + CHUNK)].bitcast(FP4X4),
+                            rhs_scale=entry_scales(side, c, a),
                             start=(a == 0),
                             stop=(a == PASSES - 1),
                         )
                 nc.scalar.activation(act[:, g, :, :], z[:].rearrange("p t n -> p n t"), ACT.Tanh)
-            scaled = ring.tile([P, 2, CHUNK, PACK], BF16, name="scaled", align_bytes=64)
-            factor = gain[:, gain_col, :, :].unsqueeze(2).to_broadcast([P, 2, CHUNK, PACK])
-            nc.vector.tensor_tensor(scaled[:], act[:], factor, MULT)
-            codes = keep.tile([P, 2 * CHUNK], U32, name=name + "_codes", align_bytes=64)
-            scales = keep.tile([P, 2 * CHUNK], U8, name=name + "_scales", align_bytes=64)
-            nc.vector.quantize_mx(
-                out=codes[:].bitcast(FP8X4), scales=scales[:], in_=scaled[:].rearrange("p g n t -> p (g n t)")
-            )
+            acts[side, c] = act
+
+        def apply_gain(side, c, product, groups):
+            factor = gain[:, ["a", "b"].index(side), groups, :].unsqueeze(2).to_broadcast(list(product.shape))
+            nc.vector.tensor_tensor(product, acts[side, c][:, groups], factor, MULT)
+
+        def quantize(values, name):
+            n = values.shape[1] // PACK
+            codes = keep.tile([P, n], U32, name=name + "_codes", align_bytes=64)
+            scales = keep.tile([P, n], U8, name=name + "_scales", align_bytes=64)
+            nc.vector.quantize_mx(out=codes[:].bitcast(FP8X4), scales=scales[:], in_=values)
             return codes, scales
 
-        b_words = {}
-        hb, ha = {}, {}
+        hb_values, hb, ha_values, ha = {}, {}, {}, {}
 
-        def hidden_b(c):
-            words, col = b_words[c]
-            planes = (s0_first, s1_first) if c < 4 else (s0_rest, s1_rest)
-            hb[c] = hidden(wb_tile, words, col, planes, CHUNK * (c % 4), 1, "hb%d" % c)
+        def gain_b(c):
+            if c % 4 == 0:
+                hb_values[c // 4] = ring.tile(
+                    [P, 2, 4, CHUNK, PACK], BF16, name="hb_values", tag="hb_values", bufs=2, align_bytes=64
+                )
+            apply_gain("b", c, hb_values[c // 4][:, :, c % 4, :, :], slice(0, 2))
 
-        def scores(pairs, dst):
-            y = psum.tile([P, 4, CHUNK], F32, tag="y", bufs=3, name="y")
-            for i, (m, c) in enumerate(pairs):
+        def quantize_hb(half, g):
+            hb[half, g] = quantize(hb_values[half][:, g].rearrange("p c n t -> p (c n t)"), "hb%d%d" % (half, g))
+
+        def gain_a(m, g0, g1):
+            if g0 == 0:
+                ha_values[m] = ring.tile([P, 2, CHUNK, PACK], BF16, name="ha_values", bufs=2, align_bytes=64)
+            apply_gain("a", m, ha_values[m][:, g0:g1], slice(g0, g1))
+
+        def quantize_ha(m, g0, g1):
+            codes, scales = quantize(ha_values[m][:, g0:g1].rearrange("p g n t -> p (g n t)"), "ha%d%d" % (m, g0))
+            for g in range(g0, g1):
+                cols = slice(CHUNK * (g - g0), CHUNK * (g - g0 + 1))
+                ha[m, g] = codes[:, cols], scales[:, cols]
+
+        def scores(m):
+            for half in range(2):
+                y = psum.tile([P, HALF], F32, tag="y", bufs=3, name="y")
                 for g in range(2):
-                    cols = slice(CHUNK * g, CHUNK * (g + 1))
                     nc.tensor.matmul_mx(
-                        out=y[:, i, :],
-                        lhsT=ha[m][0][:, cols].bitcast(FP8X4),
-                        lhsT_scale=ha[m][1][:, cols],
-                        rhs=hb[c][0][:, cols].bitcast(FP8X4),
-                        rhs_scale=hb[c][1][:, cols],
+                        out=y[:],
+                        lhsT=ha[m, g][0].bitcast(FP8X4),
+                        lhsT_scale=ha[m, g][1],
+                        rhs=hb[half, g][0][:].bitcast(FP8X4),
+                        rhs_scale=hb[half, g][1][:],
                         start=(g == 0),
                         stop=(g == 1),
                     )
-            result = ring.tile([P, 4, CHUNK], F32, name="result", bufs=4)
-            nc.scalar.activation(result[:], y[:], ACT.Exp, scale=0.015625)
-            nc.sync.dma_start(dst, result[:])
+                result = ring.tile([P, HALF], F32, name="result", bufs=4)
+                nc.scalar.activation(result[:], y[:], ACT.Exp, scale=0.015625)
+                nc.sync.dma_start(out[P * m : P * (m + 1), HALF * half : HALF * (half + 1)], result[:])
 
-        def scores_row(m):
-            dst = out[P * m : P * (m + 1), 0:HALF].rearrange("p (c n) -> p c n", n=CHUNK)
-            scores([(m, c) for c in range(4)], dst)
-
-        def scores_column(c):
-            dst = out[:, CHUNK * c : CHUNK * (c + 1)].rearrange("(m p) n -> p m n", p=P)
-            scores([(m, c) for m in range(4)], dst)
-
-        def hidden_a(m):
-            ha[m] = hidden(wa_tile, a_words, CHUNK * m, (s0_rest, s1_rest), HALF + CHUNK * m, 0, "ha%d" % m)
-
-        def gather_b(c0, n_chunks, tag="then_wb"):
-            words = gather_words(list_b[:, 8 * c0 : 8 * (c0 + n_chunks)], CHUNK * n_chunks, "vb%d" % c0, tag)
-            for i in range(n_chunks):
-                b_words[c0 + i] = (words, CHUNK * i)
-
-        gather_b(0, 2, "first")
+        first_words = keep.tile([P, 2 * CHUNK], U32, align_bytes=64, tag="then_wa")
+        gather_words(first_words[:], list_b[:, 0:16])
+        part_words(first_words[:], "b", 0)
+        load_wa()
         permute_wb()
-        gather_b(2, 2)
-        hidden_b(0)
-        gather_b(4, 2)
-        hidden_b(1)
-        hidden_b(2)
-        hidden_b(3)
-        quantize_wa(0, 0, True)
-        quantize_wa(1, 0, False)
-        a_words = gather_words(list_a[:], M, "va")
-        hidden_b(4)
-        quantize_wa(0, 1, True)
-        quantize_wa(1, 1, True)
-        gather_b(6, 2)
-        hidden_b(5)
-        hidden_a(0)
-        hidden_a(1)
-        hidden_a(2)
-        scores_row(0)
-        hidden_a(3)
-        scores_row(1)
-        hidden_b(6)
-        scores_row(2)
-        hidden_b(7)
-        scores_row(3)
-        for c in range(4, 8):
-            scores_column(c)
+        first_layer("b", 0)
+        first_layer("b", 1)
+        later_words = keep.tile([P, 6 * CHUNK + M], U32, align_bytes=64, tag="then_wb")
+        gather_words(later_words[:, 0:256], list_b[:, 16:32])
+        gather_words(later_words[:, 256:768], list_b[:, 32:64])
+        part_words(later_words[:, 0:256], "b", 2)
+        first_layer("b", 2)
+        first_layer("b", 3)
+        gather_words(later_words[:, 768:], list_a[:])
+        part_words(later_words[:, 256:768], "b", 4)
+        first_layer("b", 4)
+        gain_b(0)
+        part_words(later_words[:, 768:], "a", 0)
+        gain_b(1)
+        round_wa(0, 0, nc.scalar.copy, "act", 5)
+        first_layer("b", 5)
+        gain_b(2)
+        gain_b(3)
+        quantize_wa(0, 0)
+        round_wa(1, 0, nc.scalar.copy, "act", 5)
+        first_layer("b", 6)
+        gain_b(4)
+        quantize_hb(0, 0)
+        quantize_hb(0, 1)
+        round_wa(1, 1, nc.vector.tensor_copy, "hb_values", 2)
+        gain_b(5)
+        quantize_wa(1, 1)
+        round_wa(0, 1, nc.scalar.copy, "act", 5)
+        first_layer("b", 7)
+        quantize_wa(1, 0)
+        gain_b(6)
+        quantize_wa(0, 1)
+        first_layer("a", 0)
+        gain_b(7)
+        first_layer("a", 1)
+        gain_a(0, 0, 2)
+        quantize_hb(1, 0)
+        quantize_ha(0, 0, 2)
+        first_layer("a", 2)
+        gain_a(1, 0, 2)
+        quantize_hb(1, 1)
+        quantize_ha(1, 0, 2)
+        first_layer("a", 3)
+        scores(0)
+        gain_a(2, 0, 2)
+        scores(1)
+        gain_a(3, 0, 1)
+        quantize_ha(2, 0, 2)
+        scores(2)
+        gain_a(3, 1, 2)
+        quantize_ha(3, 0, 1)
+        quantize_ha(3, 1, 2)
+        scores(3)

@@ -117,11 +117,11 @@ def tile_list_biaff_tanh_exp_kernel(
         wb_s = keep.tile([P, PASSES, PACK, 256], U8, align_bytes=64)
 
         def permute_wb():
-            nc.vector.tensor_copy(
+            nc.gpsimd.tensor_copy(
                 wb_w[:].bitcast(I32).rearrange("p a t (q w) -> p a t q w", w=2),
                 wb_raw_w.rearrange("p a (q t w) -> p a t q w", t=PACK, w=2),
             )
-            nc.vector.tensor_copy(
+            nc.gpsimd.tensor_copy(
                 wb_s[:].bitcast(I32),
                 wb_raw_s.rearrange("p a (q t) -> p a t q", t=PACK),
             )
@@ -173,7 +173,7 @@ def tile_list_biaff_tanh_exp_kernel(
 
         def first_layer(side, c):
             parted, col = words[side, c]
-            act = ring.tile([P, 2, CHUNK, PACK], F32, name="act", tag="act", bufs=5, align_bytes=64)
+            act = ring.tile([P, 2, CHUNK, PACK], F32, name="act", tag="act", bufs=4, align_bytes=64)
             for g in range(2):
                 z = psum.tile([P, PACK, CHUNK], F32, tag="z", bufs=5, name="z")
                 for t in range(PACK):
@@ -207,7 +207,7 @@ def tile_list_biaff_tanh_exp_kernel(
         def gain_b(c):
             if c % 4 == 0:
                 hb_values[c // 4] = ring.tile(
-                    [P, 2, 4, CHUNK, PACK], BF16, name="hb_values", tag="hb_values", bufs=2, align_bytes=64
+                    [P, 2, 4, CHUNK, PACK], BF16, name="hb_values", tag="hb_values%d" % (c // 4), bufs=1, align_bytes=64
                 )
             apply_gain("b", c, hb_values[c // 4][:, :, c % 4, :, :], slice(0, 2))
 
@@ -249,7 +249,7 @@ def tile_list_biaff_tanh_exp_kernel(
         permute_wb()
         first_layer("b", 0)
         first_layer("b", 1)
-        later_words = keep.tile([P, 6 * CHUNK + M], U32, align_bytes=64, tag="then_wb")
+        later_words = keep.tile([P, 6 * CHUNK + M], U32, align_bytes=64)
         gather_words(later_words[:, 0:256], list_b[:, 16:32])
         gather_words(later_words[:, 256:768], list_b[:, 32:64])
         part_words(later_words[:, 0:256], "b", 2)
@@ -257,39 +257,39 @@ def tile_list_biaff_tanh_exp_kernel(
         first_layer("b", 3)
         gather_words(later_words[:, 768:], list_a[:])
         part_words(later_words[:, 256:768], "b", 4)
-        first_layer("b", 4)
         gain_b(0)
         part_words(later_words[:, 768:], "a", 0)
+        round_wa(0, 0, nc.scalar.copy, "act", 4)
         gain_b(1)
-        round_wa(0, 0, nc.scalar.copy, "act", 5)
-        first_layer("b", 5)
+        round_wa(1, 0, nc.scalar.copy, "act", 4)
         gain_b(2)
+        first_layer("b", 4)
         gain_b(3)
+        round_wa(0, 1, nc.scalar.copy, "act", 4)
         quantize_wa(0, 0)
-        round_wa(1, 0, nc.scalar.copy, "act", 5)
-        first_layer("b", 6)
-        gain_b(4)
+        first_layer("b", 5)
         quantize_hb(0, 0)
         quantize_hb(0, 1)
-        round_wa(1, 1, nc.vector.tensor_copy, "hb_values", 2)
-        gain_b(5)
-        quantize_wa(1, 1)
-        round_wa(0, 1, nc.scalar.copy, "act", 5)
-        first_layer("b", 7)
+        round_wa(1, 1, nc.vector.tensor_copy, "hb_values0", 1)
         quantize_wa(1, 0)
-        gain_b(6)
+        first_layer("b", 6)
+        quantize_wa(1, 1)
         quantize_wa(0, 1)
+        gain_b(4)
+        first_layer("b", 7)
         first_layer("a", 0)
-        gain_b(7)
+        gain_b(5)
         first_layer("a", 1)
+        gain_b(6)
+        first_layer("a", 2)
+        gain_b(7)
+        first_layer("a", 3)
         gain_a(0, 0, 2)
         quantize_hb(1, 0)
         quantize_ha(0, 0, 2)
-        first_layer("a", 2)
         gain_a(1, 0, 2)
         quantize_hb(1, 1)
         quantize_ha(1, 0, 2)
-        first_layer("a", 3)
         scores(0)
         gain_a(2, 0, 2)
         scores(1)

@@ -95,11 +95,11 @@ def tile_list_biaff_tanh_exp_kernel(
         nc.vector.tensor_copy(late0[:, HALF:], tab_s[:].indirect(list_a[:]))
         lift_second_pass(late0, late1)
 
-        def entry_scales(side, c, a):
-            if side == "b" and c < 4:
-                return (early0, early1)[a][:, CHUNK * c : CHUNK * (c + 1)]
-            first = CHUNK * (c - 4) if side == "b" else HALF + CHUNK * c
-            return (late0, late1)[a][:, first : first + CHUNK]
+        def entry_scales(side, first, n, a):
+            if side == "b" and first < HALF:
+                return (early0, early1)[a][:, first : first + n]
+            start = first - HALF if side == "b" else HALF + first
+            return (late0, late1)[a][:, start : start + n]
 
         wa_raw = {}
 
@@ -168,32 +168,40 @@ def tile_list_biaff_tanh_exp_kernel(
         def wb_tile(a, g, t):
             return wb_w[:, a, t, 256 * g : 256 * (g + 1)].bitcast(FP4X4), wb_s[:, a, t, P * g : P * (g + 1)]
 
-        weights = {"a": wa_tile, "b": wb_tile}
         acts = {}
 
-        def first_layer(side, c):
-            parted, col = words[side, c]
-            act = ring.tile([P, 2, CHUNK, PACK], F32, name="act", tag="act", bufs=4, align_bytes=64)
-            for g in range(2):
-                z = psum.tile([P, PACK, CHUNK], F32, tag="z", bufs=5, name="z")
-                for t in range(PACK):
-                    for a in range(PASSES):
-                        codes, scales = weights[side](a, g, t)
-                        nc.tensor.matmul_mx(
-                            out=z[:, t, :],
-                            lhsT=codes,
-                            lhsT_scale=scales,
-                            rhs=parted[:, a, 2 * col : 2 * (col + CHUNK)].bitcast(FP4X4),
-                            rhs_scale=entry_scales(side, c, a),
-                            start=(a == 0),
-                            stop=(a == PASSES - 1),
-                        )
-                nc.scalar.activation(act[:, g, :, :], z[:].rearrange("p t n -> p n t"), ACT.Tanh)
-            acts[side, c] = act
+        def products(z, weight, side, first, n):
+            parted, col = words[side, first // CHUNK]
+            for a in range(PASSES):
+                codes, scales = weight(a)
+                nc.tensor.matmul_mx(
+                    out=z,
+                    lhsT=codes,
+                    lhsT_scale=scales,
+                    rhs=parted[:, a, 2 * col : 2 * (col + n)].bitcast(FP4X4),
+                    rhs_scale=entry_scales(side, first, n, a),
+                    start=(a == 0),
+                    stop=(a == PASSES - 1),
+                )
 
-        def apply_gain(side, c, product, groups):
-            factor = gain[:, ["a", "b"].index(side), groups, :].unsqueeze(2).to_broadcast(list(product.shape))
-            nc.vector.tensor_tensor(product, acts[side, c][:, groups], factor, MULT)
+        def layer_a(m):
+            act = ring.tile([P, 2, CHUNK, PACK], F32, name="act_a", tag="act", bufs=4, align_bytes=64)
+            for g in range(2):
+                z = psum.tile([P, PACK, CHUNK], F32, tag="z", bufs=5, name="z_a")
+                for t in range(PACK):
+                    products(z[:, t, :], lambda a: wa_tile(a, g, t), "a", CHUNK * m, CHUNK)
+                nc.scalar.activation(act[:, g, :, :], z[:].rearrange("p t n -> p n t"), ACT.Tanh)
+            acts["a", m] = act
+
+        def layer_b(c):
+            pair, g = divmod(c, 2)
+            act = ring.tile([P, 2, 2 * CHUNK, 2], F32, name="act_b", tag="act", bufs=4, align_bytes=64)
+            for u in range(2):
+                z = psum.tile([P, 2, 2 * CHUNK], F32, tag="z", bufs=5, name="z_b")
+                for e in range(2):
+                    products(z[:, e, :], lambda a: wb_tile(a, g, 2 * u + e), "b", 2 * CHUNK * pair, 2 * CHUNK)
+                nc.scalar.activation(act[:, u, :, :], z[:].rearrange("p e n -> p n e"), ACT.Tanh)
+            acts["b", c] = act
 
         def quantize(values, name):
             n = values.shape[1] // PACK
@@ -205,19 +213,28 @@ def tile_list_biaff_tanh_exp_kernel(
         hb_values, hb, ha_values, ha = {}, {}, {}, {}
 
         def gain_b(c):
+            pair, g = divmod(c, 2)
+            half = pair // 2
             if c % 4 == 0:
-                hb_values[c // 4] = ring.tile(
-                    [P, 2, 4, CHUNK, PACK], BF16, name="hb_values", tag="hb_values%d" % (c // 4), bufs=1, align_bytes=64
+                hb_values[half] = ring.tile(
+                    [P, 2, HALF, PACK], BF16, name="hb_values", tag="hb_values%d" % half, bufs=1, align_bytes=64
                 )
-            apply_gain("b", c, hb_values[c // 4][:, :, c % 4, :, :], slice(0, 2))
+            first = 2 * CHUNK * (pair % 2)
+            nc.vector.tensor_tensor(
+                hb_values[half][:, g, first : first + 2 * CHUNK, :].rearrange("p n (u e) -> p n u e", u=2),
+                acts["b", c][:].rearrange("p u n e -> p n u e"),
+                gain[:, 1, g, :].rearrange("p (u e) -> p u e", u=2).unsqueeze(1).to_broadcast([P, 2 * CHUNK, 2, 2]),
+                MULT,
+            )
 
         def quantize_hb(half, g):
-            hb[half, g] = quantize(hb_values[half][:, g].rearrange("p c n t -> p (c n t)"), "hb%d%d" % (half, g))
+            hb[half, g] = quantize(hb_values[half][:, g].rearrange("p n t -> p (n t)"), "hb%d%d" % (half, g))
 
         def gain_a(m, g0, g1):
             if g0 == 0:
                 ha_values[m] = ring.tile([P, 2, CHUNK, PACK], BF16, name="ha_values", bufs=2, align_bytes=64)
-            apply_gain("a", m, ha_values[m][:, g0:g1], slice(g0, g1))
+            factor = gain[:, 0, g0:g1, :].unsqueeze(2).to_broadcast([P, g1 - g0, CHUNK, PACK])
+            nc.vector.tensor_tensor(ha_values[m][:, g0:g1], acts["a", m][:, g0:g1], factor, MULT)
 
         def quantize_ha(m, g0, g1):
             codes, scales = quantize(ha_values[m][:, g0:g1].rearrange("p g n t -> p (g n t)"), "ha%d%d" % (m, g0))
@@ -247,14 +264,14 @@ def tile_list_biaff_tanh_exp_kernel(
         part_words(first_words[:], "b", 0)
         load_wa()
         permute_wb()
-        first_layer("b", 0)
-        first_layer("b", 1)
+        layer_b(0)
+        layer_b(1)
         later_words = keep.tile([P, 6 * CHUNK + M], U32, align_bytes=64)
         gather_words(later_words[:, 0:256], list_b[:, 16:32])
         gather_words(later_words[:, 256:768], list_b[:, 32:64])
         part_words(later_words[:, 0:256], "b", 2)
-        first_layer("b", 2)
-        first_layer("b", 3)
+        layer_b(2)
+        layer_b(3)
         gather_words(later_words[:, 768:], list_a[:])
         part_words(later_words[:, 256:768], "b", 4)
         gain_b(0)
@@ -263,27 +280,27 @@ def tile_list_biaff_tanh_exp_kernel(
         gain_b(1)
         round_wa(1, 0, nc.scalar.copy, "act", 4)
         gain_b(2)
-        first_layer("b", 4)
+        layer_b(4)
         gain_b(3)
         round_wa(0, 1, nc.scalar.copy, "act", 4)
         quantize_wa(0, 0)
-        first_layer("b", 5)
+        layer_b(5)
         quantize_hb(0, 0)
         quantize_hb(0, 1)
         round_wa(1, 1, nc.vector.tensor_copy, "hb_values0", 1)
         quantize_wa(1, 0)
-        first_layer("b", 6)
+        layer_b(6)
         quantize_wa(1, 1)
         quantize_wa(0, 1)
         gain_b(4)
-        first_layer("b", 7)
-        first_layer("a", 0)
+        layer_b(7)
+        layer_a(0)
         gain_b(5)
-        first_layer("a", 1)
+        layer_a(1)
         gain_b(6)
-        first_layer("a", 2)
+        layer_a(2)
         gain_b(7)
-        first_layer("a", 3)
+        layer_a(3)
         gain_a(0, 0, 2)
         quantize_hb(1, 0)
         quantize_ha(0, 0, 2)

@@ -15,13 +15,13 @@ FP8X4 = mybir.dt.float8_e4m3fn_x4
 FP4X4 = mybir.dt.float4_e2m1fn_x4
 ACT = mybir.ActivationFunctionType
 MULT = mybir.AluOpType.mult
+ADD = mybir.AluOpType.add
 
 P = 128
 PACK = 4
 PASSES = 2
-CHUNK = 128
 HALF = 512
-B_FIRST = 5
+BANK = 512
 
 
 def tile_list_biaff_tanh_exp_kernel(
@@ -31,26 +31,31 @@ def tile_list_biaff_tanh_exp_kernel(
     with ExitStack() as ctx:
         keep = ctx.enter_context(tc.tile_pool(name="keep", bufs=1))
         ring = ctx.enter_context(tc.tile_pool(name="ring", bufs=3))
+        arena = ctx.enter_context(tc.tile_pool(name="arena", bufs=1))
         psum = ctx.enter_context(tc.psum_pool(name="psum", bufs=1))
 
         list_b = keep.tile([P, J // 16], U16)
         list_a = keep.tile([P, M // 16], U16)
-        tab_s = keep.tile([P, T], U8, align_bytes=64)
-        gain_raw = keep.tile([2, R], F32)
-        gain_rows = keep.tile([P, 2, PACK, P], F32)
+        tab_s = keep.tile([P, T], U8, align_bytes=64, tag="then_words")
+        gain_raw = keep.tile([4, HALF], F32)
         ident = keep.tile([P, P], F32)
-        zeros = keep.tile([P, P], F32, align_bytes=64, tag="then_tab")
-        warm = keep.tile([P, 8], F32, align_bytes=64, tag="then_wb")
-        early0 = keep.tile([P, HALF], U8, align_bytes=64)
-        early1 = keep.tile([P, HALF], U8, align_bytes=64)
-        late0 = keep.tile([P, HALF + M], U8, align_bytes=64)
-        late1 = keep.tile([P, HALF + M], U8, align_bytes=64)
+        zeros = keep.tile([P, P], F32, align_bytes=64)
+        warm = keep.tile([P, 8], F32, align_bytes=64)
+        early_picked = keep.tile([P, HALF], U8, align_bytes=64)
+        late_picked = keep.tile([P, HALF + M], U8, align_bytes=64)
+        early = keep.tile([P, PASSES, HALF], U8, align_bytes=64)
+        late = keep.tile([P, PASSES, HALF + M], U8, align_bytes=64)
+        wb_raw_s = keep.tile([P, PASSES, R // 4], I32, align_bytes=64)
 
-        nc.vector.memset(tab_s[:].bitcast(I32), 0)
-        nc.vector.memset(zeros[:], 0.0)
         nc.vector.memset(warm[:], 0.0)
-        nc.vector.memset(early1[:].bitcast(I32), 0)
-        nc.vector.memset(late1[:].bitcast(I32), 0)
+        nc.gpsimd.memset(wb_raw_s[:], 0)
+        for v, vec in enumerate((sa, sb)):
+            nc.gpsimd.dma_start(gain_raw[2 * v : 2 * v + 2, :], vec.rearrange("(g r) -> g r", g=2))
+        for q in range(4):
+            nc.vector.memset(tab_s[32 * q : 32 * q + 24, :].bitcast(I32), 0)
+        nc.gpsimd.memset(early[:].bitcast(I32), 0)
+        nc.gpsimd.memset(late[:].bitcast(I32), 0)
+        nc.gpsimd.memset(zeros[:], 0.0)
         nc.gpsimd.affine_select(
             out=ident[:],
             in_=zeros[:],
@@ -60,51 +65,41 @@ def tile_list_biaff_tanh_exp_kernel(
             pattern=[[-1, P]],
             channel_multiplier=1,
         )
-        nc.gpsimd.memset(gain_rows[:], 0.0)
         nc.scalar.activation(warm[:], warm[:], ACT.Exp)
 
         nc.sync.dma_start(list_b[:], offs2)
         nc.sync.dma_start(list_a[:], offs)
-        for row, vec in enumerate((sa, sb)):
-            nc.sync.dma_start(gain_raw[row : row + 1, :], vec.rearrange("(o r) -> o r", o=1))
         for q in range(4):
-            nc.sync.dma_start(tab_s[32 * q : 32 * q + 8, :].bitcast(I32), tab_scales[:, 4 * q : 4 * q + 4, :].bitcast(I32))
-        tab_w = keep.tile([P, T], I32, align_bytes=64, tag="then_tab")
+            nc.sync.dma_start(tab_s[32 * q + 24 : 32 * q + 32, :].bitcast(I32), tab_scales[:, 4 * q : 4 * q + 4, :].bitcast(I32))
+        tab_w = keep.tile([P, T], I32, align_bytes=64)
         nc.sync.dma_start(tab_w[:], tab_words[0].rearrange("p t b -> p (t b)").bitcast(I32))
-        wb_raw = keep.tile([P, R + R // 2], I32, align_bytes=64, tag="then_wb")
-        wb_raw_w = wb_raw[:, 0:R].rearrange("p (a w) -> p a w", a=PASSES)
-        wb_raw_s = wb_raw[:, R:].rearrange("p (a w) -> p a w", a=PASSES)
-        nc.vector.memset(wb_raw[:, R:], 0)
-        nc.sync.dma_start(wb_raw_w, wb_words.rearrange("a p b -> p a b").bitcast(I32))
+        wb_raw_w = keep.tile([P, PASSES, R // 2], I32, align_bytes=64)
+        nc.sync.dma_start(wb_raw_w[:], wb_words.rearrange("a p b -> p a b").bitcast(I32))
         for q in range(4):
             nc.sync.dma_start(
                 wb_raw_s[32 * q : 32 * q + 4, :, :],
                 wb_scales[:, 4 * q : 4 * q + 4, :].rearrange("a r n -> r a n").bitcast(I32),
             )
-        nc.scalar.copy(
-            gain_rows[0:2].rearrange("v g t (q i) -> v g t q i", i=4),
-            gain_raw[:].rearrange("v (g q t i) -> v g t q i", g=2, t=PACK, i=4),
-        )
 
-        def lift_second_pass(plane0, plane1):
-            nc.scalar.dma_start(plane1[0:112, :].bitcast(I32), plane0[4:116, :].bitcast(I32))
 
-        nc.vector.tensor_copy(early0[:], tab_s[:].indirect(list_b[:, 0:32]))
-        lift_second_pass(early0, early1)
-        nc.vector.tensor_copy(late0[:, 0:HALF], tab_s[:].indirect(list_b[:, 32:64]))
-        nc.vector.tensor_copy(late0[:, HALF:], tab_s[:].indirect(list_a[:]))
-        lift_second_pass(late0, late1)
+        def gather_scales(picked, offsets):
+            nc.vector.tensor_copy(picked, tab_s[:].indirect(offsets))
+
+        def lift_scales(picked, planes):
+            for a in range(PASSES):
+                drop = 24 + 4 * a
+                nc.scalar.dma_start(planes[0 : P - drop, a, :].bitcast(I32), picked[drop:P, :].bitcast(I32))
 
         def entry_scales(side, first, n, a):
             if side == "b" and first < HALF:
-                return (early0, early1)[a][:, first : first + n]
+                return early[:, a, first : first + n]
             start = first - HALF if side == "b" else HALF + first
-            return (late0, late1)[a][:, start : start + n]
+            return late[:, a, start : start + n]
 
         wa_raw = {}
 
         def load_wa():
-            wa_all = keep.tile([P, 2, PASSES, PACK, HALF], F32, align_bytes=64, tag="then_wa")
+            wa_all = arena.tile([P, 2, PASSES, PACK, HALF], F32, align_bytes=64, offset=2304)
             for g in range(2):
                 for a in range(PASSES):
                     nc.sync.dma_start(
@@ -113,207 +108,225 @@ def tile_list_biaff_tanh_exp_kernel(
                     )
                     wa_raw[a, g] = wa_all[:, g, a, :, :]
 
-        wb_w = keep.tile([P, PASSES, PACK, 512], U8, align_bytes=64)
-        wb_s = keep.tile([P, PASSES, PACK, 256], U8, align_bytes=64)
+        wb_w = keep.tile([P, 2, PASSES, PACK, 256], U8, align_bytes=64)
+        wb_s = keep.tile([P, 2, PASSES, PACK, 128], U8, align_bytes=64)
 
-        def permute_wb():
+        def permute_wb(g):
             nc.gpsimd.tensor_copy(
-                wb_w[:].bitcast(I32).rearrange("p a t (q w) -> p a t q w", w=2),
-                wb_raw_w.rearrange("p a (q t w) -> p a t q w", t=PACK, w=2),
+                wb_w[:, g].bitcast(I32).rearrange("p a t (q w) -> p a t q w", w=2),
+                wb_raw_w[:, :, 256 * g : 256 * (g + 1)].rearrange("p a (q t w) -> p a t q w", t=PACK, w=2),
             )
             nc.gpsimd.tensor_copy(
-                wb_s[:].bitcast(I32),
-                wb_raw_s.rearrange("p a (q t) -> p a t q", t=PACK),
+                wb_s[:, g].bitcast(I32),
+                wb_raw_s[:, :, 128 * g : 128 * (g + 1)].rearrange("p a (q t) -> p a t q", t=PACK),
             )
 
-        gain = keep.tile([P, 2, 2, PACK], F32)
-        for g in range(2):
-            gain_ps = psum.tile([P, PACK, P], F32, tag="y", bufs=3, name="gain_ps")
+        gain = {}
+        turn = [0]
+
+        def next_bank(shape, name):
+            turn[0] = (turn[0] + 1) % 7
+            return psum.tile(shape, F32, tag="bank%d" % turn[0], name=name)
+
+        def turn_gains():
+            gain_rows = keep.tile([P, PACK, P], F32, align_bytes=64)
+            nc.gpsimd.memset(gain_rows[:], 0.0)
+            nc.gpsimd.tensor_scalar(
+                gain_rows[0:4].rearrange("v t (q i) -> v t q i", i=4),
+                gain_raw[:].rearrange("v (q t i) -> v t q i", t=PACK, i=4),
+                1.0,
+                0.0,
+                MULT,
+                ADD,
+            )
+            gain["ps"] = psum.tile([P, PACK, P], F32, tag="bank7", name="gain_ps")
             for t in range(PACK):
-                nc.tensor.transpose(gain_ps[:, t, :], gain_rows[:, g, t, :], ident[:])
-            nc.scalar.copy(gain[:, :, g, :], gain_ps[:, :, 0:2].rearrange("p t v -> p v t"))
-
-        def gather_words(both, offsets):
-            nc.vector.tensor_copy(both, tab_w[:].bitcast(U32).indirect(offsets))
+                nc.tensor.transpose(gain["ps"][:, t, :], gain_rows[:, t, :], ident[:])
 
         words = {}
 
-        def part_words(both, side, c0):
-            n = both.shape[1]
-            parted = keep.tile([P, PASSES, 2 * n], U8, name="v%s%d" % (side, c0), align_bytes=64)
-            nc.vector.tensor_copy(parted[:].bitcast(U16), both.bitcast(U16).rearrange("p (n d) -> p d n", d=PASSES))
-            for i in range(n // CHUNK):
-                words[side, c0 + i] = (parted, CHUNK * i)
+        def gather_words(side, first, n, place):
+            offsets = (list_a if side == "a" else list_b)[:, first // 16 : (first + n) // 16]
+            if side == "a":
+                both = keep.tile([P, n], U32, name="both_a", align_bytes=64, tag="then_words")
+            else:
+                both = arena.tile([P, n], U32, name="both_b%d" % first, align_bytes=64, offset=place)
+            nc.vector.tensor_copy(both[:], tab_w[:].bitcast(U32).indirect(offsets))
+            words[side, first] = both
+
+        parted = {}
+        slots = {("b", 0): "round00", ("b", 256): "round10", ("b", 512): "round01", ("b", 768): "v_last", ("a", 0): "v_a"}
+
+        def part_words(side, first, n, gathered):
+            both = words[side, gathered][:, first - gathered : first - gathered + n]
+            tile = keep.tile([P, PASSES, 2 * n], U8, name="parted", tag=slots[side, first], align_bytes=64)
+            nc.vector.tensor_copy(tile[:].bitcast(U16), both.bitcast(U16).rearrange("p (n d) -> p d n", d=PASSES))
+            for c in range(0, n, P):
+                parted[side, first + c] = tile[:, :, 2 * c :]
 
         wa_grouped, wa_codes, wa_scales = {}, {}, {}
 
-        def round_wa(a, g, copy, tag, bufs):
-            grouped = ring.tile([P, PACK * HALF], BF16, name="wa_grouped", tag=tag, bufs=bufs, align_bytes=64)
+        def round_wa(a, g, copy, t0, t1):
+            if t0 == 0:
+                wa_grouped[a, g] = keep.tile([P, PACK, HALF], BF16, name="wa_grouped", tag="round%d%d" % (a, g), align_bytes=64)
             copy(
-                grouped[:].rearrange("p (t q i j) -> p t q j i", t=PACK, i=4, j=PACK),
-                wa_raw[a, g].rearrange("p j (q t i) -> p t q j i", t=PACK, i=4),
+                wa_grouped[a, g][:, t0:t1, :].rearrange("p t (q i j) -> p t q j i", i=4, j=PACK),
+                wa_raw[a, g].rearrange("p j (q t i) -> p t q j i", t=PACK, i=4)[:, t0:t1],
             )
-            wa_grouped[a, g] = grouped
 
         def quantize_wa(a, g):
             codes = keep.tile([P, HALF], U32, name="wa_codes_%d%d" % (a, g), align_bytes=64)
             scales = keep.tile([P, HALF], U8, name="wa_scales_%d%d" % (a, g), align_bytes=64)
-            nc.vector.quantize_mx(out=codes[:].bitcast(FP8X4), scales=scales[:], in_=wa_grouped[a, g][:])
+            nc.vector.quantize_mx(
+                out=codes[:].bitcast(FP8X4), scales=scales[:], in_=wa_grouped[a, g][:].rearrange("p t c -> p (t c)")
+            )
             wa_codes[a, g], wa_scales[a, g] = codes, scales
 
-        def wa_tile(a, g, t):
+        def weight_tile(side, a, g, t):
+            if side == "b":
+                return wb_w[:, g, a, t, :].bitcast(FP4X4), wb_s[:, g, a, t, :]
             cols = slice(P * t, P * (t + 1))
             return wa_codes[a, g][:, cols].bitcast(FP8X4), wa_scales[a, g][:, cols]
 
-        def wb_tile(a, g, t):
-            return wb_w[:, a, t, 256 * g : 256 * (g + 1)].bitcast(FP4X4), wb_s[:, a, t, P * g : P * (g + 1)]
-
-        acts = {}
-
-        def products(z, weight, side, first, n):
-            parted, col = words[side, first // CHUNK]
-            for a in range(PASSES):
-                codes, scales = weight(a)
-                nc.tensor.matmul_mx(
-                    out=z,
-                    lhsT=codes,
-                    lhsT_scale=scales,
-                    rhs=parted[:, a, 2 * col : 2 * (col + n)].bitcast(FP4X4),
-                    rhs_scale=entry_scales(side, first, n, a),
-                    start=(a == 0),
-                    stop=(a == PASSES - 1),
-                )
-
-        def layer_a(m):
-            act = ring.tile([P, 2, CHUNK, PACK], F32, name="act_a", tag="act", bufs=4, align_bytes=64)
+        acts, values = {}, {}
+        h_codes = {}
+        h_scales = {}
+        for side, count in (("a", M), ("b", J)):
             for g in range(2):
-                z = psum.tile([P, PACK, CHUNK], F32, tag="z", bufs=5, name="z_a")
-                for t in range(PACK):
-                    products(z[:, t, :], lambda a: wa_tile(a, g, t), "a", CHUNK * m, CHUNK)
-                nc.scalar.activation(act[:, g, :, :], z[:].rearrange("p t n -> p n t"), ACT.Tanh)
-            acts["a", m] = act
+                h_codes[side, g] = keep.tile([P, count], U32, name="h%s%d_codes" % (side, g), align_bytes=64)
+                h_scales[side, g] = keep.tile([P, count], U8, name="h%s%d_scales" % (side, g), align_bytes=64)
 
-        def layer_b(c):
-            pair, g = divmod(c, 2)
-            act = ring.tile([P, 2, 2 * CHUNK, 2], F32, name="act_b", tag="act", bufs=4, align_bytes=64)
-            for u in range(2):
-                z = psum.tile([P, 2, 2 * CHUNK], F32, tag="z", bufs=5, name="z_b")
-                for e in range(2):
-                    products(z[:, e, :], lambda a: wb_tile(a, g, 2 * u + e), "b", 2 * CHUNK * pair, 2 * CHUNK)
+        def layer(side, first, n, g, spare=False):
+            per_bank = BANK // n
+            banks = PACK // per_bank
+            act = ring.tile([P, banks, n, per_bank], F32, name="act", tag="act", bufs=6, align_bytes=64)
+            for u in range(banks):
+                if spare and u == 0:
+                    z = psum.tile([P, per_bank, n], F32, tag="bank7", name="z")
+                else:
+                    z = next_bank([P, per_bank, n], "z")
+                for e in range(per_bank):
+                    for a in range(PASSES):
+                        codes, scales = weight_tile(side, a, g, per_bank * u + e)
+                        nc.tensor.matmul_mx(
+                            out=z[:, e, :],
+                            lhsT=codes,
+                            lhsT_scale=scales,
+                            rhs=parted[side, first][:, a, 0 : 2 * n].bitcast(FP4X4),
+                            rhs_scale=entry_scales(side, first, n, a),
+                            start=(a == 0),
+                            stop=(a == PASSES - 1),
+                        )
                 nc.scalar.activation(act[:, u, :, :], z[:].rearrange("p e n -> p n e"), ACT.Tanh)
-            acts["b", c] = act
+            acts[side, first, g] = act
 
-        def quantize(values, name):
-            n = values.shape[1] // PACK
-            codes = keep.tile([P, n], U32, name=name + "_codes", align_bytes=64)
-            scales = keep.tile([P, n], U8, name=name + "_scales", align_bytes=64)
-            nc.vector.quantize_mx(out=codes[:].bitcast(FP8X4), scales=scales[:], in_=values)
-            return codes, scales
-
-        hb_values, hb, ha_values, ha = {}, {}, {}, {}
-
-        def gain_b(c):
-            pair, g = divmod(c, 2)
-            half = pair // 2
-            if c % 4 == 0:
-                hb_values[half] = ring.tile(
-                    [P, 2, HALF, PACK], BF16, name="hb_values", tag="hb_values%d" % half, bufs=1, align_bytes=64
-                )
-            first = 2 * CHUNK * (pair % 2)
+        def apply_gain(side, first, g):
+            act = acts[side, first, g]
+            banks, n, per_bank = act.shape[1:]
+            rounded = ring.tile([P, n, PACK], BF16, name="rounded", tag="rounded", bufs=4, align_bytes=64)
+            factor = gain["ps"][:, :, (0 if side == "a" else 2) + g].rearrange("p (u e) -> p u e", u=banks)
             nc.vector.tensor_tensor(
-                hb_values[half][:, g, first : first + 2 * CHUNK, :].rearrange("p n (u e) -> p n u e", u=2),
-                acts["b", c][:].rearrange("p u n e -> p n u e"),
-                gain[:, 1, g, :].rearrange("p (u e) -> p u e", u=2).unsqueeze(1).to_broadcast([P, 2 * CHUNK, 2, 2]),
+                rounded[:].rearrange("p n (u e) -> p n u e", u=banks),
+                act[:].rearrange("p u n e -> p n u e"),
+                factor.unsqueeze(1).to_broadcast([P, n, banks, per_bank]),
                 MULT,
             )
+            values[side, first, g] = rounded
 
-        def quantize_hb(half, g):
-            hb[half, g] = quantize(hb_values[half][:, g].rearrange("p n t -> p (n t)"), "hb%d%d" % (half, g))
+        def quantize_h(side, first, g):
+            rounded = values[side, first, g]
+            n = rounded.shape[1]
+            nc.vector.quantize_mx(
+                out=h_codes[side, g][:, first : first + n].bitcast(FP8X4),
+                scales=h_scales[side, g][:, first : first + n],
+                in_=rounded[:].rearrange("p n t -> p (n t)"),
+            )
 
-        def gain_a(m, g0, g1):
-            if g0 == 0:
-                ha_values[m] = ring.tile([P, 2, CHUNK, PACK], BF16, name="ha_values", bufs=2, align_bytes=64)
-            factor = gain[:, 0, g0:g1, :].unsqueeze(2).to_broadcast([P, g1 - g0, CHUNK, PACK])
-            nc.vector.tensor_tensor(ha_values[m][:, g0:g1], acts["a", m][:, g0:g1], factor, MULT)
-
-        def quantize_ha(m, g0, g1):
-            codes, scales = quantize(ha_values[m][:, g0:g1].rearrange("p g n t -> p (g n t)"), "ha%d%d" % (m, g0))
-            for g in range(g0, g1):
-                cols = slice(CHUNK * (g - g0), CHUNK * (g - g0 + 1))
-                ha[m, g] = codes[:, cols], scales[:, cols]
-
-        def scores(m):
-            for half in range(2):
-                y = psum.tile([P, HALF], F32, tag="y", bufs=3, name="y")
+        def scores(m0, j0, n):
+            tiles = BANK // n
+            y = next_bank([P, tiles, n], "y")
+            for i in range(tiles):
+                rows = slice(P * (m0 + i), P * (m0 + i + 1))
                 for g in range(2):
                     nc.tensor.matmul_mx(
-                        out=y[:],
-                        lhsT=ha[m, g][0].bitcast(FP8X4),
-                        lhsT_scale=ha[m, g][1],
-                        rhs=hb[half, g][0][:].bitcast(FP8X4),
-                        rhs_scale=hb[half, g][1][:],
+                        out=y[:, i, :],
+                        lhsT=h_codes["a", g][:, rows].bitcast(FP8X4),
+                        lhsT_scale=h_scales["a", g][:, rows],
+                        rhs=h_codes["b", g][:, j0 : j0 + n].bitcast(FP8X4),
+                        rhs_scale=h_scales["b", g][:, j0 : j0 + n],
                         start=(g == 0),
                         stop=(g == 1),
                     )
-                result = ring.tile([P, HALF], F32, name="result", bufs=4)
-                nc.scalar.activation(result[:], y[:], ACT.Exp, scale=0.015625)
-                nc.sync.dma_start(out[P * m : P * (m + 1), HALF * half : HALF * (half + 1)], result[:])
+            result = ring.tile([P, tiles, n], F32, name="result", tag="result", bufs=4)
+            nc.scalar.activation(result[:], y[:], ACT.Exp, scale=0.015625)
+            nc.sync.dma_start(
+                out[P * m0 : P * (m0 + tiles), j0 : j0 + n].rearrange("(i p) j -> p i j", p=P),
+                result[:],
+            )
 
-        first_words = keep.tile([P, 2 * CHUNK], U32, align_bytes=64, tag="then_wa")
-        gather_words(first_words[:], list_b[:, 0:16])
-        part_words(first_words[:], "b", 0)
+        on_scalar, on_vector = nc.scalar.copy, nc.vector.tensor_copy
+
+        gather_scales(early_picked[:], list_b[:, 0:32])
+        lift_scales(early_picked, early)
+        gather_scales(late_picked[:, 0:HALF], list_b[:, 32:64])
+        gather_scales(late_picked[:, HALF:], list_a[:])
+        lift_scales(late_picked, late)
+        gather_words("b", 0, 256, 2048)
+        permute_wb(0)
+        part_words("b", 0, 256, 0)
         load_wa()
-        permute_wb()
-        layer_b(0)
-        layer_b(1)
-        later_words = keep.tile([P, 6 * CHUNK + M], U32, align_bytes=64)
-        gather_words(later_words[:, 0:256], list_b[:, 16:32])
-        gather_words(later_words[:, 256:768], list_b[:, 32:64])
-        part_words(later_words[:, 0:256], "b", 2)
-        layer_b(2)
-        layer_b(3)
-        gather_words(later_words[:, 768:], list_a[:])
-        part_words(later_words[:, 256:768], "b", 4)
-        gain_b(0)
-        part_words(later_words[:, 768:], "a", 0)
-        round_wa(0, 0, nc.scalar.copy, "act", 4)
-        gain_b(1)
-        round_wa(1, 0, nc.scalar.copy, "act", 4)
-        gain_b(2)
-        layer_b(4)
-        gain_b(3)
-        round_wa(0, 1, nc.scalar.copy, "act", 4)
+        layer("b", 0, 256, 0)
+        permute_wb(1)
+        gather_words("b", 256, 256, 1280)
+        layer("b", 0, 256, 1, spare=True)
+        part_words("b", 256, 256, 256)
+        layer("b", 256, 256, 0)
+        turn_gains()
+        round_wa(0, 0, on_scalar, 0, 2)
+        gather_words("b", 512, 512, 0)
+        layer("b", 256, 256, 1)
+        round_wa(0, 0, on_scalar, 2, 4)
+        gather_words("a", 0, 512, None)
+        part_words("b", 512, 256, 512)
+        round_wa(1, 0, on_scalar, 0, 2)
+        part_words("a", 0, 512, 0)
+        part_words("b", 768, 256, 512)
+        layer("b", 512, 256, 0)
+        round_wa(1, 0, on_scalar, 2, 4)
+        apply_gain("b", 0, 0)
+        apply_gain("b", 0, 1)
+        quantize_h("b", 0, 0)
         quantize_wa(0, 0)
-        layer_b(5)
-        quantize_hb(0, 0)
-        quantize_hb(0, 1)
-        round_wa(1, 1, nc.vector.tensor_copy, "hb_values0", 1)
+        quantize_h("b", 0, 1)
+        apply_gain("b", 256, 0)
         quantize_wa(1, 0)
-        layer_b(6)
+        layer("b", 512, 256, 1)
+        round_wa(0, 1, on_scalar, 0, 2)
+        layer("a", 0, 256, 0)
+        round_wa(0, 1, on_scalar, 2, 4)
+        layer("a", 256, 256, 0)
+        round_wa(1, 1, on_vector, 0, 4)
+        quantize_h("b", 256, 0)
+        apply_gain("b", 256, 1)
         quantize_wa(1, 1)
         quantize_wa(0, 1)
-        gain_b(4)
-        layer_b(7)
-        layer_a(0)
-        gain_b(5)
-        layer_a(1)
-        gain_b(6)
-        layer_a(2)
-        gain_b(7)
-        layer_a(3)
-        gain_a(0, 0, 2)
-        quantize_hb(1, 0)
-        quantize_ha(0, 0, 2)
-        gain_a(1, 0, 2)
-        quantize_hb(1, 1)
-        quantize_ha(1, 0, 2)
-        scores(0)
-        gain_a(2, 0, 2)
-        scores(1)
-        gain_a(3, 0, 1)
-        quantize_ha(2, 0, 2)
-        scores(2)
-        gain_a(3, 1, 2)
-        quantize_ha(3, 0, 1)
-        quantize_ha(3, 1, 2)
-        scores(3)
+        quantize_h("b", 256, 1)
+        layer("a", 0, 256, 1)
+        layer("a", 256, 256, 1)
+        layer("b", 768, 256, 0)
+        layer("b", 768, 128, 1)
+        layer("b", 896, 128, 1)
+        order = [("b", 512, 0), ("b", 512, 1), ("a", 0, 0), ("a", 0, 1), ("a", 256, 0), ("a", 256, 1)]
+        order = order + [("b", 768, 0), ("b", 768, 1), ("b", 896, 1)]
+        for i, unit in enumerate(order):
+            apply_gain(*unit)
+            if i > 0:
+                quantize_h(*order[i - 1])
+            if i == 4 or i == 6:
+                m0 = i - 4
+                scores(m0, 0, 512)
+                scores(m0 + 1, 0, 512)
+                scores(m0, 512, 256)
+        scores(0, 768, 128)
+        quantize_h(*order[-1])
+        scores(0, 896, 128)

@@ -139,9 +139,9 @@ def tile_list_biaff_tanh_exp_kernel(
                 MULT,
                 ADD,
             )
-            gain["ps"] = psum.tile([P, PACK, P], F32, tag="bank7", name="gain_ps")
+            gain["ps"] = psum.tile([P, P, PACK], F32, tag="bank7", name="gain_ps")
             for t in range(PACK):
-                nc.tensor.transpose(gain["ps"][:, t, :], gain_rows[:, t, :], ident[:])
+                nc.tensor.transpose(gain["ps"][:, :, t], gain_rows[:, t, :], ident[:])
 
         words = {}
 
@@ -224,7 +224,7 @@ def tile_list_biaff_tanh_exp_kernel(
             act = acts[side, first, g]
             banks, n, per_bank = act.shape[1:]
             rounded = ring.tile([P, n, PACK], BF16, name="rounded", tag="rounded", bufs=4, align_bytes=64)
-            factor = gain["ps"][:, :, (0 if side == "a" else 2) + g].rearrange("p (u e) -> p u e", u=banks)
+            factor = gain["ps"][:, (0 if side == "a" else 2) + g, :].rearrange("p (u e) -> p u e", u=banks)
             nc.vector.tensor_tensor(
                 rounded[:].rearrange("p n (u e) -> p n u e", u=banks),
                 act[:].rearrange("p u n e -> p n u e"),

@@ -15,7 +15,6 @@ FP8X4 = mybir.dt.float8_e4m3fn_x4
 FP4X4 = mybir.dt.float4_e2m1fn_x4
 ACT = mybir.ActivationFunctionType
 MULT = mybir.AluOpType.mult
-ADD = mybir.AluOpType.add
 
 P = 128
 PACK = 4
@@ -32,30 +31,25 @@ def tile_list_biaff_tanh_exp_kernel(
         keep = ctx.enter_context(tc.tile_pool(name="keep", bufs=1))
         ring = ctx.enter_context(tc.tile_pool(name="ring", bufs=3))
         arena = ctx.enter_context(tc.tile_pool(name="arena", bufs=1))
+        loads = ctx.enter_context(tc.tile_pool(name="loads", bufs=1))
         psum = ctx.enter_context(tc.psum_pool(name="psum", bufs=1))
 
         list_b = keep.tile([P, J // 16], U16)
         list_a = keep.tile([P, M // 16], U16)
         tab_s = keep.tile([P, T], U8, align_bytes=64, tag="then_words")
         gain_raw = keep.tile([4, HALF], F32)
+        gain_rows = keep.tile([P, PACK, P], F32)
         ident = keep.tile([P, P], F32)
-        zeros = keep.tile([P, P], F32, align_bytes=64)
+        zeros = loads.tile([P, P], F32, align_bytes=64, offset=4 * T - 256)
         warm = keep.tile([P, 8], F32, align_bytes=64)
-        early_picked = keep.tile([P, HALF], U8, align_bytes=64)
-        late_picked = keep.tile([P, HALF + M], U8, align_bytes=64)
-        early = keep.tile([P, PASSES, HALF], U8, align_bytes=64)
-        late = keep.tile([P, PASSES, HALF + M], U8, align_bytes=64)
-        wb_raw_s = keep.tile([P, PASSES, R // 4], I32, align_bytes=64)
+        early0 = keep.tile([P, HALF], U8, align_bytes=64)
+        early1 = keep.tile([P, HALF], U8, align_bytes=64)
+        late0 = keep.tile([P, HALF + M], U8, align_bytes=64)
+        late1 = keep.tile([P, HALF + M], U8, align_bytes=64)
 
+        nc.vector.memset(tab_s[:].bitcast(I32), 0)
+        nc.vector.memset(zeros[:], 0.0)
         nc.vector.memset(warm[:], 0.0)
-        nc.gpsimd.memset(wb_raw_s[:], 0)
-        for v, vec in enumerate((sa, sb)):
-            nc.gpsimd.dma_start(gain_raw[2 * v : 2 * v + 2, :], vec.rearrange("(g r) -> g r", g=2))
-        for q in range(4):
-            nc.vector.memset(tab_s[32 * q : 32 * q + 24, :].bitcast(I32), 0)
-        nc.gpsimd.memset(early[:].bitcast(I32), 0)
-        nc.gpsimd.memset(late[:].bitcast(I32), 0)
-        nc.gpsimd.memset(zeros[:], 0.0)
         nc.gpsimd.affine_select(
             out=ident[:],
             in_=zeros[:],
@@ -69,32 +63,41 @@ def tile_list_biaff_tanh_exp_kernel(
 
         nc.sync.dma_start(list_b[:], offs2)
         nc.sync.dma_start(list_a[:], offs)
+        for v, vec in enumerate((sa, sb)):
+            nc.sync.dma_start(gain_raw[2 * v : 2 * v + 2, :], vec.rearrange("(g r) -> g r", g=2))
         for q in range(4):
-            nc.sync.dma_start(tab_s[32 * q + 24 : 32 * q + 32, :].bitcast(I32), tab_scales[:, 4 * q : 4 * q + 4, :].bitcast(I32))
-        tab_w = keep.tile([P, T], I32, align_bytes=64)
+            nc.sync.dma_start(tab_s[32 * q : 32 * q + 8, :].bitcast(I32), tab_scales[:, 4 * q : 4 * q + 4, :].bitcast(I32))
+        tab_w = loads.tile([P, T], I32, align_bytes=64, offset=0)
         nc.sync.dma_start(tab_w[:], tab_words[0].rearrange("p t b -> p (t b)").bitcast(I32))
-        wb_raw_w = keep.tile([P, PASSES, R // 2], I32, align_bytes=64)
-        nc.sync.dma_start(wb_raw_w[:], wb_words.rearrange("a p b -> p a b").bitcast(I32))
+        wb_raw = loads.tile([P, R + R // 2], I32, align_bytes=64, offset=4 * T)
+        wb_raw_w = wb_raw[:, 0:R].rearrange("p (a w) -> p a w", a=PASSES)
+        wb_raw_s = wb_raw[:, R:].rearrange("p (a w) -> p a w", a=PASSES)
+        nc.gpsimd.memset(wb_raw[:, R:], 0)
         for q in range(4):
             nc.sync.dma_start(
                 wb_raw_s[32 * q : 32 * q + 4, :, :],
                 wb_scales[:, 4 * q : 4 * q + 4, :].rearrange("a r n -> r a n").bitcast(I32),
             )
-
+        nc.sync.dma_start(wb_raw_w, wb_words.rearrange("a p b -> p a b").bitcast(I32))
+        nc.vector.memset(gain_rows[:], 0.0)
+        nc.vector.memset(early1[:].bitcast(I32), 0)
+        nc.vector.memset(late1[:].bitcast(I32), 0)
+        nc.scalar.copy(
+            gain_rows[0:4].rearrange("v t (q i) -> v t q i", i=4),
+            gain_raw[:].rearrange("v (q t i) -> v t q i", t=PACK, i=4),
+        )
 
         def gather_scales(picked, offsets):
             nc.vector.tensor_copy(picked, tab_s[:].indirect(offsets))
 
-        def lift_scales(picked, planes):
-            for a in range(PASSES):
-                drop = 24 + 4 * a
-                nc.scalar.dma_start(planes[0 : P - drop, a, :].bitcast(I32), picked[drop:P, :].bitcast(I32))
+        def lift_scales(plane0, plane1):
+            nc.scalar.dma_start(plane1[0:112, :].bitcast(I32), plane0[4:116, :].bitcast(I32))
 
         def entry_scales(side, first, n, a):
             if side == "b" and first < HALF:
-                return early[:, a, first : first + n]
+                return (early0, early1)[a][:, first : first + n]
             start = first - HALF if side == "b" else HALF + first
-            return late[:, a, start : start + n]
+            return (late0, late1)[a][:, start : start + n]
 
         wa_raw = {}
 
@@ -111,14 +114,17 @@ def tile_list_biaff_tanh_exp_kernel(
         wb_w = keep.tile([P, 2, PASSES, PACK, 256], U8, align_bytes=64)
         wb_s = keep.tile([P, 2, PASSES, PACK, 128], U8, align_bytes=64)
 
+        def permute_wb_scales():
+            for g in range(2):
+                nc.gpsimd.tensor_copy(
+                    wb_s[:, g].bitcast(I32),
+                    wb_raw_s[:, :, 128 * g : 128 * (g + 1)].rearrange("p a (q t) -> p a t q", t=PACK),
+                )
+
         def permute_wb(g):
             nc.gpsimd.tensor_copy(
                 wb_w[:, g].bitcast(I32).rearrange("p a t (q w) -> p a t q w", w=2),
                 wb_raw_w[:, :, 256 * g : 256 * (g + 1)].rearrange("p a (q t w) -> p a t q w", t=PACK, w=2),
-            )
-            nc.gpsimd.tensor_copy(
-                wb_s[:, g].bitcast(I32),
-                wb_raw_s[:, :, 128 * g : 128 * (g + 1)].rearrange("p a (q t) -> p a t q", t=PACK),
             )
 
         gain = {}
@@ -129,16 +135,6 @@ def tile_list_biaff_tanh_exp_kernel(
             return psum.tile(shape, F32, tag="bank%d" % turn[0], name=name)
 
         def turn_gains():
-            gain_rows = keep.tile([P, PACK, P], F32, align_bytes=64)
-            nc.gpsimd.memset(gain_rows[:], 0.0)
-            nc.gpsimd.tensor_scalar(
-                gain_rows[0:4].rearrange("v t (q i) -> v t q i", i=4),
-                gain_raw[:].rearrange("v (q t i) -> v t q i", t=PACK, i=4),
-                1.0,
-                0.0,
-                MULT,
-                ADD,
-            )
             gain["ps"] = psum.tile([P, P, PACK], F32, tag="bank7", name="gain_ps")
             for t in range(PACK):
                 nc.tensor.transpose(gain["ps"][:, :, t], gain_rows[:, t, :], ident[:])
@@ -266,12 +262,13 @@ def tile_list_biaff_tanh_exp_kernel(
 
         on_scalar, on_vector = nc.scalar.copy, nc.vector.tensor_copy
 
-        gather_scales(early_picked[:], list_b[:, 0:32])
-        lift_scales(early_picked, early)
-        gather_scales(late_picked[:, 0:HALF], list_b[:, 32:64])
-        gather_scales(late_picked[:, HALF:], list_a[:])
-        lift_scales(late_picked, late)
+        gather_scales(early0[:], list_b[:, 0:32])
+        lift_scales(early0, early1)
+        gather_scales(late0[:, 0:HALF], list_b[:, 32:64])
+        gather_scales(late0[:, HALF:], list_a[:])
+        lift_scales(late0, late1)
         gather_words("b", 0, 256, 2048)
+        permute_wb_scales()
         permute_wb(0)
         part_words("b", 0, 256, 0)
         load_wa()

@@ -21,6 +21,7 @@ PACK = 4
 PASSES = 2
 HALF = 512
 BANK = 512
+SHARE = {256: 56, 128: 16}
 
 
 def tile_list_biaff_tanh_exp_kernel(
@@ -138,6 +139,8 @@ def tile_list_biaff_tanh_exp_kernel(
             gain["ps"] = psum.tile([P, P, PACK], F32, tag="bank7", name="gain_ps")
             for t in range(PACK):
                 nc.tensor.transpose(gain["ps"][:, :, t], gain_rows[:, t, :], ident[:])
+            gain["sb"] = keep.tile([P, 4, PACK], F32, name="gain_sb")
+            nc.vector.tensor_copy(gain["sb"][:], gain["ps"][:, 0:4, :])
 
         words = {}
 
@@ -151,7 +154,7 @@ def tile_list_biaff_tanh_exp_kernel(
             words[side, first] = both
 
         parted = {}
-        slots = {("b", 0): "round00", ("b", 256): "round10", ("b", 512): "round01", ("b", 768): "v_last", ("a", 0): "v_a"}
+        slots = {("b", 0): "round00", ("b", 256): "round10", ("b", 512): "v_third", ("b", 768): "v_last", ("a", 0): "v_a"}
 
         def part_words(side, first, n, gathered):
             both = words[side, gathered][:, first - gathered : first - gathered + n]
@@ -219,14 +222,20 @@ def tile_list_biaff_tanh_exp_kernel(
         def apply_gain(side, first, g):
             act = acts[side, first, g]
             banks, n, per_bank = act.shape[1:]
-            rounded = ring.tile([P, n, PACK], BF16, name="rounded", tag="rounded", bufs=4, align_bytes=64)
-            factor = gain["ps"][:, (0 if side == "a" else 2) + g, :].rearrange("p (u e) -> p u e", u=banks)
-            nc.vector.tensor_tensor(
-                rounded[:].rearrange("p n (u e) -> p n u e", u=banks),
-                act[:].rearrange("p u n e -> p n u e"),
-                factor.unsqueeze(1).to_broadcast([P, n, banks, per_bank]),
-                MULT,
-            )
+            rounded = ring.tile([P, n, PACK], BF16, name="rounded", tag="rounded", bufs=2, align_bytes=64)
+            v = (0 if side == "a" else 2) + g
+            cut = n - SHARE[n]
+            for engine, factor, c0, c1 in (
+                (nc.vector, gain["ps"][:, v, :], 0, cut),
+                (nc.gpsimd, gain["sb"][:, v, :], cut, n),
+            ):
+                factor = factor.rearrange("p (u e) -> p u e", u=banks)
+                engine.tensor_tensor(
+                    rounded[:, c0:c1, :].rearrange("p n (u e) -> p n u e", u=banks),
+                    act[:, :, c0:c1, :].rearrange("p u n e -> p n u e"),
+                    factor.unsqueeze(1).to_broadcast([P, c1 - c0, banks, per_bank]),
+                    MULT,
+                )
             values[side, first, g] = rounded
 
         def quantize_h(side, first, g):
@@ -253,7 +262,7 @@ def tile_list_biaff_tanh_exp_kernel(
                         start=(g == 0),
                         stop=(g == 1),
                     )
-            result = ring.tile([P, tiles, n], F32, name="result", tag="result", bufs=4)
+            result = ring.tile([P, tiles, n], F32, name="result", tag="result", bufs=8)
             nc.scalar.activation(result[:], y[:], ACT.Exp, scale=0.015625)
             nc.sync.dma_start(
                 out[P * m0 : P * (m0 + tiles), j0 : j0 + n].rearrange("(i p) j -> p i j", p=P),
@@ -276,39 +285,38 @@ def tile_list_biaff_tanh_exp_kernel(
         permute_wb(1)
         gather_words("b", 256, 256, 1280)
         layer("b", 0, 256, 1, spare=True)
-        part_words("b", 256, 256, 256)
-        layer("b", 256, 256, 0)
         turn_gains()
+        part_words("b", 256, 256, 256)
         round_wa(0, 0, on_scalar, 0, 2)
+        layer("b", 256, 256, 0)
         gather_words("b", 512, 512, 0)
-        layer("b", 256, 256, 1)
         round_wa(0, 0, on_scalar, 2, 4)
         gather_words("a", 0, 512, None)
         part_words("b", 512, 256, 512)
+        layer("b", 256, 256, 1)
         round_wa(1, 0, on_scalar, 0, 2)
         part_words("a", 0, 512, 0)
         part_words("b", 768, 256, 512)
-        layer("b", 512, 256, 0)
         round_wa(1, 0, on_scalar, 2, 4)
+        layer("b", 512, 256, 0)
+        layer("b", 512, 256, 1)
         apply_gain("b", 0, 0)
         apply_gain("b", 0, 1)
         quantize_h("b", 0, 0)
-        quantize_wa(0, 0)
-        quantize_h("b", 0, 1)
         apply_gain("b", 256, 0)
-        quantize_wa(1, 0)
-        layer("b", 512, 256, 1)
-        round_wa(0, 1, on_scalar, 0, 2)
-        layer("a", 0, 256, 0)
-        round_wa(0, 1, on_scalar, 2, 4)
-        layer("a", 256, 256, 0)
-        round_wa(1, 1, on_vector, 0, 4)
+        quantize_h("b", 0, 1)
+        quantize_wa(0, 0)
+        round_wa(0, 1, on_vector, 0, 4)
         quantize_h("b", 256, 0)
         apply_gain("b", 256, 1)
-        quantize_wa(1, 1)
-        quantize_wa(0, 1)
+        quantize_wa(1, 0)
+        layer("a", 0, 256, 0)
+        round_wa(1, 1, on_vector, 0, 4)
         quantize_h("b", 256, 1)
+        quantize_wa(0, 1)
+        quantize_wa(1, 1)
         layer("a", 0, 256, 1)
+        layer("a", 256, 256, 0)
         layer("a", 256, 256, 1)
         layer("b", 768, 256, 0)
         layer("b", 768, 128, 1)

@@ -21,7 +21,7 @@ PACK = 4
 PASSES = 2
 HALF = 512
 BANK = 512
-SHARE = {256: 56, 128: 16}
+SHARE = 128
 
 
 def tile_list_biaff_tanh_exp_kernel(
@@ -43,10 +43,10 @@ def tile_list_biaff_tanh_exp_kernel(
         ident = keep.tile([P, P], F32)
         zeros = loads.tile([P, P], F32, align_bytes=64, offset=4 * T - 256)
         warm = keep.tile([P, 8], F32, align_bytes=64)
-        early0 = keep.tile([P, HALF], U8, align_bytes=64)
-        early1 = keep.tile([P, HALF], U8, align_bytes=64)
-        late0 = keep.tile([P, HALF + M], U8, align_bytes=64)
-        late1 = keep.tile([P, HALF + M], U8, align_bytes=64)
+        early0 = keep.tile([P, J], U8, align_bytes=64)
+        early1 = keep.tile([P, J], U8, align_bytes=64)
+        late0 = arena.tile([P, M], U8, align_bytes=64, offset=2304)
+        late1 = keep.tile([P, M], U8, align_bytes=64)
 
         nc.vector.memset(tab_s[:].bitcast(I32), 0)
         nc.vector.memset(zeros[:], 0.0)
@@ -71,7 +71,7 @@ def tile_list_biaff_tanh_exp_kernel(
         tab_w = loads.tile([P, T], I32, align_bytes=64, offset=0)
         nc.sync.dma_start(tab_w[:], tab_words[0].rearrange("p t b -> p (t b)").bitcast(I32))
         wb_raw = loads.tile([P, R + R // 2], I32, align_bytes=64, offset=4 * T)
-        wb_raw_w = wb_raw[:, 0:R].rearrange("p (a w) -> p a w", a=PASSES)
+        wb_raw_w = wb_raw[:, 0:R].rearrange("p (g a w) -> p g a w", g=2, a=PASSES)
         wb_raw_s = wb_raw[:, R:].rearrange("p (a w) -> p a w", a=PASSES)
         nc.gpsimd.memset(wb_raw[:, R:], 0)
         for q in range(4):
@@ -79,7 +79,8 @@ def tile_list_biaff_tanh_exp_kernel(
                 wb_raw_s[32 * q : 32 * q + 4, :, :],
                 wb_scales[:, 4 * q : 4 * q + 4, :].rearrange("a r n -> r a n").bitcast(I32),
             )
-        nc.sync.dma_start(wb_raw_w, wb_words.rearrange("a p b -> p a b").bitcast(I32))
+        for g in range(2):
+            nc.sync.dma_start(wb_raw_w[:, g], wb_words[:, :, R * g : R * (g + 1)].rearrange("a p b -> p a b").bitcast(I32))
         nc.vector.memset(gain_rows[:], 0.0)
         nc.vector.memset(early1[:].bitcast(I32), 0)
         nc.vector.memset(late1[:].bitcast(I32), 0)
@@ -91,19 +92,16 @@ def tile_list_biaff_tanh_exp_kernel(
         def gather_scales(picked, offsets):
             nc.vector.tensor_copy(picked, tab_s[:].indirect(offsets))
 
-        def lift_scales(plane0, plane1):
-            nc.scalar.dma_start(plane1[0:112, :].bitcast(I32), plane0[4:116, :].bitcast(I32))
+        def lift_scales(queue, plane0, plane1):
+            queue.dma_start(plane1[0:112, :].bitcast(I32), plane0[4:116, :].bitcast(I32))
 
         def entry_scales(side, first, n, a):
-            if side == "b" and first < HALF:
-                return (early0, early1)[a][:, first : first + n]
-            start = first - HALF if side == "b" else HALF + first
-            return (late0, late1)[a][:, start : start + n]
+            return ((late0, late1) if side == "a" else (early0, early1))[a][:, first : first + n]
 
         wa_raw = {}
 
         def load_wa():
-            wa_all = arena.tile([P, 2, PASSES, PACK, HALF], F32, align_bytes=64, offset=2304)
+            wa_all = arena.tile([P, 2, PASSES, PACK, HALF], F32, align_bytes=64, offset=2816)
             for g in range(2):
                 for a in range(PASSES):
                     nc.sync.dma_start(
@@ -125,7 +123,7 @@ def tile_list_biaff_tanh_exp_kernel(
         def permute_wb(g):
             nc.gpsimd.tensor_copy(
                 wb_w[:, g].bitcast(I32).rearrange("p a t (q w) -> p a t q w", w=2),
-                wb_raw_w[:, :, 256 * g : 256 * (g + 1)].rearrange("p a (q t w) -> p a t q w", t=PACK, w=2),
+                wb_raw_w[:, g].rearrange("p a (q t w) -> p a t q w", t=PACK, w=2),
             )
 
         gain = {}
@@ -154,7 +152,7 @@ def tile_list_biaff_tanh_exp_kernel(
             words[side, first] = both
 
         parted = {}
-        slots = {("b", 0): "round00", ("b", 256): "round10", ("b", 512): "v_third", ("b", 768): "v_last", ("a", 0): "v_a"}
+        slots = {("b", 0): "round10", ("b", 256): "round00", ("b", 512): "v_third", ("b", 768): "v_last", ("a", 0): "v_a"}
 
         def part_words(side, first, n, gathered):
             both = words[side, gathered][:, first - gathered : first - gathered + n]
@@ -198,7 +196,7 @@ def tile_list_biaff_tanh_exp_kernel(
         def layer(side, first, n, g, spare=False):
             per_bank = BANK // n
             banks = PACK // per_bank
-            act = ring.tile([P, banks, n, per_bank], F32, name="act", tag="act", bufs=6, align_bytes=64)
+            act = ring.tile([P, banks, n, per_bank], F32, name="act", tag="act", bufs=10, align_bytes=64)
             for u in range(banks):
                 if spare and u == 0:
                     z = psum.tile([P, per_bank, n], F32, tag="bank7", name="z")
@@ -219,16 +217,18 @@ def tile_list_biaff_tanh_exp_kernel(
                 nc.scalar.activation(act[:, u, :, :], z[:].rearrange("p e n -> p n e"), ACT.Tanh)
             acts[side, first, g] = act
 
-        def apply_gain(side, first, g):
+        def apply_gain(side, first, g, share=0, slot=None):
             act = acts[side, first, g]
             banks, n, per_bank = act.shape[1:]
-            rounded = ring.tile([P, n, PACK], BF16, name="rounded", tag="rounded", bufs=2, align_bytes=64)
+            if slot is None:
+                rounded = ring.tile([P, n, PACK], BF16, name="rounded", tag="rounded", bufs=2, align_bytes=64)
+            else:
+                rounded = keep.tile([P, n, PACK], BF16, name="rounded", tag=slot, align_bytes=64)
             v = (0 if side == "a" else 2) + g
-            cut = n - SHARE[n]
-            for engine, factor, c0, c1 in (
-                (nc.vector, gain["ps"][:, v, :], 0, cut),
-                (nc.gpsimd, gain["sb"][:, v, :], cut, n),
-            ):
+            parts = [(nc.vector, gain["ps"][:, v, :], 0, n - share)]
+            if share:
+                parts.append((nc.gpsimd, gain["sb"][:, v, :], n - share, n))
+            for engine, factor, c0, c1 in parts:
                 factor = factor.rearrange("p (u e) -> p u e", u=banks)
                 engine.tensor_tensor(
                     rounded[:, c0:c1, :].rearrange("p n (u e) -> p n u e", u=banks),
@@ -250,17 +250,17 @@ def tile_list_biaff_tanh_exp_kernel(
         def scores(m0, j0, n):
             tiles = BANK // n
             y = next_bank([P, tiles, n], "y")
-            for i in range(tiles):
-                rows = slice(P * (m0 + i), P * (m0 + i + 1))
-                for g in range(2):
+            for g in range(2):
+                for i in range(tiles):
+                    rows = slice(P * (m0 + i), P * (m0 + i + 1))
                     nc.tensor.matmul_mx(
                         out=y[:, i, :],
                         lhsT=h_codes["a", g][:, rows].bitcast(FP8X4),
                         lhsT_scale=h_scales["a", g][:, rows],
                         rhs=h_codes["b", g][:, j0 : j0 + n].bitcast(FP8X4),
                         rhs_scale=h_scales["b", g][:, j0 : j0 + n],
-                        start=(g == 0),
-                        stop=(g == 1),
+                        start=(g == 0 and i == 0),
+                        stop=(g == 1 and i == tiles - 1),
                     )
             result = ring.tile([P, tiles, n], F32, name="result", tag="result", bufs=8)
             nc.scalar.activation(result[:], y[:], ACT.Exp, scale=0.015625)
@@ -271,67 +271,74 @@ def tile_list_biaff_tanh_exp_kernel(
 
         on_scalar, on_vector = nc.scalar.copy, nc.vector.tensor_copy
 
-        gather_scales(early0[:], list_b[:, 0:32])
-        lift_scales(early0, early1)
-        gather_scales(late0[:, 0:HALF], list_b[:, 32:64])
-        gather_scales(late0[:, HALF:], list_a[:])
-        lift_scales(late0, late1)
+        for half in range(2):
+            cols = slice(HALF * half, HALF * (half + 1))
+            gather_scales(early0[:, cols], list_b[:, 32 * half : 32 * (half + 1)])
+            lift_scales(nc.scalar, early0[:, cols], early1[:, cols])
         gather_words("b", 0, 256, 2048)
         permute_wb_scales()
         permute_wb(0)
         part_words("b", 0, 256, 0)
         load_wa()
-        layer("b", 0, 256, 0)
+        layer("b", 0, 256, 0, spare=True)
+        turn_gains()
         permute_wb(1)
         gather_words("b", 256, 256, 1280)
-        layer("b", 0, 256, 1, spare=True)
-        turn_gains()
+        layer("b", 0, 256, 1)
+        gather_scales(late0[:], list_a[:])
+        lift_scales(nc.sync, late0, late1)
         part_words("b", 256, 256, 256)
-        round_wa(0, 0, on_scalar, 0, 2)
         layer("b", 256, 256, 0)
         gather_words("b", 512, 512, 0)
-        round_wa(0, 0, on_scalar, 2, 4)
+        layer("b", 256, 256, 1)
         gather_words("a", 0, 512, None)
         part_words("b", 512, 256, 512)
-        layer("b", 256, 256, 1)
-        round_wa(1, 0, on_scalar, 0, 2)
         part_words("a", 0, 512, 0)
         part_words("b", 768, 256, 512)
-        round_wa(1, 0, on_scalar, 2, 4)
+        for a in range(PASSES):
+            round_wa(a, 0, on_scalar, 0, 2)
+            round_wa(a, 0, on_scalar, 2, 4)
         layer("b", 512, 256, 0)
+        round_wa(0, 1, on_scalar, 0, 2)
         layer("b", 512, 256, 1)
-        apply_gain("b", 0, 0)
-        apply_gain("b", 0, 1)
-        quantize_h("b", 0, 0)
-        apply_gain("b", 256, 0)
-        quantize_h("b", 0, 1)
+
+        def gain_pair(side, first, slot=None):
+            apply_gain(side, first, 0)
+            apply_gain(side, first, 1, SHARE, slot)
+
+        def quantize_pair(side, first):
+            quantize_h(side, first, 0)
+            quantize_h(side, first, 1)
+
+        layer("b", 768, 256, 0)
+        gain_pair("b", 0)
+        round_wa(0, 1, on_vector, 2, 4)
+        quantize_pair("b", 0)
+        gain_pair("b", 256)
         quantize_wa(0, 0)
-        round_wa(0, 1, on_vector, 0, 4)
-        quantize_h("b", 256, 0)
-        apply_gain("b", 256, 1)
         quantize_wa(1, 0)
-        layer("a", 0, 256, 0)
         round_wa(1, 1, on_vector, 0, 4)
-        quantize_h("b", 256, 1)
         quantize_wa(0, 1)
         quantize_wa(1, 1)
-        layer("a", 0, 256, 1)
-        layer("a", 256, 256, 0)
-        layer("a", 256, 256, 1)
-        layer("b", 768, 256, 0)
+        quantize_pair("b", 256)
+        for first in (0, 256):
+            layer("a", first, 256, 0)
+            layer("a", first, 256, 1)
         layer("b", 768, 128, 1)
         layer("b", 896, 128, 1)
-        order = [("b", 512, 0), ("b", 512, 1), ("a", 0, 0), ("a", 0, 1), ("a", 256, 0), ("a", 256, 1)]
-        order = order + [("b", 768, 0), ("b", 768, 1), ("b", 896, 1)]
-        for i, unit in enumerate(order):
-            apply_gain(*unit)
-            if i > 0:
-                quantize_h(*order[i - 1])
-            if i == 4 or i == 6:
-                m0 = i - 4
-                scores(m0, 0, 512)
-                scores(m0 + 1, 0, 512)
-                scores(m0, 512, 256)
+        gain_pair("b", 512, "round11")
+        quantize_pair("b", 512)
+        for first in (0, 256):
+            gain_pair("a", first)
+            quantize_pair("a", first)
+            scores(first // P, 0, 512)
+            scores(first // P + 1, 0, 512)
+            scores(first // P, 512, 256)
+        apply_gain("b", 768, 0, SHARE // 2)
+        apply_gain("b", 768, 1)
+        quantize_h("b", 768, 0)
+        apply_gain("b", 896, 1)
+        quantize_h("b", 768, 1)
         scores(0, 768, 128)
-        quantize_h(*order[-1])
+        quantize_h("b", 896, 1)
         scores(0, 896, 128)

@@ -37,7 +37,7 @@ def tile_list_biaff_tanh_exp_kernel(
 
         list_b = keep.tile([P, J // 16], U16)
         list_a = keep.tile([P, M // 16], U16)
-        tab_s = keep.tile([P, T], U8, align_bytes=64, tag="then_words")
+        tab_s = keep.tile([P, T], U8, align_bytes=64)
         gain_raw = keep.tile([4, HALF], F32)
         gain_rows = keep.tile([P, PACK, P], F32)
         ident = keep.tile([P, P], F32)
@@ -114,14 +114,13 @@ def tile_list_biaff_tanh_exp_kernel(
         wb_s = keep.tile([P, 2, PASSES, PACK, 128], U8, align_bytes=64)
 
         def permute_wb_scales():
-            for g in range(2):
-                nc.gpsimd.tensor_copy(
-                    wb_s[:, g].bitcast(I32),
-                    wb_raw_s[:, :, 128 * g : 128 * (g + 1)].rearrange("p a (q t) -> p a t q", t=PACK),
-                )
+            nc.vector.tensor_copy(
+                wb_s[:].bitcast(I32),
+                wb_raw_s.rearrange("p a (g q t) -> p g a t q", g=2, t=PACK),
+            )
 
         def permute_wb(g):
-            nc.gpsimd.tensor_copy(
+            nc.vector.tensor_copy(
                 wb_w[:, g].bitcast(I32).rearrange("p a t (q w) -> p a t q w", w=2),
                 wb_raw_w[:, g].rearrange("p a (q t w) -> p a t q w", t=PACK, w=2),
             )
@@ -144,10 +143,7 @@ def tile_list_biaff_tanh_exp_kernel(
 
         def gather_words(side, first, n, place):
             offsets = (list_a if side == "a" else list_b)[:, first // 16 : (first + n) // 16]
-            if side == "a":
-                both = keep.tile([P, n], U32, name="both_a", align_bytes=64, tag="then_words")
-            else:
-                both = arena.tile([P, n], U32, name="both_b%d" % first, align_bytes=64, offset=place)
+            both = (arena if place < 4 * T else loads).tile([P, n], U32, name="both_%s%d" % (side, first), align_bytes=64, offset=place)
             nc.vector.tensor_copy(both[:], tab_w[:].bitcast(U32).indirect(offsets))
             words[side, first] = both
 
@@ -277,21 +273,21 @@ def tile_list_biaff_tanh_exp_kernel(
             lift_scales(nc.scalar, early0[:, cols], early1[:, cols])
         gather_words("b", 0, 256, 2048)
         permute_wb_scales()
-        permute_wb(0)
         part_words("b", 0, 256, 0)
+        permute_wb(0)
         load_wa()
         layer("b", 0, 256, 0, spare=True)
         turn_gains()
         permute_wb(1)
-        gather_words("b", 256, 256, 1280)
+        gather_words("b", 256, 256, 4 * T)
         layer("b", 0, 256, 1)
         gather_scales(late0[:], list_a[:])
         lift_scales(nc.sync, late0, late1)
         part_words("b", 256, 256, 256)
         layer("b", 256, 256, 0)
-        gather_words("b", 512, 512, 0)
+        gather_words("b", 512, 512, 4 * T + 512)
         layer("b", 256, 256, 1)
-        gather_words("a", 0, 512, None)
+        gather_words("a", 0, 512, 4 * T + 3072)
         part_words("b", 512, 256, 512)
         part_words("a", 0, 512, 0)
         part_words("b", 768, 256, 512)

@@ -21,7 +21,8 @@ PACK = 4
 PASSES = 2
 HALF = 512
 BANK = 512
-SHARE = 128
+SHARE = 120
+LAST_SHARE = 64
 
 
 def tile_list_biaff_tanh_exp_kernel(
@@ -69,18 +70,17 @@ def tile_list_biaff_tanh_exp_kernel(
         for q in range(4):
             nc.sync.dma_start(tab_s[32 * q : 32 * q + 8, :].bitcast(I32), tab_scales[:, 4 * q : 4 * q + 4, :].bitcast(I32))
         tab_w = loads.tile([P, T], I32, align_bytes=64, offset=0)
-        nc.sync.dma_start(tab_w[:], tab_words[0].rearrange("p t b -> p (t b)").bitcast(I32))
         wb_raw = loads.tile([P, R + R // 2], I32, align_bytes=64, offset=4 * T)
-        wb_raw_w = wb_raw[:, 0:R].rearrange("p (g a w) -> p g a w", g=2, a=PASSES)
+        wb_raw_w = wb_raw[:, 0:R].rearrange("p (a w) -> p a w", a=PASSES)
         wb_raw_s = wb_raw[:, R:].rearrange("p (a w) -> p a w", a=PASSES)
         nc.gpsimd.memset(wb_raw[:, R:], 0)
+        nc.sync.dma_start(wb_raw_w, wb_words.rearrange("a p b -> p a b").bitcast(I32))
         for q in range(4):
             nc.sync.dma_start(
                 wb_raw_s[32 * q : 32 * q + 4, :, :],
                 wb_scales[:, 4 * q : 4 * q + 4, :].rearrange("a r n -> r a n").bitcast(I32),
             )
-        for g in range(2):
-            nc.sync.dma_start(wb_raw_w[:, g], wb_words[:, :, R * g : R * (g + 1)].rearrange("a p b -> p a b").bitcast(I32))
+        nc.sync.dma_start(tab_w[:], tab_words[0].rearrange("p t b -> p (t b)").bitcast(I32))
         nc.vector.memset(gain_rows[:], 0.0)
         nc.vector.memset(early1[:].bitcast(I32), 0)
         nc.vector.memset(late1[:].bitcast(I32), 0)
@@ -101,7 +101,7 @@ def tile_list_biaff_tanh_exp_kernel(
         wa_raw = {}
 
         def load_wa():
-            wa_all = arena.tile([P, 2, PASSES, PACK, HALF], F32, align_bytes=64, offset=2816)
+            wa_all = loads.tile([P, 2, PASSES, PACK, HALF], F32, align_bytes=64, offset=4 * T + 1024)
             for g in range(2):
                 for a in range(PASSES):
                     nc.sync.dma_start(
@@ -110,19 +110,16 @@ def tile_list_biaff_tanh_exp_kernel(
                     )
                     wa_raw[a, g] = wa_all[:, g, a, :, :]
 
-        wb_w = keep.tile([P, 2, PASSES, PACK, 256], U8, align_bytes=64)
-        wb_s = keep.tile([P, 2, PASSES, PACK, 128], U8, align_bytes=64)
+        wb_w = keep.tile([P, PASSES, PACK, 512], U8, align_bytes=64)
+        wb_s = keep.tile([P, PASSES, PACK, 256], U8, align_bytes=64)
 
         def permute_wb_scales():
-            nc.vector.tensor_copy(
-                wb_s[:].bitcast(I32),
-                wb_raw_s.rearrange("p a (g q t) -> p g a t q", g=2, t=PACK),
-            )
+            nc.vector.tensor_copy(wb_s[:].bitcast(I32), wb_raw_s.rearrange("p a (q t) -> p a t q", t=PACK))
 
-        def permute_wb(g):
+        def permute_wb_words():
             nc.vector.tensor_copy(
-                wb_w[:, g].bitcast(I32).rearrange("p a t (q w) -> p a t q w", w=2),
-                wb_raw_w[:, g].rearrange("p a (q t w) -> p a t q w", t=PACK, w=2),
+                wb_w[:].bitcast(I32).rearrange("p a t (q w) -> p a t q w", w=2),
+                wb_raw_w.rearrange("p a (q t w) -> p a t q w", t=PACK, w=2),
             )
 
         gain = {}
@@ -143,12 +140,12 @@ def tile_list_biaff_tanh_exp_kernel(
 
         def gather_words(side, first, n, place):
             offsets = (list_a if side == "a" else list_b)[:, first // 16 : (first + n) // 16]
-            both = (arena if place < 4 * T else loads).tile([P, n], U32, name="both_%s%d" % (side, first), align_bytes=64, offset=place)
+            both = arena.tile([P, n], U32, name="both_%s%d" % (side, first), align_bytes=64, offset=place)
             nc.vector.tensor_copy(both[:], tab_w[:].bitcast(U32).indirect(offsets))
             words[side, first] = both
 
         parted = {}
-        slots = {("b", 0): "round10", ("b", 256): "round00", ("b", 512): "v_third", ("b", 768): "v_last", ("a", 0): "v_a"}
+        slots = {("b", 0): "round00", ("b", 256): "round01", ("b", 512): "v_rest", ("a", 0): "v_a"}
 
         def part_words(side, first, n, gathered):
             both = words[side, gathered][:, first - gathered : first - gathered + n]
@@ -177,7 +174,7 @@ def tile_list_biaff_tanh_exp_kernel(
 
         def weight_tile(side, a, g, t):
             if side == "b":
-                return wb_w[:, g, a, t, :].bitcast(FP4X4), wb_s[:, g, a, t, :]
+                return wb_w[:, a, t, 256 * g : 256 * (g + 1)].bitcast(FP4X4), wb_s[:, a, t, P * g : P * (g + 1)]
             cols = slice(P * t, P * (t + 1))
             return wa_codes[a, g][:, cols].bitcast(FP8X4), wa_scales[a, g][:, cols]
 
@@ -218,6 +215,8 @@ def tile_list_biaff_tanh_exp_kernel(
             banks, n, per_bank = act.shape[1:]
             if slot is None:
                 rounded = ring.tile([P, n, PACK], BF16, name="rounded", tag="rounded", bufs=2, align_bytes=64)
+            elif slot == "words_a":
+                rounded = arena.tile([P, n, PACK], BF16, name="rounded_first", align_bytes=64, offset=2816)
             else:
                 rounded = keep.tile([P, n, PACK], BF16, name="rounded", tag=slot, align_bytes=64)
             v = (0 if side == "a" else 2) + g
@@ -243,8 +242,7 @@ def tile_list_biaff_tanh_exp_kernel(
                 in_=rounded[:].rearrange("p n t -> p (n t)"),
             )
 
-        def scores(m0, j0, n):
-            tiles = BANK // n
+        def scores(m0, tiles, j0, n):
             y = next_bank([P, tiles, n], "y")
             for g in range(2):
                 for i in range(tiles):
@@ -258,7 +256,7 @@ def tile_list_biaff_tanh_exp_kernel(
                         start=(g == 0 and i == 0),
                         stop=(g == 1 and i == tiles - 1),
                     )
-            result = ring.tile([P, tiles, n], F32, name="result", tag="result", bufs=8)
+            result = ring.tile([P, tiles, n], F32, name="result", tag="result", bufs=9)
             nc.scalar.activation(result[:], y[:], ACT.Exp, scale=0.015625)
             nc.sync.dma_start(
                 out[P * m0 : P * (m0 + tiles), j0 : j0 + n].rearrange("(i p) j -> p i j", p=P),
@@ -271,31 +269,30 @@ def tile_list_biaff_tanh_exp_kernel(
             cols = slice(HALF * half, HALF * (half + 1))
             gather_scales(early0[:, cols], list_b[:, 32 * half : 32 * (half + 1)])
             lift_scales(nc.scalar, early0[:, cols], early1[:, cols])
-        gather_words("b", 0, 256, 2048)
+        permute_wb_words()
         permute_wb_scales()
-        part_words("b", 0, 256, 0)
-        permute_wb(0)
         load_wa()
+        gather_words("b", 0, 256, 2048)
+        part_words("b", 0, 256, 0)
         layer("b", 0, 256, 0, spare=True)
         turn_gains()
-        permute_wb(1)
-        gather_words("b", 256, 256, 4 * T)
-        layer("b", 0, 256, 1)
+        gather_words("b", 256, 256, 1280)
         gather_scales(late0[:], list_a[:])
         lift_scales(nc.sync, late0, late1)
+        layer("b", 0, 256, 1)
         part_words("b", 256, 256, 256)
+        round_wa(0, 0, on_scalar, 0, 2)
+        round_wa(0, 0, on_scalar, 2, 4)
         layer("b", 256, 256, 0)
-        gather_words("b", 512, 512, 4 * T + 512)
+        gather_words("b", 512, 512, 0)
+        round_wa(1, 0, on_scalar, 0, 2)
         layer("b", 256, 256, 1)
-        gather_words("a", 0, 512, 4 * T + 3072)
-        part_words("b", 512, 256, 512)
+        gather_words("a", 0, 512, 2816)
+        part_words("b", 512, 512, 512)
         part_words("a", 0, 512, 0)
-        part_words("b", 768, 256, 512)
-        for a in range(PASSES):
-            round_wa(a, 0, on_scalar, 0, 2)
-            round_wa(a, 0, on_scalar, 2, 4)
-        layer("b", 512, 256, 0)
         round_wa(0, 1, on_scalar, 0, 2)
+        round_wa(0, 1, on_scalar, 2, 4)
+        layer("b", 512, 256, 0)
         layer("b", 512, 256, 1)
 
         def gain_pair(side, first, slot=None):
@@ -306,20 +303,20 @@ def tile_list_biaff_tanh_exp_kernel(
             quantize_h(side, first, 0)
             quantize_h(side, first, 1)
 
-        layer("b", 768, 256, 0)
-        gain_pair("b", 0)
-        round_wa(0, 1, on_vector, 2, 4)
-        quantize_pair("b", 0)
-        gain_pair("b", 256)
+        gain_pair("b", 0, "words_a")
         quantize_wa(0, 0)
+        round_wa(1, 0, on_vector, 2, 4)
+        quantize_pair("b", 0)
         quantize_wa(1, 0)
+        gain_pair("b", 256, "round10")
         round_wa(1, 1, on_vector, 0, 4)
+        quantize_pair("b", 256)
         quantize_wa(0, 1)
         quantize_wa(1, 1)
-        quantize_pair("b", 256)
         for first in (0, 256):
             layer("a", first, 256, 0)
             layer("a", first, 256, 1)
+        layer("b", 768, 256, 0)
         layer("b", 768, 128, 1)
         layer("b", 896, 128, 1)
         gain_pair("b", 512, "round11")
@@ -327,14 +324,15 @@ def tile_list_biaff_tanh_exp_kernel(
         for first in (0, 256):
             gain_pair("a", first)
             quantize_pair("a", first)
-            scores(first // P, 0, 512)
-            scores(first // P + 1, 0, 512)
-            scores(first // P, 512, 256)
-        apply_gain("b", 768, 0, SHARE // 2)
+            scores(first // P, 1, 0, 512)
+            scores(first // P + 1, 1, 0, 512)
+            scores(first // P, 2, 512, 256)
+        apply_gain("b", 768, 0, LAST_SHARE)
         apply_gain("b", 768, 1)
         quantize_h("b", 768, 0)
         apply_gain("b", 896, 1)
         quantize_h("b", 768, 1)
-        scores(0, 768, 128)
+        scores(0, 4, 768, 128)
         quantize_h("b", 896, 1)
-        scores(0, 896, 128)
+        scores(0, 2, 896, 128)
+        scores(2, 2, 896, 128)

@@ -21,7 +21,9 @@ PACK = 4
 PASSES = 2
 HALF = 512
 BANK = 512
-SHARE = 120
+TABLE_AT = 4096
+WB_AT = TABLE_AT + 4 * T
+SHARE = 128
 LAST_SHARE = 64
 
 
@@ -42,26 +44,24 @@ def tile_list_biaff_tanh_exp_kernel(
         gain_raw = keep.tile([4, HALF], F32)
         gain_rows = keep.tile([P, PACK, P], F32)
         ident = keep.tile([P, P], F32)
-        zeros = loads.tile([P, P], F32, align_bytes=64, offset=4 * T - 256)
-        warm = keep.tile([P, 8], F32, align_bytes=64)
         early0 = keep.tile([P, J], U8, align_bytes=64)
         early1 = keep.tile([P, J], U8, align_bytes=64)
         late0 = arena.tile([P, M], U8, align_bytes=64, offset=2304)
         late1 = keep.tile([P, M], U8, align_bytes=64)
 
         nc.vector.memset(tab_s[:].bitcast(I32), 0)
-        nc.vector.memset(zeros[:], 0.0)
-        nc.vector.memset(warm[:], 0.0)
-        nc.gpsimd.affine_select(
-            out=ident[:],
-            in_=zeros[:],
-            compare_op=mybir.AluOpType.not_equal,
-            fill=1.0,
-            base=0,
-            pattern=[[-1, P]],
-            channel_multiplier=1,
-        )
-        nc.scalar.activation(warm[:], warm[:], ACT.Exp)
+        for half, place in enumerate((WB_AT - P, TABLE_AT - P)):
+            zeros = loads.tile([P, P // 2], F32, name="zeros%d" % half, align_bytes=64, offset=place)
+            nc.vector.memset(zeros[:], 0.0)
+            nc.gpsimd.affine_select(
+                out=ident[:, 64 * half : 64 * (half + 1)],
+                in_=zeros[:],
+                compare_op=mybir.AluOpType.not_equal,
+                fill=1.0,
+                base=-64 * half,
+                pattern=[[-1, P // 2]],
+                channel_multiplier=1,
+            )
 
         nc.sync.dma_start(list_b[:], offs2)
         nc.sync.dma_start(list_a[:], offs)
@@ -69,8 +69,8 @@ def tile_list_biaff_tanh_exp_kernel(
             nc.sync.dma_start(gain_raw[2 * v : 2 * v + 2, :], vec.rearrange("(g r) -> g r", g=2))
         for q in range(4):
             nc.sync.dma_start(tab_s[32 * q : 32 * q + 8, :].bitcast(I32), tab_scales[:, 4 * q : 4 * q + 4, :].bitcast(I32))
-        tab_w = loads.tile([P, T], I32, align_bytes=64, offset=0)
-        wb_raw = loads.tile([P, R + R // 2], I32, align_bytes=64, offset=4 * T)
+        tab_w = loads.tile([P, T], I32, align_bytes=64, offset=TABLE_AT)
+        wb_raw = loads.tile([P, R + R // 2], I32, align_bytes=64, offset=WB_AT)
         wb_raw_w = wb_raw[:, 0:R].rearrange("p (a w) -> p a w", a=PASSES)
         wb_raw_s = wb_raw[:, R:].rearrange("p (a w) -> p a w", a=PASSES)
         nc.gpsimd.memset(wb_raw[:, R:], 0)
@@ -100,14 +100,18 @@ def tile_list_biaff_tanh_exp_kernel(
 
         wa_raw = {}
 
+        def wa_rows(a, c0, c1):
+            return wa[512 * a : 512 * (a + 1), c0:c1].rearrange("(p j) c -> p j c", j=PACK)
+
+        wa_first = loads.tile([P, PACK, 256], F32, align_bytes=64, offset=0)
+        nc.sync.dma_start(wa_first[:], wa_rows(0, 0, 256))
+
         def load_wa():
-            wa_all = loads.tile([P, 2, PASSES, PACK, HALF], F32, align_bytes=64, offset=4 * T + 1024)
+            wa_all = loads.tile([P, 2, PASSES, PACK, HALF], F32, align_bytes=64, offset=WB_AT + 1024)
             for g in range(2):
                 for a in range(PASSES):
-                    nc.sync.dma_start(
-                        wa_all[:, g, a, :, :],
-                        wa[512 * a : 512 * (a + 1), HALF * g : HALF * (g + 1)].rearrange("(p j) c -> p j c", j=PACK),
-                    )
+                    h0 = 1 if (a, g) == (0, 0) else 0
+                    nc.sync.dma_start(wa_all[:, g, a, :, 256 * h0 :], wa_rows(a, HALF * g + 256 * h0, HALF * (g + 1)))
                     wa_raw[a, g] = wa_all[:, g, a, :, :]
 
         wb_w = keep.tile([P, PASSES, PACK, 512], U8, align_bytes=64)
@@ -145,7 +149,7 @@ def tile_list_biaff_tanh_exp_kernel(
             words[side, first] = both
 
         parted = {}
-        slots = {("b", 0): "round00", ("b", 256): "round01", ("b", 512): "v_rest", ("a", 0): "v_a"}
+        slots = {("b", 0): "round10", ("b", 256): "round01", ("b", 512): "v_rest", ("a", 0): "v_a"}
 
         def part_words(side, first, n, gathered):
             both = words[side, gathered][:, first - gathered : first - gathered + n]
@@ -156,12 +160,13 @@ def tile_list_biaff_tanh_exp_kernel(
 
         wa_grouped, wa_codes, wa_scales = {}, {}, {}
 
-        def round_wa(a, g, copy, t0, t1):
-            if t0 == 0:
+        def round_wa(a, g, c0, c1, copy):
+            if c0 == 0:
                 wa_grouped[a, g] = keep.tile([P, PACK, HALF], BF16, name="wa_grouped", tag="round%d%d" % (a, g), align_bytes=64)
+            raw = wa_first[:] if (a, g, c0) == (0, 0, 0) else wa_raw[a, g][:, :, c0:c1]
             copy(
-                wa_grouped[a, g][:, t0:t1, :].rearrange("p t (q i j) -> p t q j i", i=4, j=PACK),
-                wa_raw[a, g].rearrange("p j (q t i) -> p t q j i", t=PACK, i=4)[:, t0:t1],
+                wa_grouped[a, g][:, :, c0:c1].rearrange("p t (q i j) -> p t q j i", i=4, j=PACK),
+                raw.rearrange("p j (q t i) -> p t q j i", t=PACK, i=4),
             )
 
         def quantize_wa(a, g):
@@ -274,6 +279,7 @@ def tile_list_biaff_tanh_exp_kernel(
         load_wa()
         gather_words("b", 0, 256, 2048)
         part_words("b", 0, 256, 0)
+        round_wa(0, 0, 0, 256, on_scalar)
         layer("b", 0, 256, 0, spare=True)
         turn_gains()
         gather_words("b", 256, 256, 1280)
@@ -281,17 +287,17 @@ def tile_list_biaff_tanh_exp_kernel(
         lift_scales(nc.sync, late0, late1)
         layer("b", 0, 256, 1)
         part_words("b", 256, 256, 256)
-        round_wa(0, 0, on_scalar, 0, 2)
-        round_wa(0, 0, on_scalar, 2, 4)
+        round_wa(0, 0, 256, 512, on_scalar)
+        round_wa(1, 0, 0, 256, on_scalar)
         layer("b", 256, 256, 0)
         gather_words("b", 512, 512, 0)
-        round_wa(1, 0, on_scalar, 0, 2)
+        round_wa(1, 0, 256, 512, on_scalar)
         layer("b", 256, 256, 1)
         gather_words("a", 0, 512, 2816)
         part_words("b", 512, 512, 512)
         part_words("a", 0, 512, 0)
-        round_wa(0, 1, on_scalar, 0, 2)
-        round_wa(0, 1, on_scalar, 2, 4)
+        round_wa(0, 1, 0, 256, on_scalar)
+        round_wa(0, 1, 256, 512, on_scalar)
         layer("b", 512, 256, 0)
         layer("b", 512, 256, 1)
 
@@ -305,11 +311,10 @@ def tile_list_biaff_tanh_exp_kernel(
 
         gain_pair("b", 0, "words_a")
         quantize_wa(0, 0)
-        round_wa(1, 0, on_vector, 2, 4)
         quantize_pair("b", 0)
         quantize_wa(1, 0)
         gain_pair("b", 256, "round10")
-        round_wa(1, 1, on_vector, 0, 4)
+        round_wa(1, 1, 0, 512, on_vector)
         quantize_pair("b", 256)
         quantize_wa(0, 1)
         quantize_wa(1, 1)

@@ -20,9 +20,20 @@ P = 128
 PACK = 4
 PASSES = 2
 HALF = 512
+UNIT = 256
 BANK = 512
-TABLE_AT = 4096
-WB_AT = TABLE_AT + 4 * T
+EARLY_BANKS = 4
+ROTATING_BANKS = 7
+WB_WORDS_AT = 0
+FIRST_AT = WB_WORDS_AT + 3072
+SECOND_WORDS_AT = FIRST_AT + 4 * PACK * HALF
+WB_AT = SECOND_WORDS_AT + 768
+PARTED_AT = WB_AT + 256
+SCALES_A_AT = WB_AT + 1280
+TABLE_AT = WB_AT + 2048
+GAINS_AT = TABLE_AT + 4 * T
+WA_AT = GAINS_AT + 1024
+WORDS_AT = {("b", 0): 2048, ("b", 512): 256, ("a", 0): 2816}
 SHARE = 128
 LAST_SHARE = 64
 
@@ -41,96 +52,107 @@ def tile_list_biaff_tanh_exp_kernel(
         list_b = keep.tile([P, J // 16], U16)
         list_a = keep.tile([P, M // 16], U16)
         tab_s = keep.tile([P, T], U8, align_bytes=64)
-        gain_raw = keep.tile([4, HALF], F32)
+        gain_raw = loads.tile([4, HALF], F32, align_bytes=64, offset=GAINS_AT)
+        blank = keep.tile([P, 2 * P], F32)
         gain_rows = keep.tile([P, PACK, P], F32)
         ident = keep.tile([P, P], F32)
-        early0 = keep.tile([P, J], U8, align_bytes=64)
-        early1 = keep.tile([P, J], U8, align_bytes=64)
-        late0 = arena.tile([P, M], U8, align_bytes=64, offset=2304)
-        late1 = keep.tile([P, M], U8, align_bytes=64)
+        b_plane0 = keep.tile([P, J], U8, align_bytes=64)
+        b_plane1 = keep.tile([P, J], U8, align_bytes=64)
+        a_plane0 = loads.tile([P, M], U8, align_bytes=64, offset=SCALES_A_AT)
+        a_plane1 = keep.tile([P, M], U8, align_bytes=64)
 
         nc.vector.memset(tab_s[:].bitcast(I32), 0)
-        for half, place in enumerate((WB_AT - P, TABLE_AT - P)):
-            zeros = loads.tile([P, P // 2], F32, name="zeros%d" % half, align_bytes=64, offset=place)
+        for t, place in enumerate((TABLE_AT - 256, GAINS_AT)):
+            zeros = loads.tile([P, P], F32, name="zeros%d" % t, align_bytes=64, offset=place)
             nc.vector.memset(zeros[:], 0.0)
-            nc.gpsimd.affine_select(
-                out=ident[:, 64 * half : 64 * (half + 1)],
-                in_=zeros[:],
-                compare_op=mybir.AluOpType.not_equal,
-                fill=1.0,
-                base=-64 * half,
-                pattern=[[-1, P // 2]],
-                channel_multiplier=1,
-            )
-
+            nc.vector.tensor_copy(gain_rows[:, t, :], zeros[:])
+        wb_raw_w = loads.tile([P, PASSES, R // 2], I32, align_bytes=64, offset=WB_WORDS_AT)
+        nc.sync.dma_start(wb_raw_w[:], wb_words.rearrange("a p b -> p a b").bitcast(I32))
         nc.sync.dma_start(list_b[:], offs2)
         nc.sync.dma_start(list_a[:], offs)
+        for r in range(4):
+            nc.sync.dma_start(
+                tab_s[r:P:16, :].bitcast(I32), tab_scales[:, r:16:4, :].rearrange("a q n -> q a n").bitcast(I32)
+            )
+        tab_w = loads.tile([P, T], I32, align_bytes=64, offset=TABLE_AT)
+        nc.sync.dma_start(tab_w[:], tab_words[0].rearrange("p t b -> p (t b)").bitcast(I32))
         for v, vec in enumerate((sa, sb)):
             nc.sync.dma_start(gain_raw[2 * v : 2 * v + 2, :], vec.rearrange("(g r) -> g r", g=2))
-        for q in range(4):
-            nc.sync.dma_start(tab_s[32 * q : 32 * q + 8, :].bitcast(I32), tab_scales[:, 4 * q : 4 * q + 4, :].bitcast(I32))
-        tab_w = loads.tile([P, T], I32, align_bytes=64, offset=TABLE_AT)
-        wb_raw = loads.tile([P, R + R // 2], I32, align_bytes=64, offset=WB_AT)
-        wb_raw_w = wb_raw[:, 0:R].rearrange("p (a w) -> p a w", a=PASSES)
-        wb_raw_s = wb_raw[:, R:].rearrange("p (a w) -> p a w", a=PASSES)
-        nc.gpsimd.memset(wb_raw[:, R:], 0)
-        nc.sync.dma_start(wb_raw_w, wb_words.rearrange("a p b -> p a b").bitcast(I32))
-        for q in range(4):
+        wb_raw_s = loads.tile([P, PASSES, R // 4], I32, align_bytes=64, offset=WB_AT)
+        nc.vector.memset(wb_raw_s[:], 0)
+        for r in range(4):
             nc.sync.dma_start(
-                wb_raw_s[32 * q : 32 * q + 4, :, :],
-                wb_scales[:, 4 * q : 4 * q + 4, :].rearrange("a r n -> r a n").bitcast(I32),
+                wb_raw_s[r:P:32, :, :], wb_scales[:, r:16:4, :].rearrange("a q n -> q a n").bitcast(I32)
             )
-        nc.sync.dma_start(tab_w[:], tab_words[0].rearrange("p t b -> p (t b)").bitcast(I32))
-        nc.vector.memset(gain_rows[:], 0.0)
-        nc.vector.memset(early1[:].bitcast(I32), 0)
-        nc.vector.memset(late1[:].bitcast(I32), 0)
-        nc.scalar.copy(
-            gain_rows[0:4].rearrange("v t (q i) -> v t q i", i=4),
-            gain_raw[:].rearrange("v (q t i) -> v t q i", t=PACK, i=4),
+        nc.vector.memset(blank[:], 0.0)
+        nc.scalar.copy(gain_rows[:, 2:4, :].rearrange("p t c -> p (t c)"), blank[:])
+        nc.gpsimd.affine_select(
+            out=ident[:],
+            in_=blank[:, 0:P],
+            compare_op=mybir.AluOpType.not_equal,
+            fill=1.0,
+            base=0,
+            pattern=[[-1, P]],
+            channel_multiplier=1,
         )
+        nc.vector.memset(b_plane1[:].bitcast(I32), 0)
+        nc.vector.memset(a_plane1[:].bitcast(I32), 0)
+
+        def load_gains():
+            nc.scalar.copy(
+                gain_rows[0:4].rearrange("v t (q i) -> v t q i", i=4),
+                gain_raw[:].rearrange("v (q t i) -> v t q i", t=PACK, i=4),
+            )
 
         def gather_scales(picked, offsets):
             nc.vector.tensor_copy(picked, tab_s[:].indirect(offsets))
 
         def lift_scales(queue, plane0, plane1):
-            queue.dma_start(plane1[0:112, :].bitcast(I32), plane0[4:116, :].bitcast(I32))
+            queue.dma_start(plane1[0:112, :].bitcast(I32), plane0[16:128, :].bitcast(I32))
 
         def entry_scales(side, first, n, a):
-            return ((late0, late1) if side == "a" else (early0, early1))[a][:, first : first + n]
+            return ((a_plane0, a_plane1) if side == "a" else (b_plane0, b_plane1))[a][:, first : first + n]
 
         wa_raw = {}
 
         def wa_rows(a, c0, c1):
             return wa[512 * a : 512 * (a + 1), c0:c1].rearrange("(p j) c -> p j c", j=PACK)
 
-        wa_first = loads.tile([P, PACK, 256], F32, align_bytes=64, offset=0)
-        nc.sync.dma_start(wa_first[:], wa_rows(0, 0, 256))
+        def load_wa_first():
+            wa_first = loads.tile([P, 2, PACK, UNIT], F32, align_bytes=64, offset=FIRST_AT)
+            for h in range(2):
+                nc.sync.dma_start(wa_first[:, h], wa_rows(0, UNIT * h, UNIT * (h + 1)))
+                wa_raw[0, UNIT * h] = wa_first[:, h]
 
         def load_wa():
-            wa_all = loads.tile([P, 2, PASSES, PACK, HALF], F32, align_bytes=64, offset=WB_AT + 1024)
-            for g in range(2):
-                for a in range(PASSES):
-                    h0 = 1 if (a, g) == (0, 0) else 0
-                    nc.sync.dma_start(wa_all[:, g, a, :, 256 * h0 :], wa_rows(a, HALF * g + 256 * h0, HALF * (g + 1)))
-                    wa_raw[a, g] = wa_all[:, g, a, :, :]
+            wa_rest = loads.tile([P, 3 * PACK * HALF], F32, align_bytes=64, offset=WA_AT)
+            place = 0
+            for a, c0, c1 in ((1, 0, UNIT), (0, HALF, R), (1, UNIT, HALF), (1, HALF, R)):
+                piece = wa_rest[:, place : place + PACK * (c1 - c0)].rearrange("p (j c) -> p j c", j=PACK)
+                nc.sync.dma_start(piece, wa_rows(a, c0, c1))
+                wa_raw[a, c0] = piece
+                place = place + PACK * (c1 - c0)
 
-        wb_w = keep.tile([P, PASSES, PACK, 512], U8, align_bytes=64)
-        wb_s = keep.tile([P, PASSES, PACK, 256], U8, align_bytes=64)
+        wb_w = keep.tile([P, PACK, PASSES, 512], U8, align_bytes=64)
+        wb_s = keep.tile([P, PACK, PASSES, 256], U8, align_bytes=64)
 
         def permute_wb_scales():
-            nc.vector.tensor_copy(wb_s[:].bitcast(I32), wb_raw_s.rearrange("p a (q t) -> p a t q", t=PACK))
+            nc.vector.tensor_copy(
+                wb_s[:].bitcast(I32).rearrange("p (u e) a q -> p u (a q) e", e=2),
+                wb_raw_s[:].rearrange("p a (q u e) -> p u (a q) e", u=2, e=2),
+            )
 
         def permute_wb_words():
             nc.vector.tensor_copy(
-                wb_w[:].bitcast(I32).rearrange("p a t (q w) -> p a t q w", w=2),
-                wb_raw_w.rearrange("p a (q t w) -> p a t q w", t=PACK, w=2),
+                wb_w[:].bitcast(I32).rearrange("p t a (q w) -> p t (a q) w", w=2),
+                wb_raw_w[:].rearrange("p a (q t w) -> p t (a q) w", t=PACK, w=2),
             )
 
         gain = {}
-        turn = [0]
+        turn = [-1]
 
-        def next_bank(shape, name):
-            turn[0] = (turn[0] + 1) % 7
+        def next_bank(shape, name, rotation=ROTATING_BANKS):
+            turn[0] = (turn[0] + 1) % rotation
             return psum.tile(shape, F32, tag="bank%d" % turn[0], name=name)
 
         def turn_gains():
@@ -138,22 +160,29 @@ def tile_list_biaff_tanh_exp_kernel(
             for t in range(PACK):
                 nc.tensor.transpose(gain["ps"][:, :, t], gain_rows[:, t, :], ident[:])
             gain["sb"] = keep.tile([P, 4, PACK], F32, name="gain_sb")
-            nc.vector.tensor_copy(gain["sb"][:], gain["ps"][:, 0:4, :])
+            nc.scalar.copy(gain["sb"][:], gain["ps"][:, 0:4, :])
 
         words = {}
 
-        def gather_words(side, first, n, place):
+        def gather_words(side, first, n):
             offsets = (list_a if side == "a" else list_b)[:, first // 16 : (first + n) // 16]
-            both = arena.tile([P, n], U32, name="both_%s%d" % (side, first), align_bytes=64, offset=place)
+            if first == UNIT:
+                both = loads.tile([P, n], U32, name="both_second", align_bytes=64, offset=SECOND_WORDS_AT)
+            else:
+                both = arena.tile([P, n], U32, name="both_%s%d" % (side, first), align_bytes=64, offset=WORDS_AT[side, first])
             nc.vector.tensor_copy(both[:], tab_w[:].bitcast(U32).indirect(offsets))
             words[side, first] = both
 
         parted = {}
-        slots = {("b", 0): "round10", ("b", 256): "round01", ("b", 512): "v_rest", ("a", 0): "v_a"}
+        slots = {("b", 256): "round01", ("b", 512): "v_rest", ("a", 0): "v_a"}
 
-        def part_words(side, first, n, gathered):
-            both = words[side, gathered][:, first - gathered : first - gathered + n]
-            tile = keep.tile([P, PASSES, 2 * n], U8, name="parted", tag=slots[side, first], align_bytes=64)
+        def part_words(side, first):
+            both = words[side, first][:]
+            n = both.shape[1]
+            if (side, first) == ("b", 0):
+                tile = loads.tile([P, PASSES, 2 * n], U8, name="parted_first", align_bytes=64, offset=PARTED_AT)
+            else:
+                tile = keep.tile([P, PASSES, 2 * n], U8, name="parted", tag=slots[side, first], align_bytes=64)
             nc.vector.tensor_copy(tile[:].bitcast(U16), both.bitcast(U16).rearrange("p (n d) -> p d n", d=PASSES))
             for c in range(0, n, P):
                 parted[side, first + c] = tile[:, :, 2 * c :]
@@ -162,8 +191,10 @@ def tile_list_biaff_tanh_exp_kernel(
 
         def round_wa(a, g, c0, c1, copy):
             if c0 == 0:
-                wa_grouped[a, g] = keep.tile([P, PACK, HALF], BF16, name="wa_grouped", tag="round%d%d" % (a, g), align_bytes=64)
-            raw = wa_first[:] if (a, g, c0) == (0, 0, 0) else wa_raw[a, g][:, :, c0:c1]
+                wa_grouped[a, g] = keep.tile(
+                    [P, PACK, HALF], BF16, name="wa_grouped", tag="round%d%d" % (a, g), align_bytes=64
+                )
+            raw = wa_raw[a, c0] if g == 0 else wa_raw[a, HALF][:, :, c0:c1]
             copy(
                 wa_grouped[a, g][:, :, c0:c1].rearrange("p t (q i j) -> p t q j i", i=4, j=PACK),
                 raw.rearrange("p j (q t i) -> p t q j i", t=PACK, i=4),
@@ -179,7 +210,7 @@ def tile_list_biaff_tanh_exp_kernel(
 
         def weight_tile(side, a, g, t):
             if side == "b":
-                return wb_w[:, a, t, 256 * g : 256 * (g + 1)].bitcast(FP4X4), wb_s[:, a, t, P * g : P * (g + 1)]
+                return wb_w[:, t, a, 256 * g : 256 * (g + 1)].bitcast(FP4X4), wb_s[:, t, a, P * g : P * (g + 1)]
             cols = slice(P * t, P * (t + 1))
             return wa_codes[a, g][:, cols].bitcast(FP8X4), wa_scales[a, g][:, cols]
 
@@ -191,15 +222,12 @@ def tile_list_biaff_tanh_exp_kernel(
                 h_codes[side, g] = keep.tile([P, count], U32, name="h%s%d_codes" % (side, g), align_bytes=64)
                 h_scales[side, g] = keep.tile([P, count], U8, name="h%s%d_scales" % (side, g), align_bytes=64)
 
-        def layer(side, first, n, g, spare=False):
+        def layer(side, first, n, g, rotation=ROTATING_BANKS):
             per_bank = BANK // n
             banks = PACK // per_bank
             act = ring.tile([P, banks, n, per_bank], F32, name="act", tag="act", bufs=10, align_bytes=64)
             for u in range(banks):
-                if spare and u == 0:
-                    z = psum.tile([P, per_bank, n], F32, tag="bank7", name="z")
-                else:
-                    z = next_bank([P, per_bank, n], "z")
+                z = next_bank([P, per_bank, n], "z", rotation)
                 for e in range(per_bank):
                     for a in range(PASSES):
                         codes, scales = weight_tile(side, a, g, per_bank * u + e)
@@ -221,7 +249,7 @@ def tile_list_biaff_tanh_exp_kernel(
             if slot is None:
                 rounded = ring.tile([P, n, PACK], BF16, name="rounded", tag="rounded", bufs=2, align_bytes=64)
             elif slot == "words_a":
-                rounded = arena.tile([P, n, PACK], BF16, name="rounded_first", align_bytes=64, offset=2816)
+                rounded = arena.tile([P, n, PACK], BF16, name="rounded_first", align_bytes=64, offset=WORDS_AT["a", 0])
             else:
                 rounded = keep.tile([P, n, PACK], BF16, name="rounded", tag=slot, align_bytes=64)
             v = (0 if side == "a" else 2) + g
@@ -270,36 +298,37 @@ def tile_list_biaff_tanh_exp_kernel(
 
         on_scalar, on_vector = nc.scalar.copy, nc.vector.tensor_copy
 
-        for half in range(2):
-            cols = slice(HALF * half, HALF * (half + 1))
-            gather_scales(early0[:, cols], list_b[:, 32 * half : 32 * (half + 1)])
-            lift_scales(nc.scalar, early0[:, cols], early1[:, cols])
         permute_wb_words()
-        permute_wb_scales()
-        load_wa()
-        gather_words("b", 0, 256, 2048)
-        part_words("b", 0, 256, 0)
-        round_wa(0, 0, 0, 256, on_scalar)
-        layer("b", 0, 256, 0, spare=True)
+        load_gains()
         turn_gains()
-        gather_words("b", 256, 256, 1280)
-        gather_scales(late0[:], list_a[:])
-        lift_scales(nc.sync, late0, late1)
-        layer("b", 0, 256, 1)
-        part_words("b", 256, 256, 256)
+        load_wa_first()
+        for half in range(2):
+            gather_scales(b_plane0[:, HALF * half : HALF * (half + 1)], list_b[:, 32 * half : 32 * (half + 1)])
+        lift_scales(nc.sync, b_plane0, b_plane1)
+        gather_words("b", 0, 256)
+        permute_wb_scales()
+        part_words("b", 0)
+        gather_words("b", 256, 256)
+        load_wa()
+        round_wa(0, 0, 0, 256, on_scalar)
         round_wa(0, 0, 256, 512, on_scalar)
+        layer("b", 0, 256, 0, EARLY_BANKS)
+        gather_scales(a_plane0[:], list_a[:])
+        lift_scales(nc.sync, a_plane0, a_plane1)
+        layer("b", 0, 256, 1, EARLY_BANKS)
+        part_words("b", 256)
+        layer("b", 256, 256, 0, EARLY_BANKS)
+        gather_words("b", 512, 512)
+        layer("b", 256, 256, 1, EARLY_BANKS)
+        gather_words("a", 0, 512)
+        part_words("b", 512)
+        part_words("a", 0)
         round_wa(1, 0, 0, 256, on_scalar)
-        layer("b", 256, 256, 0)
-        gather_words("b", 512, 512, 0)
         round_wa(1, 0, 256, 512, on_scalar)
-        layer("b", 256, 256, 1)
-        gather_words("a", 0, 512, 2816)
-        part_words("b", 512, 512, 512)
-        part_words("a", 0, 512, 0)
         round_wa(0, 1, 0, 256, on_scalar)
         round_wa(0, 1, 256, 512, on_scalar)
-        layer("b", 512, 256, 0)
-        layer("b", 512, 256, 1)
+        layer("b", 512, 256, 0, EARLY_BANKS)
+        layer("b", 512, 256, 1, EARLY_BANKS)
 
         def gain_pair(side, first, slot=None):
             apply_gain(side, first, 0)
@@ -312,8 +341,8 @@ def tile_list_biaff_tanh_exp_kernel(
         gain_pair("b", 0, "words_a")
         quantize_wa(0, 0)
         quantize_pair("b", 0)
+        gain_pair("b", 256, "words_a")
         quantize_wa(1, 0)
-        gain_pair("b", 256, "round10")
         round_wa(1, 1, 0, 512, on_vector)
         quantize_pair("b", 256)
         quantize_wa(0, 1)

@@ -22,6 +22,11 @@ PASSES = 2
 HALF = 512
 UNIT = 256
 BANK = 512
+PAIRS = (("b", 0), ("b", 256), ("b", 512), ("a", 0), ("a", 256), ("b", 768), ("b", 896))
+ACT_BYTES = 4096
+ROUNDED_BYTES = 2048
+SLOT_AT = {"round01": 2 * len(PAIRS) * ACT_BYTES, "round11": (2 * len(PAIRS) + 1) * ACT_BYTES}
+FIRST_ROUNDED_AT = (2 * len(PAIRS) + 2) * ACT_BYTES
 EARLY_BANKS = 4
 ROTATING_BANKS = 7
 WB_WORDS_AT = 0
@@ -34,8 +39,12 @@ TABLE_AT = WB_AT + 2048
 GAINS_AT = TABLE_AT + 4 * T
 WA_AT = GAINS_AT + 1024
 WORDS_AT = {("b", 0): 2048, ("b", 512): 256, ("a", 0): 2816}
-SHARE = 128
-LAST_SHARE = 64
+SHARE = 144
+LAST_SHARE = 48
+
+
+def act_at(side, first, g):
+    return ACT_BYTES * (len(PAIRS) * g + PAIRS.index((side, first)))
 
 
 def tile_list_biaff_tanh_exp_kernel(
@@ -47,6 +56,7 @@ def tile_list_biaff_tanh_exp_kernel(
         ring = ctx.enter_context(tc.tile_pool(name="ring", bufs=3))
         arena = ctx.enter_context(tc.tile_pool(name="arena", bufs=1))
         loads = ctx.enter_context(tc.tile_pool(name="loads", bufs=1))
+        steps = ctx.enter_context(tc.tile_pool(name="steps", bufs=1))
         psum = ctx.enter_context(tc.psum_pool(name="psum", bufs=1))
 
         list_b = keep.tile([P, J // 16], U16)
@@ -150,13 +160,15 @@ def tile_list_biaff_tanh_exp_kernel(
 
         gain = {}
         turn = [-1]
+        taken = []
 
         def next_bank(shape, name, rotation=ROTATING_BANKS):
             turn[0] = (turn[0] + 1) % rotation
-            return psum.tile(shape, F32, tag="bank%d" % turn[0], name=name)
+            taken.append(turn[0])
+            return psum.tile(shape, F32, offset=4 * BANK * turn[0], name="%s%d" % (name, len(taken)))
 
         def turn_gains():
-            gain["ps"] = psum.tile([P, P, PACK], F32, tag="bank7", name="gain_ps")
+            gain["ps"] = psum.tile([P, P, PACK], F32, offset=4 * BANK * ROTATING_BANKS, name="gain_ps")
             for t in range(PACK):
                 nc.tensor.transpose(gain["ps"][:, :, t], gain_rows[:, t, :], ident[:])
             gain["sb"] = keep.tile([P, 4, PACK], F32, name="gain_sb")
@@ -174,15 +186,16 @@ def tile_list_biaff_tanh_exp_kernel(
             words[side, first] = both
 
         parted = {}
-        slots = {("b", 256): "round01", ("b", 512): "v_rest", ("a", 0): "v_a"}
 
         def part_words(side, first):
             both = words[side, first][:]
             n = both.shape[1]
             if (side, first) == ("b", 0):
                 tile = loads.tile([P, PASSES, 2 * n], U8, name="parted_first", align_bytes=64, offset=PARTED_AT)
+            elif (side, first) == ("b", 256):
+                tile = steps.tile([P, PASSES, 2 * n], U8, name="parted_second", align_bytes=64, offset=SLOT_AT["round01"])
             else:
-                tile = keep.tile([P, PASSES, 2 * n], U8, name="parted", tag=slots[side, first], align_bytes=64)
+                tile = keep.tile([P, PASSES, 2 * n], U8, name="parted_%s" % side, align_bytes=64)
             nc.vector.tensor_copy(tile[:].bitcast(U16), both.bitcast(U16).rearrange("p (n d) -> p d n", d=PASSES))
             for c in range(0, n, P):
                 parted[side, first + c] = tile[:, :, 2 * c :]
@@ -191,9 +204,11 @@ def tile_list_biaff_tanh_exp_kernel(
 
         def round_wa(a, g, c0, c1, copy):
             if c0 == 0:
-                wa_grouped[a, g] = keep.tile(
-                    [P, PACK, HALF], BF16, name="wa_grouped", tag="round%d%d" % (a, g), align_bytes=64
-                )
+                name = "round%d%d" % (a, g)
+                if g == 0:
+                    wa_grouped[a, g] = keep.tile([P, PACK, HALF], BF16, name=name, align_bytes=64)
+                else:
+                    wa_grouped[a, g] = steps.tile([P, PACK, HALF], BF16, name=name, align_bytes=64, offset=SLOT_AT[name])
             raw = wa_raw[a, c0] if g == 0 else wa_raw[a, HALF][:, :, c0:c1]
             copy(
                 wa_grouped[a, g][:, :, c0:c1].rearrange("p t (q i j) -> p t q j i", i=4, j=PACK),
@@ -225,7 +240,9 @@ def tile_list_biaff_tanh_exp_kernel(
         def layer(side, first, n, g, rotation=ROTATING_BANKS):
             per_bank = BANK // n
             banks = PACK // per_bank
-            act = ring.tile([P, banks, n, per_bank], F32, name="act", tag="act", bufs=10, align_bytes=64)
+            act = steps.tile(
+                [P, banks, n, per_bank], F32, name="act%d" % len(acts), align_bytes=64, offset=act_at(side, first, g)
+            )
             for u in range(banks):
                 z = next_bank([P, per_bank, n], "z", rotation)
                 for e in range(per_bank):
@@ -243,15 +260,11 @@ def tile_list_biaff_tanh_exp_kernel(
                 nc.scalar.activation(act[:, u, :, :], z[:].rearrange("p e n -> p n e"), ACT.Tanh)
             acts[side, first, g] = act
 
-        def apply_gain(side, first, g, share=0, slot=None):
+        def apply_gain(side, first, g, pool, place, share=0):
             act = acts[side, first, g]
             banks, n, per_bank = act.shape[1:]
-            if slot is None:
-                rounded = ring.tile([P, n, PACK], BF16, name="rounded", tag="rounded", bufs=2, align_bytes=64)
-            elif slot == "words_a":
-                rounded = arena.tile([P, n, PACK], BF16, name="rounded_first", align_bytes=64, offset=WORDS_AT["a", 0])
-            else:
-                rounded = keep.tile([P, n, PACK], BF16, name="rounded", tag=slot, align_bytes=64)
+            name = "rounded_%s%d_%d" % (side, first, g)
+            rounded = pool.tile([P, n, PACK], BF16, name=name, align_bytes=64, offset=place)
             v = (0 if side == "a" else 2) + g
             parts = [(nc.vector, gain["ps"][:, v, :], 0, n - share)]
             if share:
@@ -326,47 +339,52 @@ def tile_list_biaff_tanh_exp_kernel(
         round_wa(1, 0, 0, 256, on_scalar)
         round_wa(1, 0, 256, 512, on_scalar)
         round_wa(0, 1, 0, 256, on_scalar)
-        round_wa(0, 1, 256, 512, on_scalar)
+        round_wa(0, 1, 256, 384, on_scalar)
         layer("b", 512, 256, 0, EARLY_BANKS)
         layer("b", 512, 256, 1, EARLY_BANKS)
 
-        def gain_pair(side, first, slot=None):
-            apply_gain(side, first, 0)
-            apply_gain(side, first, 1, SHARE, slot)
+        def gain_pair(side, first, alone_at, shared_at, shared_pool=steps, share=SHARE):
+            apply_gain(side, first, 0, steps, alone_at)
+            apply_gain(side, first, 1, shared_pool, shared_at, share)
+
+        def after_share(side, first):
+            return act_at(side, first, 1) + ROUNDED_BYTES // 2
 
         def quantize_pair(side, first):
             quantize_h(side, first, 0)
             quantize_h(side, first, 1)
 
-        gain_pair("b", 0, "words_a")
         quantize_wa(0, 0)
+        gain_pair("b", 0, FIRST_ROUNDED_AT, WORDS_AT["a", 0], arena)
         quantize_pair("b", 0)
-        gain_pair("b", 256, "words_a")
+        gain_pair("b", 256, after_share("b", 0), FIRST_ROUNDED_AT)
         quantize_wa(1, 0)
+        round_wa(0, 1, 384, 512, on_vector)
         round_wa(1, 1, 0, 512, on_vector)
         quantize_pair("b", 256)
-        quantize_wa(0, 1)
         quantize_wa(1, 1)
+        quantize_wa(0, 1)
         for first in (0, 256):
             layer("a", first, 256, 0)
             layer("a", first, 256, 1)
-        layer("b", 768, 256, 0)
-        layer("b", 768, 128, 1)
-        layer("b", 896, 128, 1)
-        gain_pair("b", 512, "round11")
+        for first in (768, 896):
+            layer("b", first, 128, 0)
+            layer("b", first, 128, 1)
+        gain_pair("b", 512, SLOT_AT["round11"], SLOT_AT["round11"] + ROUNDED_BYTES)
         quantize_pair("b", 512)
-        for first in (0, 256):
-            gain_pair("a", first)
+        for first, alone_at, shared_at in (
+            (0, after_share("b", 512), SLOT_AT["round11"]),
+            (256, after_share("a", 0), after_share("b", 512)),
+        ):
+            gain_pair("a", first, alone_at, shared_at)
             quantize_pair("a", first)
             scores(first // P, 1, 0, 512)
             scores(first // P + 1, 1, 0, 512)
             scores(first // P, 2, 512, 256)
-        apply_gain("b", 768, 0, LAST_SHARE)
-        apply_gain("b", 768, 1)
-        quantize_h("b", 768, 0)
-        apply_gain("b", 896, 1)
-        quantize_h("b", 768, 1)
+        gain_pair("b", 768, after_share("a", 256), after_share("a", 0), share=LAST_SHARE)
+        quantize_pair("b", 768)
         scores(0, 4, 768, 128)
-        quantize_h("b", 896, 1)
+        gain_pair("b", 896, after_share("b", 768), after_share("a", 256), share=LAST_SHARE)
+        quantize_pair("b", 896)
         scores(0, 2, 896, 128)
         scores(2, 2, 896, 128)

@@ -15,68 +15,91 @@ FP8X4 = mybir.dt.float8_e4m3fn_x4
 FP4X4 = mybir.dt.float4_e2m1fn_x4
 ACT = mybir.ActivationFunctionType
 MULT = mybir.AluOpType.mult
+ADD = mybir.AluOpType.add
 
 P = 128
 PACK = 4
 PASSES = 2
 HALF = 512
-UNIT = 256
+SLAB = 256
 BANK = 512
-PAIRS = (("b", 0), ("b", 256), ("b", 512), ("a", 0), ("a", 256), ("b", 768), ("b", 896))
-ACT_BYTES = 4096
-ROUNDED_BYTES = 2048
-SLOT_AT = {"round01": 2 * len(PAIRS) * ACT_BYTES, "round11": (2 * len(PAIRS) + 1) * ACT_BYTES}
-FIRST_ROUNDED_AT = (2 * len(PAIRS) + 2) * ACT_BYTES
-EARLY_BANKS = 4
 ROTATING_BANKS = 7
-WB_WORDS_AT = 0
-FIRST_AT = WB_WORDS_AT + 3072
-SECOND_WORDS_AT = FIRST_AT + 4 * PACK * HALF
-WB_AT = SECOND_WORDS_AT + 768
-PARTED_AT = WB_AT + 256
-SCALES_A_AT = WB_AT + 1280
-TABLE_AT = WB_AT + 2048
-GAINS_AT = TABLE_AT + 4 * T
-WA_AT = GAINS_AT + 1024
-WORDS_AT = {("b", 0): 2048, ("b", 512): 256, ("a", 0): 2816}
+EDGE = 64
 SHARE = 144
+FIRST_CUT = 384
 LAST_SHARE = 48
 
+REGIONS = (
+    ("wb_words", 4096, 0),
+    ("raw00", 8192, EDGE),
+    ("round10", 4096, 0),
+    ("words_256", 1024, EDGE),
+    ("wb_scales", 2048, EDGE),
+    ("table", 8192, 0),
+    ("raw10", 8192, 0),
+    ("gains", 2048, EDGE),
+    ("raw01", 8192, EDGE),
+    ("gain_rows", 2048, 0),
+    ("raw11", 8192, EDGE),
+    ("words_a", 2048, 0),
+    ("words_0", 1024, EDGE),
+    ("words_512", 2048, EDGE),
+    ("act0", 4096, 0),
+    ("parted_256", 4096, 0),
+    ("round11a", 2048, 0),
+    ("rounded_first", 2048, 0),
+    ("act1", 4608, 0),
+    ("act2", 4096, 0),
+    ("act3", 4096, 0),
+    ("act5", 4096, 0),
+    ("act6", 4096, 0),
+    ("act7", 4096, 0),
+    ("act8", 4096, 0),
+    ("act9", 4096, 0),
+    ("act10", 4096, 0),
+    ("act11", 4096, 0),
+)
 
-def act_at(side, first, g):
-    return ACT_BYTES * (len(PAIRS) * g + PAIRS.index((side, first)))
+
+def region_starts():
+    starts, top = {}, 0
+    for name, size, shared in REGIONS:
+        starts[name] = top - shared
+        top = starts[name] + size
+    return starts
 
 
 def tile_list_biaff_tanh_exp_kernel(
     tc, tab_words, tab_scales, wa, wb_words, wb_scales, sa, sb, offs, offs2, out
 ):
     nc = tc.nc
+    at = region_starts()
     with ExitStack() as ctx:
         keep = ctx.enter_context(tc.tile_pool(name="keep", bufs=1))
-        ring = ctx.enter_context(tc.tile_pool(name="ring", bufs=3))
-        arena = ctx.enter_context(tc.tile_pool(name="arena", bufs=1))
-        loads = ctx.enter_context(tc.tile_pool(name="loads", bufs=1))
-        steps = ctx.enter_context(tc.tile_pool(name="steps", bufs=1))
+        mem = ctx.enter_context(tc.tile_pool(name="mem", bufs=1))
         psum = ctx.enter_context(tc.psum_pool(name="psum", bufs=1))
+
+        def tile(name, shape, dtype, place=None):
+            if place is None:
+                return keep.tile(shape, dtype, name=name, align_bytes=64)
+            return mem.tile(shape, dtype, name=name, align_bytes=64, offset=place)
 
         list_b = keep.tile([P, J // 16], U16)
         list_a = keep.tile([P, M // 16], U16)
-        tab_s = keep.tile([P, T], U8, align_bytes=64)
-        gain_raw = loads.tile([4, HALF], F32, align_bytes=64, offset=GAINS_AT)
-        blank = keep.tile([P, 2 * P], F32)
-        gain_rows = keep.tile([P, PACK, P], F32)
-        ident = keep.tile([P, P], F32)
-        b_plane0 = keep.tile([P, J], U8, align_bytes=64)
-        b_plane1 = keep.tile([P, J], U8, align_bytes=64)
-        a_plane0 = loads.tile([P, M], U8, align_bytes=64, offset=SCALES_A_AT)
-        a_plane1 = keep.tile([P, M], U8, align_bytes=64)
+        tab_s = tile("tab_s", [P, T], U8)
+        gain_raw = tile("gain_raw", [4, HALF], F32, at["gains"])
+        gain_rows = tile("gain_rows", [P, PACK, P], F32, at["gain_rows"])
+        blank = tile("blank", [P, 2 * P], F32)
+        ident = tile("ident", [P, P], F32)
+        planes = {"b": [tile("plane_b%d" % a, [P, J], U8) for a in range(PASSES)]}
+        planes["a"] = [tile("plane_a0", [P, M], U8, at["words_0"] + EDGE), tile("plane_a1", [P, M], U8)]
 
         nc.vector.memset(tab_s[:].bitcast(I32), 0)
-        for t, place in enumerate((TABLE_AT - 256, GAINS_AT)):
-            zeros = loads.tile([P, P], F32, name="zeros%d" % t, align_bytes=64, offset=place)
+        for t, place in enumerate((at["table"] - 256, at["gains"] + 256)):
+            zeros = tile("zeros%d" % t, [P, P], F32, place)
             nc.vector.memset(zeros[:], 0.0)
             nc.vector.tensor_copy(gain_rows[:, t, :], zeros[:])
-        wb_raw_w = loads.tile([P, PASSES, R // 2], I32, align_bytes=64, offset=WB_WORDS_AT)
+        wb_raw_w = tile("wb_raw_w", [P, PASSES, R // 2], I32, at["wb_words"])
         nc.sync.dma_start(wb_raw_w[:], wb_words.rearrange("a p b -> p a b").bitcast(I32))
         nc.sync.dma_start(list_b[:], offs2)
         nc.sync.dma_start(list_a[:], offs)
@@ -84,11 +107,11 @@ def tile_list_biaff_tanh_exp_kernel(
             nc.sync.dma_start(
                 tab_s[r:P:16, :].bitcast(I32), tab_scales[:, r:16:4, :].rearrange("a q n -> q a n").bitcast(I32)
             )
-        tab_w = loads.tile([P, T], I32, align_bytes=64, offset=TABLE_AT)
+        tab_w = tile("tab_w", [P, T], I32, at["table"])
         nc.sync.dma_start(tab_w[:], tab_words[0].rearrange("p t b -> p (t b)").bitcast(I32))
         for v, vec in enumerate((sa, sb)):
             nc.sync.dma_start(gain_raw[2 * v : 2 * v + 2, :], vec.rearrange("(g r) -> g r", g=2))
-        wb_raw_s = loads.tile([P, PASSES, R // 4], I32, align_bytes=64, offset=WB_AT)
+        wb_raw_s = tile("wb_raw_s", [P, PASSES, R // 4], I32, at["wb_scales"])
         nc.vector.memset(wb_raw_s[:], 0)
         for r in range(4):
             nc.sync.dma_start(
@@ -105,286 +128,263 @@ def tile_list_biaff_tanh_exp_kernel(
             pattern=[[-1, P]],
             channel_multiplier=1,
         )
-        nc.vector.memset(b_plane1[:].bitcast(I32), 0)
-        nc.vector.memset(a_plane1[:].bitcast(I32), 0)
+        for key in planes:
+            nc.vector.memset(planes[key][1][:].bitcast(I32), 0)
 
-        def load_gains():
-            nc.scalar.copy(
-                gain_rows[0:4].rearrange("v t (q i) -> v t q i", i=4),
-                gain_raw[:].rearrange("v (q t i) -> v t q i", t=PACK, i=4),
-            )
+        raw = {}
+
+        def load_wa(name, a, cuts):
+            whole = tile(name, [P, PACK * HALF], F32, at[name])
+            for c0, c1 in zip(cuts, cuts[1:]):
+                place = PACK * (c0 - cuts[0])
+                piece = whole[:, place : place + PACK * (c1 - c0)].rearrange("p (j c) -> p j c", j=PACK)
+                nc.sync.dma_start(piece, wa[512 * a : 512 * (a + 1), c0:c1].rearrange("(p j) c -> p j c", j=PACK))
+                raw[name, c0 - cuts[0]] = piece
+
+        wb_w = tile("wb_w", [P, PACK, PASSES, 512], U8)
+        wb_s = tile("wb_s", [P, PACK, PASSES, 256], U8)
 
         def gather_scales(picked, offsets):
             nc.vector.tensor_copy(picked, tab_s[:].indirect(offsets))
 
-        def lift_scales(queue, plane0, plane1):
-            queue.dma_start(plane1[0:112, :].bitcast(I32), plane0[16:128, :].bitcast(I32))
+        def lift(queue, key):
+            queue.dma_start(planes[key][1][0:112, :].bitcast(I32), planes[key][0][16:128, :].bitcast(I32))
 
-        def entry_scales(side, first, n, a):
-            return ((a_plane0, a_plane1) if side == "a" else (b_plane0, b_plane1))[a][:, first : first + n]
+        words, parted = {}, {}
 
-        wa_raw = {}
-
-        def wa_rows(a, c0, c1):
-            return wa[512 * a : 512 * (a + 1), c0:c1].rearrange("(p j) c -> p j c", j=PACK)
-
-        def load_wa_first():
-            wa_first = loads.tile([P, 2, PACK, UNIT], F32, align_bytes=64, offset=FIRST_AT)
-            for h in range(2):
-                nc.sync.dma_start(wa_first[:, h], wa_rows(0, UNIT * h, UNIT * (h + 1)))
-                wa_raw[0, UNIT * h] = wa_first[:, h]
-
-        def load_wa():
-            wa_rest = loads.tile([P, 3 * PACK * HALF], F32, align_bytes=64, offset=WA_AT)
-            place = 0
-            for a, c0, c1 in ((1, 0, UNIT), (0, HALF, R), (1, UNIT, HALF), (1, HALF, R)):
-                piece = wa_rest[:, place : place + PACK * (c1 - c0)].rearrange("p (j c) -> p j c", j=PACK)
-                nc.sync.dma_start(piece, wa_rows(a, c0, c1))
-                wa_raw[a, c0] = piece
-                place = place + PACK * (c1 - c0)
-
-        wb_w = keep.tile([P, PACK, PASSES, 512], U8, align_bytes=64)
-        wb_s = keep.tile([P, PACK, PASSES, 256], U8, align_bytes=64)
-
-        def permute_wb_scales():
-            nc.vector.tensor_copy(
-                wb_s[:].bitcast(I32).rearrange("p (u e) a q -> p u (a q) e", e=2),
-                wb_raw_s[:].rearrange("p a (q u e) -> p u (a q) e", u=2, e=2),
-            )
-
-        def permute_wb_words():
-            nc.vector.tensor_copy(
-                wb_w[:].bitcast(I32).rearrange("p t a (q w) -> p t (a q) w", w=2),
-                wb_raw_w[:].rearrange("p a (q t w) -> p t (a q) w", t=PACK, w=2),
-            )
-
-        gain = {}
-        turn = [-1]
-        taken = []
-
-        def next_bank(shape, name, rotation=ROTATING_BANKS):
-            turn[0] = (turn[0] + 1) % rotation
-            taken.append(turn[0])
-            return psum.tile(shape, F32, offset=4 * BANK * turn[0], name="%s%d" % (name, len(taken)))
-
-        def turn_gains():
-            gain["ps"] = psum.tile([P, P, PACK], F32, offset=4 * BANK * ROTATING_BANKS, name="gain_ps")
-            for t in range(PACK):
-                nc.tensor.transpose(gain["ps"][:, :, t], gain_rows[:, t, :], ident[:])
-            gain["sb"] = keep.tile([P, 4, PACK], F32, name="gain_sb")
-            nc.scalar.copy(gain["sb"][:], gain["ps"][:, 0:4, :])
-
-        words = {}
-
-        def gather_words(side, first, n):
+        def gather_words(side, first, n, place):
             offsets = (list_a if side == "a" else list_b)[:, first // 16 : (first + n) // 16]
-            if first == UNIT:
-                both = loads.tile([P, n], U32, name="both_second", align_bytes=64, offset=SECOND_WORDS_AT)
-            else:
-                both = arena.tile([P, n], U32, name="both_%s%d" % (side, first), align_bytes=64, offset=WORDS_AT[side, first])
+            both = tile("words_%s%d" % (side, first), [P, n], U32, place)
             nc.vector.tensor_copy(both[:], tab_w[:].bitcast(U32).indirect(offsets))
             words[side, first] = both
 
-        parted = {}
-
-        def part_words(side, first):
+        def part_words(side, first, place=None):
             both = words[side, first][:]
             n = both.shape[1]
-            if (side, first) == ("b", 0):
-                tile = loads.tile([P, PASSES, 2 * n], U8, name="parted_first", align_bytes=64, offset=PARTED_AT)
-            elif (side, first) == ("b", 256):
-                tile = steps.tile([P, PASSES, 2 * n], U8, name="parted_second", align_bytes=64, offset=SLOT_AT["round01"])
-            else:
-                tile = keep.tile([P, PASSES, 2 * n], U8, name="parted_%s" % side, align_bytes=64)
-            nc.vector.tensor_copy(tile[:].bitcast(U16), both.bitcast(U16).rearrange("p (n d) -> p d n", d=PASSES))
+            runs = tile("parted_%s%d" % (side, first), [P, PASSES, 2 * n], U8, place)
+            nc.vector.tensor_copy(runs[:].bitcast(U16), both.bitcast(U16).rearrange("p (n d) -> p d n", d=PASSES))
             for c in range(0, n, P):
-                parted[side, first + c] = tile[:, :, 2 * c :]
+                parted[side, first + c] = runs[:, :, 2 * c :]
 
-        wa_grouped, wa_codes, wa_scales = {}, {}, {}
+        def entry_scales(side, first, n, a):
+            return planes[side][a][:, first : first + n]
 
-        def round_wa(a, g, c0, c1, copy):
-            if c0 == 0:
-                name = "round%d%d" % (a, g)
-                if g == 0:
-                    wa_grouped[a, g] = keep.tile([P, PACK, HALF], BF16, name=name, align_bytes=64)
-                else:
-                    wa_grouped[a, g] = steps.tile([P, PACK, HALF], BF16, name=name, align_bytes=64, offset=SLOT_AT[name])
-            raw = wa_raw[a, c0] if g == 0 else wa_raw[a, HALF][:, :, c0:c1]
-            copy(
-                wa_grouped[a, g][:, :, c0:c1].rearrange("p t (q i j) -> p t q j i", i=4, j=PACK),
-                raw.rearrange("p j (q t i) -> p t q j i", t=PACK, i=4),
-            )
+        turn = [0]
 
-        def quantize_wa(a, g):
-            codes = keep.tile([P, HALF], U32, name="wa_codes_%d%d" % (a, g), align_bytes=64)
-            scales = keep.tile([P, HALF], U8, name="wa_scales_%d%d" % (a, g), align_bytes=64)
+        def next_bank(shape):
+            turn[0] = turn[0] + 1
+            return psum.tile(shape, F32, offset=4 * BANK * ((turn[0] - 1) % ROTATING_BANKS), name="bank%d" % turn[0])
+
+        def grouped_view(grouped, c0, c1, walk):
+            return grouped[:, :, c0:c1].rearrange("p t (q i j) -> p " + walk, i=4, j=PACK)
+
+        def raw_view(name, c0, walk):
+            return raw[name, c0].rearrange("p j (q t i) -> p " + walk, t=PACK, i=4)
+
+        wa_tiles = {}
+
+        def quantize_wa(a, g, t0, grouped, place):
+            n = grouped.shape[1] * P
+            codes = tile("wa_codes_%d%d%d" % (a, g, t0), [P, n], U32)
+            scales = tile("wa_scales_%d%d%d" % (a, g, t0), [P, n], U8, place)
             nc.vector.quantize_mx(
-                out=codes[:].bitcast(FP8X4), scales=scales[:], in_=wa_grouped[a, g][:].rearrange("p t c -> p (t c)")
+                out=codes[:].bitcast(FP8X4), scales=scales[:], in_=grouped[:].rearrange("p t c -> p (t c)")
             )
-            wa_codes[a, g], wa_scales[a, g] = codes, scales
+            for c in range(0, n, P):
+                wa_tiles[a, g, t0 + c // P] = (codes[:, c : c + P].bitcast(FP8X4), scales[:, c : c + P])
 
         def weight_tile(side, a, g, t):
             if side == "b":
                 return wb_w[:, t, a, 256 * g : 256 * (g + 1)].bitcast(FP4X4), wb_s[:, t, a, P * g : P * (g + 1)]
-            cols = slice(P * t, P * (t + 1))
-            return wa_codes[a, g][:, cols].bitcast(FP8X4), wa_scales[a, g][:, cols]
+            return wa_tiles[a, g, t]
 
-        acts, values = {}, {}
-        h_codes = {}
-        h_scales = {}
-        for side, count in (("a", M), ("b", J)):
-            for g in range(2):
-                h_codes[side, g] = keep.tile([P, count], U32, name="h%s%d_codes" % (side, g), align_bytes=64)
-                h_scales[side, g] = keep.tile([P, count], U8, name="h%s%d_scales" % (side, g), align_bytes=64)
+        acts, rounded, h_codes, h_scales = {}, {}, {}, {}
 
-        def layer(side, first, n, g, rotation=ROTATING_BANKS):
-            per_bank = BANK // n
-            banks = PACK // per_bank
-            act = steps.tile(
-                [P, banks, n, per_bank], F32, name="act%d" % len(acts), align_bytes=64, offset=act_at(side, first, g)
-            )
-            for u in range(banks):
-                z = next_bank([P, per_bank, n], "z", rotation)
-                for e in range(per_bank):
-                    for a in range(PASSES):
-                        codes, scales = weight_tile(side, a, g, per_bank * u + e)
-                        nc.tensor.matmul_mx(
-                            out=z[:, e, :],
-                            lhsT=codes,
-                            lhsT_scale=scales,
-                            rhs=parted[side, first][:, a, 0 : 2 * n].bitcast(FP4X4),
-                            rhs_scale=entry_scales(side, first, n, a),
-                            start=(a == 0),
-                            stop=(a == PASSES - 1),
-                        )
-                nc.scalar.activation(act[:, u, :, :], z[:].rearrange("p e n -> p n e"), ACT.Tanh)
-            acts[side, first, g] = act
+        def layer(slab, place, unlifted_first=False):
+            side, first, halves = slab
+            n = SLAB // len(halves)
+            act = tile("act_%s%d_%d" % (side, first, halves[0]), [P, 2, SLAB, 2], F32, place)
+            for u in range(2):
+                z = next_bank([P, len(halves), 2, n])
+                if unlifted_first:
+                    passes = [(0, e, a, e + a == 0, e + a == 2) for a in range(PASSES) for e in range(2)]
+                else:
+                    passes = [(k, e, a, a == 1, a == 0) for k in range(len(halves)) for e in range(2) for a in (1, 0)]
+                for k, e, a, start, stop in passes:
+                    codes, scales = weight_tile(side, a, halves[k], 2 * u + e)
+                    nc.tensor.matmul_mx(
+                        out=z[:, k, e, :],
+                        lhsT=codes,
+                        lhsT_scale=scales,
+                        rhs=parted[side, first][:, a, 0 : 2 * n].bitcast(FP4X4),
+                        rhs_scale=entry_scales(side, first, n, a),
+                        start=start,
+                        stop=stop,
+                    )
+                nc.scalar.activation(
+                    act[:, u, :, :].rearrange("p (k n) e -> p k n e", n=n), z[:].rearrange("p k e n -> p k n e"), ACT.Tanh
+                )
+            acts[slab] = act
 
-        def apply_gain(side, first, g, pool, place, share=0):
-            act = acts[side, first, g]
-            banks, n, per_bank = act.shape[1:]
-            name = "rounded_%s%d_%d" % (side, first, g)
-            rounded = pool.tile([P, n, PACK], BF16, name=name, align_bytes=64, offset=place)
-            v = (0 if side == "a" else 2) + g
-            parts = [(nc.vector, gain["ps"][:, v, :], 0, n - share)]
+        def apply_gain(slab, place, share=0):
+            side, first, halves = slab
+            n = SLAB // len(halves)
+            values = tile("rounded_%s%d_%d" % (side, first, halves[0]), [P, SLAB, PACK], BF16, place)
+            parts = [(nc.vector, gain_ps, g, n * k, min(n * (k + 1), SLAB - share)) for k, g in enumerate(halves)]
             if share:
-                parts.append((nc.gpsimd, gain["sb"][:, v, :], n - share, n))
-            for engine, factor, c0, c1 in parts:
-                factor = factor.rearrange("p (u e) -> p u e", u=banks)
+                parts.append((nc.gpsimd, gain_sb, halves[-1], SLAB - share, SLAB))
+            for engine, gains, g, c0, c1 in parts:
+                factor = gains[:, (0 if side == "a" else 2) + g, :].rearrange("p (u e) -> p u e", u=2)
                 engine.tensor_tensor(
-                    rounded[:, c0:c1, :].rearrange("p n (u e) -> p n u e", u=banks),
-                    act[:, :, c0:c1, :].rearrange("p u n e -> p n u e"),
-                    factor.unsqueeze(1).to_broadcast([P, c1 - c0, banks, per_bank]),
+                    values[:, c0:c1, :].rearrange("p n (u e) -> p n u e", u=2),
+                    acts[slab][:, :, c0:c1, :].rearrange("p u n e -> p n u e"),
+                    factor.unsqueeze(1).to_broadcast([P, c1 - c0, 2, 2]),
                     MULT,
                 )
-            values[side, first, g] = rounded
+            rounded[slab] = values
 
-        def quantize_h(side, first, g):
-            rounded = values[side, first, g]
-            n = rounded.shape[1]
-            nc.vector.quantize_mx(
-                out=h_codes[side, g][:, first : first + n].bitcast(FP8X4),
-                scales=h_scales[side, g][:, first : first + n],
-                in_=rounded[:].rearrange("p n t -> p (n t)"),
-            )
+        def quantize_h(slab, place=None, calls=1):
+            side, first, halves = slab
+            n = SLAB // len(halves)
+            codes = tile("codes_%s%d_%d" % (side, first, halves[0]), [P, SLAB], U32)
+            scales = tile("scales_%s%d_%d" % (side, first, halves[0]), [P, SLAB], U8, place)
+            for c in range(0, SLAB, SLAB // calls):
+                cols = slice(c, c + SLAB // calls)
+                nc.vector.quantize_mx(
+                    out=codes[:, cols].bitcast(FP8X4),
+                    scales=scales[:, cols],
+                    in_=rounded[slab][:, cols, :].rearrange("p n t -> p (n t)"),
+                )
+            for k, g in enumerate(halves):
+                for c in range(0, n, P):
+                    h_codes[side, first + c, g] = codes[:, n * k + c :]
+                    h_scales[side, first + c, g] = scales[:, n * k + c :]
 
-        def scores(m0, tiles, j0, n):
-            y = next_bank([P, tiles, n], "y")
-            for g in range(2):
-                for i in range(tiles):
-                    rows = slice(P * (m0 + i), P * (m0 + i + 1))
-                    nc.tensor.matmul_mx(
-                        out=y[:, i, :],
-                        lhsT=h_codes["a", g][:, rows].bitcast(FP8X4),
-                        lhsT_scale=h_scales["a", g][:, rows],
-                        rhs=h_codes["b", g][:, j0 : j0 + n].bitcast(FP8X4),
-                        rhs_scale=h_scales["b", g][:, j0 : j0 + n],
-                        start=(g == 0 and i == 0),
-                        stop=(g == 1 and i == tiles - 1),
-                    )
-            result = ring.tile([P, tiles, n], F32, name="result", tag="result", bufs=9)
+        def scores(row_tiles, chunks):
+            j0 = chunks[0][0]
+            width = sum(n for first, n in chunks)
+            y = next_bank([P, len(row_tiles), width])
+            passes = [(g, i, first, n) for g in range(2) for i in range(len(row_tiles)) for first, n in chunks]
+            for k, (g, i, first, n) in enumerate(passes):
+                m0 = P * row_tiles[i]
+                nc.tensor.matmul_mx(
+                    out=y[:, i, first - j0 : first - j0 + n],
+                    lhsT=h_codes["a", m0, g][:, 0:P].bitcast(FP8X4),
+                    lhsT_scale=h_scales["a", m0, g][:, 0:P],
+                    rhs=h_codes["b", first, g][:, 0:n].bitcast(FP8X4),
+                    rhs_scale=h_scales["b", first, g][:, 0:n],
+                    start=(k == 0),
+                    stop=(k == len(passes) - 1),
+                )
+            result = tile("result_%d_%d" % (row_tiles[0], j0), [P, len(row_tiles), width], F32)
             nc.scalar.activation(result[:], y[:], ACT.Exp, scale=0.015625)
-            nc.sync.dma_start(
-                out[P * m0 : P * (m0 + tiles), j0 : j0 + n].rearrange("(i p) j -> p i j", p=P),
-                result[:],
+            rows = slice(P * row_tiles[0], P * (row_tiles[-1] + 1))
+            nc.sync.dma_start(out[rows, j0 : j0 + width].rearrange("(i p) j -> p i j", p=P), result[:])
+
+        b0, b1, b2, b3, b4, b5 = [("b", first, (g,)) for first in (0, 256, 512) for g in range(2)]
+        a0, a1, a2, a3 = [("a", first, (g,)) for first in (0, 256) for g in range(2)]
+        b6, b7 = [("b", first, (0, 1)) for first in (768, 896)]
+
+        nc.vector.tensor_copy(
+            wb_w[:].bitcast(I32).rearrange("p t a (q w) -> p t (a q) w", w=2),
+            wb_raw_w[:].rearrange("p a (q t w) -> p t (a q) w", t=PACK, w=2),
+        )
+        nc.scalar.copy(
+            gain_rows[0:4].rearrange("v t (q i) -> v t q i", i=4),
+            gain_raw[:].rearrange("v (q t i) -> v t q i", t=PACK, i=4),
+        )
+        gain_ps = psum.tile([P, P, PACK], F32, offset=4 * BANK * ROTATING_BANKS, name="gain_ps")
+        for t in range(PACK):
+            nc.tensor.transpose(gain_ps[:, :, t], gain_rows[:, t, :], ident[:])
+        gain_sb = tile("gain_sb", [P, 4, PACK], F32)
+        nc.scalar.copy(gain_sb[:], gain_ps[:, 0:4, :])
+        load_wa("raw00", 0, (0, FIRST_CUT, HALF))
+        for h in range(2):
+            gather_scales(planes["b"][0][:, HALF * h : HALF * (h + 1)], list_b[:, 32 * h : 32 * (h + 1)])
+        lift(nc.sync, "b")
+        load_wa("raw10", 1, (0, 256, HALF))
+        load_wa("raw01", 0, (HALF, R))
+        load_wa("raw11", 1, (HALF, R))
+        gather_words("b", 0, 256, at["words_0"])
+        nc.vector.tensor_copy(
+            wb_s[:].bitcast(I32).rearrange("p (u e) a q -> p u (a q) e", e=2),
+            wb_raw_s[:].rearrange("p a (q u e) -> p u (a q) e", u=2, e=2),
+        )
+        part_words("b", 0, at["wb_scales"] + EDGE)
+        gather_words("b", 256, 256, at["words_256"])
+        part_words("b", 256, at["parted_256"])
+        round00 = tile("round00", [P, PACK, HALF], BF16)
+        for c0, c1 in ((0, FIRST_CUT), (FIRST_CUT, HALF)):
+            nc.scalar.copy(grouped_view(round00, c0, c1, "t q j i"), raw_view("raw00", c0, "t q j i"))
+        layer(b0, at["act0"], True)
+        layer(b1, at["act1"])
+        layer(b2, at["act2"])
+        layer(b3, at["act3"])
+
+        gather_words("b", 512, 512, at["words_512"])
+        gather_scales(planes["a"][0][:], list_a[:])
+        lift(nc.sync, "a")
+        gather_words("a", 0, 512, at["words_a"])
+        round10 = tile("round10", [P, PACK, HALF], BF16, at["round10"])
+        for h in range(2):
+            nc.gpsimd.tensor_scalar(
+                grouped_view(round10, 256 * h, 256 * (h + 1), "q t i j"),
+                raw_view("raw10", 256 * h, "q t i j"),
+                1.0,
+                0.0,
+                MULT,
+                ADD,
             )
+        apply_gain(b1, at["rounded_first"])
+        apply_gain(b0, None)
+        quantize_h(b1)
+        part_words("b", 512, at["act0"])
+        part_words("a", 0, at["act0"] + 2048)
+        quantize_h(b0)
 
-        on_scalar, on_vector = nc.scalar.copy, nc.vector.tensor_copy
+        round01 = tile("round01", [P, PACK, HALF], BF16, at["parted_256"])
+        nc.scalar.copy(grouped_view(round01, 0, HALF, "t q j i"), raw_view("raw01", 0, "t q j i"))
+        round11a = tile("round11a", [P, 2, HALF], BF16)
+        nc.scalar.copy(grouped_view(round11a, 0, HALF, "t q j i"), raw_view("raw11", 0, "t q j i")[:, 0:2])
+        for slab, place in ((b4, at["raw01"] + EDGE), (b5, at["act5"])):
+            layer(slab, place)
 
-        permute_wb_words()
-        load_gains()
-        turn_gains()
-        load_wa_first()
-        for half in range(2):
-            gather_scales(b_plane0[:, HALF * half : HALF * (half + 1)], list_b[:, 32 * half : 32 * (half + 1)])
-        lift_scales(nc.sync, b_plane0, b_plane1)
-        gather_words("b", 0, 256)
-        permute_wb_scales()
-        part_words("b", 0)
-        gather_words("b", 256, 256)
-        load_wa()
-        round_wa(0, 0, 0, 256, on_scalar)
-        round_wa(0, 0, 256, 512, on_scalar)
-        layer("b", 0, 256, 0, EARLY_BANKS)
-        gather_scales(a_plane0[:], list_a[:])
-        lift_scales(nc.sync, a_plane0, a_plane1)
-        layer("b", 0, 256, 1, EARLY_BANKS)
-        part_words("b", 256)
-        layer("b", 256, 256, 0, EARLY_BANKS)
-        gather_words("b", 512, 512)
-        layer("b", 256, 256, 1, EARLY_BANKS)
-        gather_words("a", 0, 512)
-        part_words("b", 512)
-        part_words("a", 0)
-        round_wa(1, 0, 0, 256, on_scalar)
-        round_wa(1, 0, 256, 512, on_scalar)
-        round_wa(0, 1, 0, 256, on_scalar)
-        round_wa(0, 1, 256, 384, on_scalar)
-        layer("b", 512, 256, 0, EARLY_BANKS)
-        layer("b", 512, 256, 1, EARLY_BANKS)
+        apply_gain(b3, at["words_512"])
+        apply_gain(b2, at["words_a"], SHARE)
+        quantize_h(b3)
+        round11b = tile("round11b", [P, 2, HALF], BF16, at["act2"] + 2048)
+        nc.vector.tensor_copy(grouped_view(round11b, 0, HALF, "t q j i"), raw_view("raw11", 0, "t q j i")[:, 2:4])
+        quantize_wa(0, 0, 0, round00, at["act2"])
+        quantize_wa(1, 0, 0, round10, at["act2"] + 512)
+        quantize_wa(0, 1, 0, round01, at["act2"] + 1024)
+        quantize_wa(1, 1, 0, round11a, at["act2"] + 1536)
+        quantize_wa(1, 1, 2, round11b, None)
+        quantize_h(b2, at["parted_256"] + 2048)
+        for slab, place in ((a0, at["act7"]), (a1, at["act8"]), (a2, at["act9"]), (a3, at["act10"]), (b6, at["act6"]), (b7, at["act11"])):
+            layer(slab, place)
 
-        def gain_pair(side, first, alone_at, shared_at, shared_pool=steps, share=SHARE):
-            apply_gain(side, first, 0, steps, alone_at)
-            apply_gain(side, first, 1, shared_pool, shared_at, share)
-
-        def after_share(side, first):
-            return act_at(side, first, 1) + ROUNDED_BYTES // 2
-
-        def quantize_pair(side, first):
-            quantize_h(side, first, 0)
-            quantize_h(side, first, 1)
-
-        quantize_wa(0, 0)
-        gain_pair("b", 0, FIRST_ROUNDED_AT, WORDS_AT["a", 0], arena)
-        quantize_pair("b", 0)
-        gain_pair("b", 256, after_share("b", 0), FIRST_ROUNDED_AT)
-        quantize_wa(1, 0)
-        round_wa(0, 1, 384, 512, on_vector)
-        round_wa(1, 1, 0, 512, on_vector)
-        quantize_pair("b", 256)
-        quantize_wa(1, 1)
-        quantize_wa(0, 1)
-        for first in (0, 256):
-            layer("a", first, 256, 0)
-            layer("a", first, 256, 1)
-        for first in (768, 896):
-            layer("b", first, 128, 0)
-            layer("b", first, 128, 1)
-        gain_pair("b", 512, SLOT_AT["round11"], SLOT_AT["round11"] + ROUNDED_BYTES)
-        quantize_pair("b", 512)
-        for first, alone_at, shared_at in (
-            (0, after_share("b", 512), SLOT_AT["round11"]),
-            (256, after_share("a", 0), after_share("b", 512)),
-        ):
-            gain_pair("a", first, alone_at, shared_at)
-            quantize_pair("a", first)
-            scores(first // P, 1, 0, 512)
-            scores(first // P + 1, 1, 0, 512)
-            scores(first // P, 2, 512, 256)
-        gain_pair("b", 768, after_share("a", 256), after_share("a", 0), share=LAST_SHARE)
-        quantize_pair("b", 768)
-        scores(0, 4, 768, 128)
-        gain_pair("b", 896, after_share("b", 768), after_share("a", 256), share=LAST_SHARE)
-        quantize_pair("b", 896)
-        scores(0, 2, 896, 128)
-        scores(2, 2, 896, 128)
+        apply_gain(b5, at["parted_256"])
+        apply_gain(b4, at["act2"] + 2048, SHARE)
+        quantize_h(b5)
+        quantize_h(b4)
+        apply_gain(a1, at["raw01"] + EDGE)
+        apply_gain(a0, at["parted_256"], SHARE)
+        quantize_h(a1)
+        quantize_h(a0)
+        for i in (0, 1):
+            scores([i], [(0, 256), (256, 256)])
+        scores([0, 1], [(512, 256)])
+        apply_gain(a3, at["act7"])
+        apply_gain(a2, at["raw01"] + EDGE, SHARE)
+        quantize_h(a3)
+        quantize_h(a2)
+        for i in (2, 3):
+            scores([i], [(0, 256), (256, 256)])
+        scores([2, 3], [(512, 256)])
+        apply_gain(b6, at["act7"], LAST_SHARE)
+        quantize_h(b6, None, 2)
+        scores([0, 1, 2, 3], [(768, 128)])
+        apply_gain(b7, at["act6"])
+        quantize_h(b7, None, 2)
+        scores([0, 1], [(896, 128)])
+        scores([2, 3], [(896, 128)])

@@ -26,7 +26,7 @@ BANK = 512
 ROTATING_BANKS = 7
 EDGE = 64
 SHARE = 144
-FIRST_CUT = 384
+FIRST_CUT = 256
 LAST_SHARE = 48
 
 REGIONS = (
@@ -37,10 +37,8 @@ REGIONS = (
     ("wb_scales", 2048, EDGE),
     ("table", 8192, 0),
     ("raw10", 8192, 0),
-    ("gains", 2048, EDGE),
-    ("raw01", 8192, EDGE),
-    ("gain_rows", 2048, 0),
-    ("raw11", 8192, EDGE),
+    ("raw01", 8192, 0),
+    ("raw11", 8192, 0),
     ("words_a", 2048, 0),
     ("words_0", 1024, EDGE),
     ("words_512", 2048, EDGE),
@@ -87,18 +85,20 @@ def tile_list_biaff_tanh_exp_kernel(
         list_b = keep.tile([P, J // 16], U16)
         list_a = keep.tile([P, M // 16], U16)
         tab_s = tile("tab_s", [P, T], U8)
-        gain_raw = tile("gain_raw", [4, HALF], F32, at["gains"])
-        gain_rows = tile("gain_rows", [P, PACK, P], F32, at["gain_rows"])
-        blank = tile("blank", [P, 2 * P], F32)
+        gain_raw = tile("gain_raw", [4, 3 * PACK * HALF], F32, at["raw10"])
+        gain_rows = tile("gain_rows", [P, PACK, P], F32)
+        blank = tile("blank", [P, 3 * P], F32)
         ident = tile("ident", [P, P], F32)
-        planes = {"b": [tile("plane_b%d" % a, [P, J], U8) for a in range(PASSES)]}
-        planes["a"] = [tile("plane_a0", [P, M], U8, at["words_0"] + EDGE), tile("plane_a1", [P, M], U8)]
+        planes = {}
+        for key, place in ((("b", 0), None), (("b", HALF), None), (("a", 0), at["words_0"] + EDGE)):
+            planes[key] = [tile("plane0_%s%d" % key, [P, HALF], U8, place), tile("plane1_%s%d" % key, [P, HALF], U8)]
 
         nc.vector.memset(tab_s[:].bitcast(I32), 0)
-        for t, place in enumerate((at["table"] - 256, at["gains"] + 256)):
-            zeros = tile("zeros%d" % t, [P, P], F32, place)
-            nc.vector.memset(zeros[:], 0.0)
-            nc.vector.tensor_copy(gain_rows[:, t, :], zeros[:])
+        for v, vec in enumerate((sa, sb)):
+            nc.gpsimd.dma_start(gain_raw[2 * v : 2 * v + 2, 0:HALF], vec.rearrange("(g r) -> g r", g=2))
+        zeros = tile("zeros", [P, P], F32, at["table"] - 256)
+        nc.vector.memset(zeros[:], 0.0)
+        nc.vector.tensor_copy(gain_rows[:, 0, :], zeros[:])
         wb_raw_w = tile("wb_raw_w", [P, PASSES, R // 2], I32, at["wb_words"])
         nc.sync.dma_start(wb_raw_w[:], wb_words.rearrange("a p b -> p a b").bitcast(I32))
         nc.sync.dma_start(list_b[:], offs2)
@@ -109,8 +109,6 @@ def tile_list_biaff_tanh_exp_kernel(
             )
         tab_w = tile("tab_w", [P, T], I32, at["table"])
         nc.sync.dma_start(tab_w[:], tab_words[0].rearrange("p t b -> p (t b)").bitcast(I32))
-        for v, vec in enumerate((sa, sb)):
-            nc.sync.dma_start(gain_raw[2 * v : 2 * v + 2, :], vec.rearrange("(g r) -> g r", g=2))
         wb_raw_s = tile("wb_raw_s", [P, PASSES, R // 4], I32, at["wb_scales"])
         nc.vector.memset(wb_raw_s[:], 0)
         for r in range(4):
@@ -118,7 +116,7 @@ def tile_list_biaff_tanh_exp_kernel(
                 wb_raw_s[r:P:32, :, :], wb_scales[:, r:16:4, :].rearrange("a q n -> q a n").bitcast(I32)
             )
         nc.vector.memset(blank[:], 0.0)
-        nc.scalar.copy(gain_rows[:, 2:4, :].rearrange("p t c -> p (t c)"), blank[:])
+        nc.scalar.copy(gain_rows[:, 1:4, :].rearrange("p t c -> p (t c)"), blank[:])
         nc.gpsimd.affine_select(
             out=ident[:],
             in_=blank[:, 0:P],
@@ -167,7 +165,7 @@ def tile_list_biaff_tanh_exp_kernel(
                 parted[side, first + c] = runs[:, :, 2 * c :]
 
         def entry_scales(side, first, n, a):
-            return planes[side][a][:, first : first + n]
+            return planes[side, first // HALF * HALF][a][:, first % HALF : first % HALF + n]
 
         turn = [0]
 
@@ -291,7 +289,7 @@ def tile_list_biaff_tanh_exp_kernel(
         )
         nc.scalar.copy(
             gain_rows[0:4].rearrange("v t (q i) -> v t q i", i=4),
-            gain_raw[:].rearrange("v (q t i) -> v t q i", t=PACK, i=4),
+            gain_raw[:, 0:HALF].rearrange("v (q t i) -> v t q i", t=PACK, i=4),
         )
         gain_ps = psum.tile([P, P, PACK], F32, offset=4 * BANK * ROTATING_BANKS, name="gain_ps")
         for t in range(PACK):
@@ -300,11 +298,12 @@ def tile_list_biaff_tanh_exp_kernel(
         nc.scalar.copy(gain_sb[:], gain_ps[:, 0:4, :])
         load_wa("raw00", 0, (0, FIRST_CUT, HALF))
         for h in range(2):
-            gather_scales(planes["b"][0][:, HALF * h : HALF * (h + 1)], list_b[:, 32 * h : 32 * (h + 1)])
-        lift(nc.sync, "b")
+            gather_scales(planes["b", HALF * h][0][:], list_b[:, 32 * h : 32 * (h + 1)])
+        lift(nc.sync, ("b", 0))
         load_wa("raw10", 1, (0, 256, HALF))
         load_wa("raw01", 0, (HALF, R))
         load_wa("raw11", 1, (HALF, R))
+        lift(nc.sync, ("b", HALF))
         gather_words("b", 0, 256, at["words_0"])
         nc.vector.tensor_copy(
             wb_s[:].bitcast(I32).rearrange("p (u e) a q -> p u (a q) e", e=2),
@@ -322,8 +321,8 @@ def tile_list_biaff_tanh_exp_kernel(
         layer(b3, at["act3"])
 
         gather_words("b", 512, 512, at["words_512"])
-        gather_scales(planes["a"][0][:], list_a[:])
-        lift(nc.sync, "a")
+        gather_scales(planes["a", 0][0][:], list_a[:])
+        lift(nc.sync, ("a", 0))
         gather_words("a", 0, 512, at["words_a"])
         round10 = tile("round10", [P, PACK, HALF], BF16, at["round10"])
         for h in range(2):
@@ -336,7 +335,7 @@ def tile_list_biaff_tanh_exp_kernel(
                 ADD,
             )
         apply_gain(b1, at["rounded_first"])
-        apply_gain(b0, None)
+        apply_gain(b0, at["raw10"], SHARE)
         quantize_h(b1)
         part_words("b", 512, at["act0"])
         part_words("a", 0, at["act0"] + 2048)
@@ -346,7 +345,7 @@ def tile_list_biaff_tanh_exp_kernel(
         nc.scalar.copy(grouped_view(round01, 0, HALF, "t q j i"), raw_view("raw01", 0, "t q j i"))
         round11a = tile("round11a", [P, 2, HALF], BF16)
         nc.scalar.copy(grouped_view(round11a, 0, HALF, "t q j i"), raw_view("raw11", 0, "t q j i")[:, 0:2])
-        for slab, place in ((b4, at["raw01"] + EDGE), (b5, at["act5"])):
+        for slab, place in ((b4, at["raw01"]), (b5, at["act5"])):
             layer(slab, place)
 
         apply_gain(b3, at["words_512"])
@@ -367,7 +366,7 @@ def tile_list_biaff_tanh_exp_kernel(
         apply_gain(b4, at["act2"] + 2048, SHARE)
         quantize_h(b5)
         quantize_h(b4)
-        apply_gain(a1, at["raw01"] + EDGE)
+        apply_gain(a1, at["raw01"])
         apply_gain(a0, at["parted_256"], SHARE)
         quantize_h(a1)
         quantize_h(a0)
@@ -375,7 +374,7 @@ def tile_list_biaff_tanh_exp_kernel(
             scores([i], [(0, 256), (256, 256)])
         scores([0, 1], [(512, 256)])
         apply_gain(a3, at["act7"])
-        apply_gain(a2, at["raw01"] + EDGE, SHARE)
+        apply_gain(a2, at["raw01"], SHARE)
         quantize_h(a3)
         quantize_h(a2)
         for i in (2, 3):

@@ -335,7 +335,7 @@ def tile_list_biaff_tanh_exp_kernel(
                 ADD,
             )
         apply_gain(b1, at["rounded_first"])
-        apply_gain(b0, at["raw10"], SHARE)
+        apply_gain(b0, None)
         quantize_h(b1)
         part_words("b", 512, at["act0"])
         part_words("a", 0, at["act0"] + 2048)

@@ -28,6 +28,7 @@ EDGE = 64
 SHARE = 144
 FIRST_CUT = 256
 LAST_SHARE = 48
+WARM_UPS = 6
 
 REGIONS = (
     ("wb_words", 4096, 0),
@@ -287,6 +288,17 @@ def tile_list_biaff_tanh_exp_kernel(
             wb_w[:].bitcast(I32).rearrange("p t a (q w) -> p t (a q) w", w=2),
             wb_raw_w[:].rearrange("p a (q t w) -> p t (a q) w", t=PACK, w=2),
         )
+        unread = psum.tile([P, BANK], F32, offset=4 * BANK * (ROTATING_BANKS - 1), name="unread")
+        for k in range(WARM_UPS):
+            nc.tensor.matmul_mx(
+                out=unread[:],
+                lhsT=wb_w[:, 0, 0, 0:256].bitcast(FP4X4),
+                lhsT_scale=tab_s[:, 0:P],
+                rhs=wb_w[:, 1, :, :].rearrange("p a c -> p (a c)").bitcast(FP4X4),
+                rhs_scale=tab_s[:, 0:BANK],
+                start=True,
+                stop=True,
+            )
         nc.scalar.copy(
             gain_rows[0:4].rearrange("v t (q i) -> v t q i", i=4),
             gain_raw[:, 0:HALF].rearrange("v (q t i) -> v t q i", t=PACK, i=4),

@@ -28,13 +28,13 @@ EDGE = 64
 SHARE = 144
 FIRST_CUT = 256
 LAST_SHARE = 48
+FIRST_SHARE = 64
 WARM_UPS = 6
 
 REGIONS = (
     ("wb_words", 4096, 0),
     ("raw00", 8192, EDGE),
-    ("round10", 4096, 0),
-    ("words_256", 1024, EDGE),
+    ("words_256", 1024, 0),
     ("wb_scales", 2048, EDGE),
     ("table", 8192, 0),
     ("raw10", 8192, 0),
@@ -43,7 +43,8 @@ REGIONS = (
     ("words_a", 2048, 0),
     ("words_0", 1024, EDGE),
     ("words_512", 2048, EDGE),
-    ("act0", 4096, 0),
+    ("round10", 4096, 0),
+    ("act0", 5120, 0),
     ("parted_256", 4096, 0),
     ("round11a", 2048, 0),
     ("rounded_first", 2048, 0),
@@ -151,14 +152,14 @@ def tile_list_biaff_tanh_exp_kernel(
 
         words, parted = {}, {}
 
-        def gather_words(side, first, n, place):
+        def gather_words(side, first, n, place, room=0):
             offsets = (list_a if side == "a" else list_b)[:, first // 16 : (first + n) // 16]
-            both = tile("words_%s%d" % (side, first), [P, n], U32, place)
-            nc.vector.tensor_copy(both[:], tab_w[:].bitcast(U32).indirect(offsets))
+            both = tile("words_%s%d" % (side, first), [P, n + room], U32, place)[:, 0:n]
+            nc.vector.tensor_copy(both, tab_w[:].bitcast(U32).indirect(offsets))
             words[side, first] = both
 
         def part_words(side, first, place=None):
-            both = words[side, first][:]
+            both = words[side, first]
             n = both.shape[1]
             runs = tile("parted_%s%d" % (side, first), [P, PASSES, 2 * n], U8, place)
             nc.vector.tensor_copy(runs[:].bitcast(U16), both.bitcast(U16).rearrange("p (n d) -> p d n", d=PASSES))
@@ -199,10 +200,11 @@ def tile_list_biaff_tanh_exp_kernel(
 
         acts, rounded, h_codes, h_scales = {}, {}, {}, {}
 
-        def layer(slab, place, unlifted_first=False):
+        def layer(slab, place, unlifted_first=False, room=4 * SLAB):
             side, first, halves = slab
             n = SLAB // len(halves)
-            act = tile("act_%s%d_%d" % (side, first, halves[0]), [P, 2, SLAB, 2], F32, place)
+            act = tile("act_%s%d_%d" % (side, first, halves[0]), [P, room], F32, place)[:, 0 : 4 * SLAB]
+            act = act.rearrange("p (u c e) -> p u c e", u=2, e=2)
             for u in range(2):
                 z = next_bank([P, len(halves), 2, n])
                 if unlifted_first:
@@ -323,16 +325,17 @@ def tile_list_biaff_tanh_exp_kernel(
         )
         part_words("b", 0, at["wb_scales"] + EDGE)
         gather_words("b", 256, 256, at["words_256"])
+        gather_words("b", 512, 512, at["words_512"], EDGE)
         part_words("b", 256, at["parted_256"])
+        part_words("b", 512)
         round00 = tile("round00", [P, PACK, HALF], BF16)
         for c0, c1 in ((0, FIRST_CUT), (FIRST_CUT, HALF)):
             nc.scalar.copy(grouped_view(round00, c0, c1, "t q j i"), raw_view("raw00", c0, "t q j i"))
-        layer(b0, at["act0"], True)
+        layer(b0, at["act0"], True, 5 * SLAB)
         layer(b1, at["act1"])
         layer(b2, at["act2"])
         layer(b3, at["act3"])
 
-        gather_words("b", 512, 512, at["words_512"])
         gather_scales(planes["a", 0][0][:], list_a[:])
         lift(nc.sync, ("a", 0))
         gather_words("a", 0, 512, at["words_a"])
@@ -347,31 +350,31 @@ def tile_list_biaff_tanh_exp_kernel(
                 ADD,
             )
         apply_gain(b1, at["rounded_first"])
-        apply_gain(b0, None)
+        apply_gain(b0, at["raw10"], FIRST_SHARE)
         quantize_h(b1)
-        part_words("b", 512, at["act0"])
+        quantize_wa(0, 0, 0, round00, at["act0"] + 4096)
+        quantize_wa(1, 0, 0, round10, at["act0"] + 4608)
         part_words("a", 0, at["act0"] + 2048)
         quantize_h(b0)
 
         round01 = tile("round01", [P, PACK, HALF], BF16, at["parted_256"])
         nc.scalar.copy(grouped_view(round01, 0, HALF, "t q j i"), raw_view("raw01", 0, "t q j i"))
+        layer(b4, at["raw01"])
         round11a = tile("round11a", [P, 2, HALF], BF16)
         nc.scalar.copy(grouped_view(round11a, 0, HALF, "t q j i"), raw_view("raw11", 0, "t q j i")[:, 0:2])
-        for slab, place in ((b4, at["raw01"]), (b5, at["act5"])):
+        for slab, place in ((b5, at["act5"]), (a0, at["act7"]), (a2, at["act9"])):
             layer(slab, place)
 
-        apply_gain(b3, at["words_512"])
+        apply_gain(b3, at["act0"])
         apply_gain(b2, at["words_a"], SHARE)
         quantize_h(b3)
         round11b = tile("round11b", [P, 2, HALF], BF16, at["act2"] + 2048)
         nc.vector.tensor_copy(grouped_view(round11b, 0, HALF, "t q j i"), raw_view("raw11", 0, "t q j i")[:, 2:4])
-        quantize_wa(0, 0, 0, round00, at["act2"])
-        quantize_wa(1, 0, 0, round10, at["act2"] + 512)
         quantize_wa(0, 1, 0, round01, at["act2"] + 1024)
         quantize_wa(1, 1, 0, round11a, at["act2"] + 1536)
         quantize_wa(1, 1, 2, round11b, None)
         quantize_h(b2, at["parted_256"] + 2048)
-        for slab, place in ((a0, at["act7"]), (a1, at["act8"]), (a2, at["act9"]), (a3, at["act10"]), (b6, at["act6"]), (b7, at["act11"])):
+        for slab, place in ((a1, at["act8"]), (a3, at["act10"]), (b6, at["act6"]), (b7, at["act11"])):
             layer(slab, place)
 
         apply_gain(b5, at["parted_256"])

@@ -26,9 +26,7 @@ BANK = 512
 ROTATING_BANKS = 7
 EDGE = 64
 SHARE = 144
-FIRST_CUT = 256
 LAST_SHARE = 48
-FIRST_SHARE = 64
 WARM_UPS = 6
 
 REGIONS = (
@@ -44,9 +42,9 @@ REGIONS = (
     ("words_0", 1024, EDGE),
     ("words_512", 2048, EDGE),
     ("round10", 4096, 0),
-    ("act0", 5120, 0),
+    ("act0", 7168, 0),
     ("parted_256", 4096, 0),
-    ("round11a", 2048, 0),
+    ("round11", 4096, 0),
     ("rounded_first", 2048, 0),
     ("act1", 4608, 0),
     ("act2", 4096, 0),
@@ -93,7 +91,8 @@ def tile_list_biaff_tanh_exp_kernel(
         ident = tile("ident", [P, P], F32)
         planes = {}
         for key, place in ((("b", 0), None), (("b", HALF), None), (("a", 0), at["words_0"] + EDGE)):
-            planes[key] = [tile("plane0_%s%d" % key, [P, HALF], U8, place), tile("plane1_%s%d" % key, [P, HALF], U8)]
+            lifted_at = at["words_512"] + EDGE if key[0] == "a" else None
+            planes[key] = [tile("plane0_%s%d" % key, [P, HALF], U8, place), tile("plane1_%s%d" % key, [P, HALF], U8, lifted_at)]
 
         nc.vector.memset(tab_s[:].bitcast(I32), 0)
         for v, vec in enumerate((sa, sb)):
@@ -128,7 +127,7 @@ def tile_list_biaff_tanh_exp_kernel(
             pattern=[[-1, P]],
             channel_multiplier=1,
         )
-        for key in planes:
+        for key in (("b", 0), ("b", HALF)):
             nc.vector.memset(planes[key][1][:].bitcast(I32), 0)
 
         raw = {}
@@ -261,11 +260,11 @@ def tile_list_biaff_tanh_exp_kernel(
                     h_codes[side, first + c, g] = codes[:, n * k + c :]
                     h_scales[side, first + c, g] = scales[:, n * k + c :]
 
-        def scores(row_tiles, chunks):
+        def scores(row_tiles, chunks, order=(1, 0)):
             j0 = chunks[0][0]
             width = sum(n for first, n in chunks)
             y = next_bank([P, len(row_tiles), width])
-            passes = [(g, i, first, n) for g in range(2) for i in range(len(row_tiles)) for first, n in chunks]
+            passes = [(g, i, first, n) for g in order for i in range(len(row_tiles)) for first, n in chunks]
             for k, (g, i, first, n) in enumerate(passes):
                 m0 = P * row_tiles[i]
                 nc.tensor.matmul_mx(
@@ -310,11 +309,11 @@ def tile_list_biaff_tanh_exp_kernel(
             nc.tensor.transpose(gain_ps[:, :, t], gain_rows[:, t, :], ident[:])
         gain_sb = tile("gain_sb", [P, 4, PACK], F32)
         nc.scalar.copy(gain_sb[:], gain_ps[:, 0:4, :])
-        load_wa("raw00", 0, (0, FIRST_CUT, HALF))
+        load_wa("raw00", 0, (0, 256, HALF))
         for h in range(2):
             gather_scales(planes["b", HALF * h][0][:], list_b[:, 32 * h : 32 * (h + 1)])
         lift(nc.sync, ("b", 0))
-        load_wa("raw10", 1, (0, 256, HALF))
+        load_wa("raw10", 1, (0, HALF))
         load_wa("raw01", 0, (HALF, R))
         load_wa("raw11", 1, (HALF, R))
         lift(nc.sync, ("b", HALF))
@@ -329,56 +328,59 @@ def tile_list_biaff_tanh_exp_kernel(
         part_words("b", 256, at["parted_256"])
         part_words("b", 512)
         round00 = tile("round00", [P, PACK, HALF], BF16)
-        for c0, c1 in ((0, FIRST_CUT), (FIRST_CUT, HALF)):
-            nc.scalar.copy(grouped_view(round00, c0, c1, "t q j i"), raw_view("raw00", c0, "t q j i"))
-        layer(b0, at["act0"], True, 5 * SLAB)
+        nc.scalar.copy(grouped_view(round00, 0, 256, "t q j i"), raw_view("raw00", 0, "t q j i"))
+        layer(b0, at["act0"], True, 7 * SLAB)
         layer(b1, at["act1"])
         layer(b2, at["act2"])
         layer(b3, at["act3"])
 
+        nc.gpsimd.memset(planes["a", 0][1][:].bitcast(I32), 0)
         gather_scales(planes["a", 0][0][:], list_a[:])
         lift(nc.sync, ("a", 0))
         gather_words("a", 0, 512, at["words_a"])
-        round10 = tile("round10", [P, PACK, HALF], BF16, at["round10"])
-        for h in range(2):
+        round10a = tile("round10a", [P, 2, HALF], BF16, at["round10"])
+        for target, source in (
+            (grouped_view(round00, 256, HALF, "q t i j"), raw_view("raw00", 256, "q t i j")),
+            (grouped_view(round10a, 0, HALF, "q t i j"), raw_view("raw10", 0, "q t i j")[:, :, 0:2]),
+        ):
             nc.gpsimd.tensor_scalar(
-                grouped_view(round10, 256 * h, 256 * (h + 1), "q t i j"),
-                raw_view("raw10", 256 * h, "q t i j"),
+                target,
+                source,
                 1.0,
                 0.0,
                 MULT,
                 ADD,
             )
         apply_gain(b1, at["rounded_first"])
-        apply_gain(b0, at["raw10"], FIRST_SHARE)
+        apply_gain(b0, None)
         quantize_h(b1)
+        round10b = tile("round10b", [P, 2, HALF], BF16, at["act0"] + 5120)
+        nc.vector.tensor_copy(grouped_view(round10b, 0, HALF, "t q j i"), raw_view("raw10", 0, "t q j i")[:, 2:4])
         quantize_wa(0, 0, 0, round00, at["act0"] + 4096)
-        quantize_wa(1, 0, 0, round10, at["act0"] + 4608)
+        quantize_wa(1, 0, 0, round10a, at["act0"] + 4608)
+        quantize_wa(1, 0, 2, round10b, None)
         part_words("a", 0, at["act0"] + 2048)
         quantize_h(b0)
 
         round01 = tile("round01", [P, PACK, HALF], BF16, at["parted_256"])
         nc.scalar.copy(grouped_view(round01, 0, HALF, "t q j i"), raw_view("raw01", 0, "t q j i"))
         layer(b4, at["raw01"])
-        round11a = tile("round11a", [P, 2, HALF], BF16)
-        nc.scalar.copy(grouped_view(round11a, 0, HALF, "t q j i"), raw_view("raw11", 0, "t q j i")[:, 0:2])
-        for slab, place in ((b5, at["act5"]), (a0, at["act7"]), (a2, at["act9"])):
+        round11 = tile("round11", [P, PACK, HALF], BF16, at["round11"])
+        nc.scalar.copy(grouped_view(round11, 0, HALF, "t q j i"), raw_view("raw11", 0, "t q j i"))
+        for slab, place in ((b5, at["act5"]), (a0, at["act7"])):
             layer(slab, place)
 
         apply_gain(b3, at["act0"])
         apply_gain(b2, at["words_a"], SHARE)
         quantize_h(b3)
-        round11b = tile("round11b", [P, 2, HALF], BF16, at["act2"] + 2048)
-        nc.vector.tensor_copy(grouped_view(round11b, 0, HALF, "t q j i"), raw_view("raw11", 0, "t q j i")[:, 2:4])
         quantize_wa(0, 1, 0, round01, at["act2"] + 1024)
-        quantize_wa(1, 1, 0, round11a, at["act2"] + 1536)
-        quantize_wa(1, 1, 2, round11b, None)
+        quantize_wa(1, 1, 0, round11, at["act2"] + 1536)
         quantize_h(b2, at["parted_256"] + 2048)
-        for slab, place in ((a1, at["act8"]), (a3, at["act10"]), (b6, at["act6"]), (b7, at["act11"])):
+        for slab, place in ((a1, at["act8"]), (a2, at["act9"]), (a3, at["act10"]), (b6, at["act6"]), (b7, at["act11"])):
             layer(slab, place)
 
         apply_gain(b5, at["parted_256"])
-        apply_gain(b4, at["act2"] + 2048, SHARE)
+        apply_gain(b4, at["round11"], SHARE)
         quantize_h(b5)
         quantize_h(b4)
         apply_gain(a1, at["raw01"])
@@ -400,5 +402,5 @@ def tile_list_biaff_tanh_exp_kernel(
         scores([0, 1, 2, 3], [(768, 128)])
         apply_gain(b7, at["act6"])
         quantize_h(b7, None, 2)
-        scores([0, 1], [(896, 128)])
-        scores([2, 3], [(896, 128)])
+        scores([0, 1], [(896, 128)], (0, 1))
+        scores([2, 3], [(896, 128)], (0, 1))

@@ -27,6 +27,7 @@ ROTATING_BANKS = 7
 EDGE = 64
 SHARE = 144
 LAST_SHARE = 48
+FIRST_SHARE = 128
 WARM_UPS = 6
 
 REGIONS = (
@@ -41,8 +42,7 @@ REGIONS = (
     ("words_a", 2048, 0),
     ("words_0", 1024, EDGE),
     ("words_512", 2048, EDGE),
-    ("round10", 4096, 0),
-    ("act0", 7168, 0),
+    ("act0", 9216, 0),
     ("parted_256", 4096, 0),
     ("round11", 4096, 0),
     ("rounded_first", 2048, 0),
@@ -199,12 +199,14 @@ def tile_list_biaff_tanh_exp_kernel(
 
         acts, rounded, h_codes, h_scales = {}, {}, {}, {}
 
-        def layer(slab, place, unlifted_first=False, room=4 * SLAB):
+        def layer(slab, place, unlifted_first=False, room=4 * SLAB, banks=(0, 1)):
             side, first, halves = slab
             n = SLAB // len(halves)
-            act = tile("act_%s%d_%d" % (side, first, halves[0]), [P, room], F32, place)[:, 0 : 4 * SLAB]
-            act = act.rearrange("p (u c e) -> p u c e", u=2, e=2)
-            for u in range(2):
+            if slab not in acts:
+                act = tile("act_%s%d_%d" % (side, first, halves[0]), [P, room], F32, place)[:, 0 : 4 * SLAB]
+                acts[slab] = act.rearrange("p (u c e) -> p u c e", u=2, e=2)
+            act = acts[slab]
+            for u in banks:
                 z = next_bank([P, len(halves), 2, n])
                 if unlifted_first:
                     passes = [(0, e, a, e + a == 0, e + a == 2) for a in range(PASSES) for e in range(2)]
@@ -224,7 +226,6 @@ def tile_list_biaff_tanh_exp_kernel(
                 nc.scalar.activation(
                     act[:, u, :, :].rearrange("p (k n) e -> p k n e", n=n), z[:].rearrange("p k e n -> p k n e"), ACT.Tanh
                 )
-            acts[slab] = act
 
         def apply_gain(slab, place, share=0):
             side, first, halves = slab
@@ -324,12 +325,12 @@ def tile_list_biaff_tanh_exp_kernel(
         )
         part_words("b", 0, at["wb_scales"] + EDGE)
         gather_words("b", 256, 256, at["words_256"])
-        gather_words("b", 512, 512, at["words_512"], EDGE)
+        gather_words("b", 512, 512, at["words_512"])
         part_words("b", 256, at["parted_256"])
         part_words("b", 512)
         round00 = tile("round00", [P, PACK, HALF], BF16)
         nc.scalar.copy(grouped_view(round00, 0, 256, "t q j i"), raw_view("raw00", 0, "t q j i"))
-        layer(b0, at["act0"], True, 7 * SLAB)
+        layer(b0, at["act0"], True, 9 * SLAB)
         layer(b1, at["act1"])
         layer(b2, at["act2"])
         layer(b3, at["act3"])
@@ -338,27 +339,16 @@ def tile_list_biaff_tanh_exp_kernel(
         gather_scales(planes["a", 0][0][:], list_a[:])
         lift(nc.sync, ("a", 0))
         gather_words("a", 0, 512, at["words_a"])
-        round10a = tile("round10a", [P, 2, HALF], BF16, at["round10"])
-        for target, source in (
-            (grouped_view(round00, 256, HALF, "q t i j"), raw_view("raw00", 256, "q t i j")),
-            (grouped_view(round10a, 0, HALF, "q t i j"), raw_view("raw10", 0, "q t i j")[:, :, 0:2]),
-        ):
-            nc.gpsimd.tensor_scalar(
-                target,
-                source,
-                1.0,
-                0.0,
-                MULT,
-                ADD,
-            )
+        nc.gpsimd.tensor_scalar(
+            grouped_view(round00, 256, HALF, "q t i j"), raw_view("raw00", 256, "q t i j"), 1.0, 0.0, MULT, ADD
+        )
         apply_gain(b1, at["rounded_first"])
-        apply_gain(b0, None)
+        apply_gain(b0, at["raw00"] + EDGE, FIRST_SHARE)
         quantize_h(b1)
-        round10b = tile("round10b", [P, 2, HALF], BF16, at["act0"] + 5120)
-        nc.vector.tensor_copy(grouped_view(round10b, 0, HALF, "t q j i"), raw_view("raw10", 0, "t q j i")[:, 2:4])
+        round10 = tile("round10", [P, PACK, HALF], BF16, at["act0"] + 5120)
+        nc.vector.tensor_copy(grouped_view(round10, 0, HALF, "t q j i"), raw_view("raw10", 0, "t q j i"))
         quantize_wa(0, 0, 0, round00, at["act0"] + 4096)
-        quantize_wa(1, 0, 0, round10a, at["act0"] + 4608)
-        quantize_wa(1, 0, 2, round10b, None)
+        quantize_wa(1, 0, 0, round10, None)
         part_words("a", 0, at["act0"] + 2048)
         quantize_h(b0)
 
@@ -369,6 +359,7 @@ def tile_list_biaff_tanh_exp_kernel(
         nc.scalar.copy(grouped_view(round11, 0, HALF, "t q j i"), raw_view("raw11", 0, "t q j i"))
         for slab, place in ((b5, at["act5"]), (a0, at["act7"])):
             layer(slab, place)
+        layer(a2, at["act9"], banks=(0,))
 
         apply_gain(b3, at["act0"])
         apply_gain(b2, at["words_a"], SHARE)
@@ -376,7 +367,9 @@ def tile_list_biaff_tanh_exp_kernel(
         quantize_wa(0, 1, 0, round01, at["act2"] + 1024)
         quantize_wa(1, 1, 0, round11, at["act2"] + 1536)
         quantize_h(b2, at["parted_256"] + 2048)
-        for slab, place in ((a1, at["act8"]), (a2, at["act9"]), (a3, at["act10"]), (b6, at["act6"]), (b7, at["act11"])):
+        layer(a1, at["act8"])
+        layer(a2, at["act9"], banks=(1,))
+        for slab, place in ((a3, at["act10"]), (b6, at["act6"]), (b7, at["act11"])):
             layer(slab, place)
 
         apply_gain(b5, at["parted_256"])

@@ -25,9 +25,9 @@ SLAB = 256
 BANK = 512
 ROTATING_BANKS = 7
 EDGE = 64
-SHARE = 144
+SHARE = 152
 LAST_SHARE = 48
-FIRST_SHARE = 128
+FIRST_SHARE = 176
 WARM_UPS = 6
 
 REGIONS = (
@@ -227,39 +227,36 @@ def tile_list_biaff_tanh_exp_kernel(
                     act[:, u, :, :].rearrange("p (k n) e -> p k n e", n=n), z[:].rearrange("p k e n -> p k n e"), ACT.Tanh
                 )
 
-        def apply_gain(slab, place, share=0):
+        def apply_gain(slab, place, share=0, k=0):
             side, first, halves = slab
             n = SLAB // len(halves)
-            values = tile("rounded_%s%d_%d" % (side, first, halves[0]), [P, SLAB, PACK], BF16, place)
-            parts = [(nc.vector, gain_ps, g, n * k, min(n * (k + 1), SLAB - share)) for k, g in enumerate(halves)]
+            g = halves[k]
+            values = tile("rounded_%s%d_%d" % (side, first, g), [P, n, PACK], BF16, place)
+            parts = [(nc.vector, gain_ps, 0, n - share)]
             if share:
-                parts.append((nc.gpsimd, gain_sb, halves[-1], SLAB - share, SLAB))
-            for engine, gains, g, c0, c1 in parts:
+                parts.append((nc.gpsimd, gain_sb, n - share, n))
+            for engine, gains, c0, c1 in parts:
                 factor = gains[:, (0 if side == "a" else 2) + g, :].rearrange("p (u e) -> p u e", u=2)
                 engine.tensor_tensor(
                     values[:, c0:c1, :].rearrange("p n (u e) -> p n u e", u=2),
-                    acts[slab][:, :, c0:c1, :].rearrange("p u n e -> p n u e"),
+                    acts[slab][:, :, n * k + c0 : n * k + c1, :].rearrange("p u n e -> p n u e"),
                     factor.unsqueeze(1).to_broadcast([P, c1 - c0, 2, 2]),
                     MULT,
                 )
-            rounded[slab] = values
+            rounded[slab, k] = values
 
-        def quantize_h(slab, place=None, calls=1):
+        def quantize_h(slab, k=0, place=None):
             side, first, halves = slab
             n = SLAB // len(halves)
-            codes = tile("codes_%s%d_%d" % (side, first, halves[0]), [P, SLAB], U32)
-            scales = tile("scales_%s%d_%d" % (side, first, halves[0]), [P, SLAB], U8, place)
-            for c in range(0, SLAB, SLAB // calls):
-                cols = slice(c, c + SLAB // calls)
-                nc.vector.quantize_mx(
-                    out=codes[:, cols].bitcast(FP8X4),
-                    scales=scales[:, cols],
-                    in_=rounded[slab][:, cols, :].rearrange("p n t -> p (n t)"),
-                )
-            for k, g in enumerate(halves):
-                for c in range(0, n, P):
-                    h_codes[side, first + c, g] = codes[:, n * k + c :]
-                    h_scales[side, first + c, g] = scales[:, n * k + c :]
+            g = halves[k]
+            codes = tile("codes_%s%d_%d" % (side, first, g), [P, n], U32)
+            scales = tile("scales_%s%d_%d" % (side, first, g), [P, n], U8, place)
+            nc.vector.quantize_mx(
+                out=codes[:].bitcast(FP8X4), scales=scales[:], in_=rounded[slab, k][:].rearrange("p n t -> p (n t)")
+            )
+            for c in range(0, n, P):
+                h_codes[side, first + c, g] = codes[:, c:]
+                h_scales[side, first + c, g] = scales[:, c:]
 
         def scores(row_tiles, chunks, order=(1, 0)):
             j0 = chunks[0][0]
@@ -366,7 +363,7 @@ def tile_list_biaff_tanh_exp_kernel(
         quantize_h(b3)
         quantize_wa(0, 1, 0, round01, at["act2"] + 1024)
         quantize_wa(1, 1, 0, round11, at["act2"] + 1536)
-        quantize_h(b2, at["parted_256"] + 2048)
+        quantize_h(b2, 0, at["parted_256"] + 2048)
         layer(a1, at["act8"])
         layer(a2, at["act9"], banks=(1,))
         for slab, place in ((a3, at["act10"]), (b6, at["act6"]), (b7, at["act11"])):
@@ -390,10 +387,14 @@ def tile_list_biaff_tanh_exp_kernel(
         for i in (2, 3):
             scores([i], [(0, 256), (256, 256)])
         scores([2, 3], [(512, 256)])
-        apply_gain(b6, at["act7"], LAST_SHARE)
-        quantize_h(b6, None, 2)
-        scores([0, 1, 2, 3], [(768, 128)])
+        apply_gain(b6, at["act9"])
+        apply_gain(b6, at["act7"], LAST_SHARE, 1)
+        quantize_h(b6)
+        quantize_h(b6, 1)
+        scores([0, 1, 2, 3], [(768, 128)], (0, 1))
         apply_gain(b7, at["act6"])
-        quantize_h(b7, None, 2)
+        apply_gain(b7, at["act9"], LAST_SHARE, 1)
+        quantize_h(b7)
+        quantize_h(b7, 1)
         scores([0, 1], [(896, 128)], (0, 1))
         scores([2, 3], [(896, 128)], (0, 1))

from contextlib import ExitStack

import concourse.mybir as mybir

K, R, T, M, J = 1024, 1024, 2048, 512, 1024
FLOPS = 2 * K * R * (M + J) + 2 * R * M * J

F32 = mybir.dt.float32
BF16 = mybir.dt.bfloat16
I32 = mybir.dt.int32
U32 = mybir.dt.uint32
U16 = mybir.dt.uint16
U8 = mybir.dt.uint8
FP8X4 = mybir.dt.float8_e4m3fn_x4
FP4X4 = mybir.dt.float4_e2m1fn_x4
ACT = mybir.ActivationFunctionType
MULT = mybir.AluOpType.mult
ADD = mybir.AluOpType.add

P = 128
PACK = 4
PASSES = 2
HALF = 512
SLAB = 256
BANK = 512
ROTATING_BANKS = 7
EDGE = 64
SHARE = 152
LAST_SHARE = 48
FIRST_SHARE = 176
WARM_UPS = 6

REGIONS = (
    ("wb_words", 4096, 0),
    ("raw00", 8192, EDGE),
    ("words_256", 1024, 0),
    ("wb_scales", 2048, EDGE),
    ("table", 8192, 0),
    ("raw10", 8192, 0),
    ("raw01", 8192, 0),
    ("raw11", 8192, 0),
    ("words_a", 2048, 0),
    ("words_0", 1024, EDGE),
    ("words_512", 2048, EDGE),
    ("act0", 9216, 0),
    ("parted_256", 4096, 0),
    ("round11", 4096, 0),
    ("rounded_first", 2048, 0),
    ("act1", 4608, 0),
    ("act2", 4096, 0),
    ("act3", 4096, 0),
    ("act5", 4096, 0),
    ("act6", 4096, 0),
    ("act7", 4096, 0),
    ("act8", 4096, 0),
    ("act9", 4096, 0),
    ("act10", 4096, 0),
    ("act11", 4096, 0),
)


def region_starts():
    starts, top = {}, 0
    for name, size, shared in REGIONS:
        starts[name] = top - shared
        top = starts[name] + size
    return starts


def tile_list_biaff_tanh_exp_kernel(
    tc, tab_words, tab_scales, wa, wb_words, wb_scales, sa, sb, offs, offs2, out
):
    nc = tc.nc
    at = region_starts()
    with ExitStack() as ctx:
        keep = ctx.enter_context(tc.tile_pool(name="keep", bufs=1))
        mem = ctx.enter_context(tc.tile_pool(name="mem", bufs=1))
        psum = ctx.enter_context(tc.psum_pool(name="psum", bufs=1))

        def tile(name, shape, dtype, place=None):
            if place is None:
                return keep.tile(shape, dtype, name=name, align_bytes=64)
            return mem.tile(shape, dtype, name=name, align_bytes=64, offset=place)

        list_b = keep.tile([P, J // 16], U16)
        list_a = keep.tile([P, M // 16], U16)
        tab_s = tile("tab_s", [P, T], U8)
        gain_raw = tile("gain_raw", [4, 3 * PACK * HALF], F32, at["raw10"])
        gain_rows = tile("gain_rows", [P, PACK, P], F32)
        blank = tile("blank", [P, 3 * P], F32)
        ident = tile("ident", [P, P], F32)
        planes = {}
        for key, place in ((("b", 0), None), (("b", HALF), None), (("a", 0), at["words_0"] + EDGE)):
            lifted_at = at["words_512"] + EDGE if key[0] == "a" else None
            planes[key] = [tile("plane0_%s%d" % key, [P, HALF], U8, place), tile("plane1_%s%d" % key, [P, HALF], U8, lifted_at)]

        nc.vector.memset(tab_s[:].bitcast(I32), 0)
        for v, vec in enumerate((sa, sb)):
            nc.gpsimd.dma_start(gain_raw[2 * v : 2 * v + 2, 0:HALF], vec.rearrange("(g r) -> g r", g=2))
        zeros = tile("zeros", [P, P], F32, at["table"] - 256)
        nc.vector.memset(zeros[:], 0.0)
        nc.vector.tensor_copy(gain_rows[:, 0, :], zeros[:])
        wb_raw_w = tile("wb_raw_w", [P, PASSES, R // 2], I32, at["wb_words"])
        nc.sync.dma_start(wb_raw_w[:], wb_words.rearrange("a p b -> p a b").bitcast(I32))
        nc.sync.dma_start(list_b[:], offs2)
        nc.sync.dma_start(list_a[:], offs)
        for r in range(4):
            nc.sync.dma_start(
                tab_s[r:P:16, :].bitcast(I32), tab_scales[:, r:16:4, :].rearrange("a q n -> q a n").bitcast(I32)
            )
        tab_w = tile("tab_w", [P, T], I32, at["table"])
        nc.sync.dma_start(tab_w[:], tab_words[0].rearrange("p t b -> p (t b)").bitcast(I32))
        wb_raw_s = tile("wb_raw_s", [P, PASSES, R // 4], I32, at["wb_scales"])
        nc.vector.memset(wb_raw_s[:], 0)
        for r in range(4):
            nc.sync.dma_start(
                wb_raw_s[r:P:32, :, :], wb_scales[:, r:16:4, :].rearrange("a q n -> q a n").bitcast(I32)
            )
        nc.vector.memset(blank[:], 0.0)
        nc.scalar.copy(gain_rows[:, 1:4, :].rearrange("p t c -> p (t c)"), blank[:])
        nc.gpsimd.affine_select(
            out=ident[:],
            in_=blank[:, 0:P],
            compare_op=mybir.AluOpType.not_equal,
            fill=1.0,
            base=0,
            pattern=[[-1, P]],
            channel_multiplier=1,
        )
        for key in (("b", 0), ("b", HALF)):
            nc.vector.memset(planes[key][1][:].bitcast(I32), 0)

        raw = {}

        def load_wa(name, a, cuts):
            whole = tile(name, [P, PACK * HALF], F32, at[name])
            for c0, c1 in zip(cuts, cuts[1:]):
                place = PACK * (c0 - cuts[0])
                piece = whole[:, place : place + PACK * (c1 - c0)].rearrange("p (j c) -> p j c", j=PACK)
                nc.sync.dma_start(piece, wa[512 * a : 512 * (a + 1), c0:c1].rearrange("(p j) c -> p j c", j=PACK))
                raw[name, c0 - cuts[0]] = piece

        wb_w = tile("wb_w", [P, PACK, PASSES, 512], U8)
        wb_s = tile("wb_s", [P, PACK, PASSES, 256], U8)

        def gather_scales(picked, offsets):
            nc.vector.tensor_copy(picked, tab_s[:].indirect(offsets))

        def lift(queue, key):
            queue.dma_start(planes[key][1][0:112, :].bitcast(I32), planes[key][0][16:128, :].bitcast(I32))

        words, parted = {}, {}

        def gather_words(side, first, n, place, room=0):
            offsets = (list_a if side == "a" else list_b)[:, first // 16 : (first + n) // 16]
            both = tile("words_%s%d" % (side, first), [P, n + room], U32, place)[:, 0:n]
            nc.vector.tensor_copy(both, tab_w[:].bitcast(U32).indirect(offsets))
            words[side, first] = both

        def part_words(side, first, place=None):
            both = words[side, first]
            n = both.shape[1]
            runs = tile("parted_%s%d" % (side, first), [P, PASSES, 2 * n], U8, place)
            nc.vector.tensor_copy(runs[:].bitcast(U16), both.bitcast(U16).rearrange("p (n d) -> p d n", d=PASSES))
            for c in range(0, n, P):
                parted[side, first + c] = runs[:, :, 2 * c :]

        def entry_scales(side, first, n, a):
            return planes[side, first // HALF * HALF][a][:, first % HALF : first % HALF + n]

        turn = [0]

        def next_bank(shape):
            turn[0] = turn[0] + 1
            return psum.tile(shape, F32, offset=4 * BANK * ((turn[0] - 1) % ROTATING_BANKS), name="bank%d" % turn[0])

        def grouped_view(grouped, c0, c1, walk):
            return grouped[:, :, c0:c1].rearrange("p t (q i j) -> p " + walk, i=4, j=PACK)

        def raw_view(name, c0, walk):
            return raw[name, c0].rearrange("p j (q t i) -> p " + walk, t=PACK, i=4)

        wa_tiles = {}

        def quantize_wa(a, g, t0, grouped, place):
            n = grouped.shape[1] * P
            codes = tile("wa_codes_%d%d%d" % (a, g, t0), [P, n], U32)
            scales = tile("wa_scales_%d%d%d" % (a, g, t0), [P, n], U8, place)
            nc.vector.quantize_mx(
                out=codes[:].bitcast(FP8X4), scales=scales[:], in_=grouped[:].rearrange("p t c -> p (t c)")
            )
            for c in range(0, n, P):
                wa_tiles[a, g, t0 + c // P] = (codes[:, c : c + P].bitcast(FP8X4), scales[:, c : c + P])

        def weight_tile(side, a, g, t):
            if side == "b":
                return wb_w[:, t, a, 256 * g : 256 * (g + 1)].bitcast(FP4X4), wb_s[:, t, a, P * g : P * (g + 1)]
            return wa_tiles[a, g, t]

        acts, rounded, h_codes, h_scales = {}, {}, {}, {}

        def layer(slab, place, unlifted_first=False, room=4 * SLAB, banks=(0, 1)):
            side, first, halves = slab
            n = SLAB // len(halves)
            if slab not in acts:
                act = tile("act_%s%d_%d" % (side, first, halves[0]), [P, room], F32, place)[:, 0 : 4 * SLAB]
                acts[slab] = act.rearrange("p (u c e) -> p u c e", u=2, e=2)
            act = acts[slab]
            for u in banks:
                z = next_bank([P, len(halves), 2, n])
                if unlifted_first:
                    passes = [(0, e, a, e + a == 0, e + a == 2) for a in range(PASSES) for e in range(2)]
                else:
                    passes = [(k, e, a, a == 1, a == 0) for k in range(len(halves)) for e in range(2) for a in (1, 0)]
                for k, e, a, start, stop in passes:
                    codes, scales = weight_tile(side, a, halves[k], 2 * u + e)
                    nc.tensor.matmul_mx(
                        out=z[:, k, e, :],
                        lhsT=codes,
                        lhsT_scale=scales,
                        rhs=parted[side, first][:, a, 0 : 2 * n].bitcast(FP4X4),
                        rhs_scale=entry_scales(side, first, n, a),
                        start=start,
                        stop=stop,
                    )
                nc.scalar.activation(
                    act[:, u, :, :].rearrange("p (k n) e -> p k n e", n=n), z[:].rearrange("p k e n -> p k n e"), ACT.Tanh
                )

        def apply_gain(slab, place, share=0, k=0):
            side, first, halves = slab
            n = SLAB // len(halves)
            g = halves[k]
            values = tile("rounded_%s%d_%d" % (side, first, g), [P, n, PACK], BF16, place)
            parts = [(nc.vector, gain_ps, 0, n - share)]
            if share:
                parts.append((nc.gpsimd, gain_sb, n - share, n))
            for engine, gains, c0, c1 in parts:
                factor = gains[:, (0 if side == "a" else 2) + g, :].rearrange("p (u e) -> p u e", u=2)
                engine.tensor_tensor(
                    values[:, c0:c1, :].rearrange("p n (u e) -> p n u e", u=2),
                    acts[slab][:, :, n * k + c0 : n * k + c1, :].rearrange("p u n e -> p n u e"),
                    factor.unsqueeze(1).to_broadcast([P, c1 - c0, 2, 2]),
                    MULT,
                )
            rounded[slab, k] = values

        def quantize_h(slab, k=0, place=None):
            side, first, halves = slab
            n = SLAB // len(halves)
            g = halves[k]
            codes = tile("codes_%s%d_%d" % (side, first, g), [P, n], U32)
            scales = tile("scales_%s%d_%d" % (side, first, g), [P, n], U8, place)
            nc.vector.quantize_mx(
                out=codes[:].bitcast(FP8X4), scales=scales[:], in_=rounded[slab, k][:].rearrange("p n t -> p (n t)")
            )
            for c in range(0, n, P):
                h_codes[side, first + c, g] = codes[:, c:]
                h_scales[side, first + c, g] = scales[:, c:]

        def scores(row_tiles, chunks, order=(1, 0)):
            j0 = chunks[0][0]
            width = sum(n for first, n in chunks)
            y = next_bank([P, len(row_tiles), width])
            passes = [(g, i, first, n) for g in order for i in range(len(row_tiles)) for first, n in chunks]
            for k, (g, i, first, n) in enumerate(passes):
                m0 = P * row_tiles[i]
                nc.tensor.matmul_mx(
                    out=y[:, i, first - j0 : first - j0 + n],
                    lhsT=h_codes["a", m0, g][:, 0:P].bitcast(FP8X4),
                    lhsT_scale=h_scales["a", m0, g][:, 0:P],
                    rhs=h_codes["b", first, g][:, 0:n].bitcast(FP8X4),
                    rhs_scale=h_scales["b", first, g][:, 0:n],
                    start=(k == 0),
                    stop=(k == len(passes) - 1),
                )
            result = tile("result_%d_%d" % (row_tiles[0], j0), [P, len(row_tiles), width], F32)
            nc.scalar.activation(result[:], y[:], ACT.Exp, scale=0.015625)
            rows = slice(P * row_tiles[0], P * (row_tiles[-1] + 1))
            nc.sync.dma_start(out[rows, j0 : j0 + width].rearrange("(i p) j -> p i j", p=P), result[:])

        b0, b1, b2, b3, b4, b5 = [("b", first, (g,)) for first in (0, 256, 512) for g in range(2)]
        a0, a1, a2, a3 = [("a", first, (g,)) for first in (0, 256) for g in range(2)]
        b6, b7 = [("b", first, (0, 1)) for first in (768, 896)]

        nc.vector.tensor_copy(
            wb_w[:].bitcast(I32).rearrange("p t a (q w) -> p t (a q) w", w=2),
            wb_raw_w[:].rearrange("p a (q t w) -> p t (a q) w", t=PACK, w=2),
        )
        unread = psum.tile([P, BANK], F32, offset=4 * BANK * (ROTATING_BANKS - 1), name="unread")
        for k in range(WARM_UPS):
            nc.tensor.matmul_mx(
                out=unread[:],
                lhsT=wb_w[:, 0, 0, 0:256].bitcast(FP4X4),
                lhsT_scale=tab_s[:, 0:P],
                rhs=wb_w[:, 1, :, :].rearrange("p a c -> p (a c)").bitcast(FP4X4),
                rhs_scale=tab_s[:, 0:BANK],
                start=True,
                stop=True,
            )
        nc.scalar.copy(
            gain_rows[0:4].rearrange("v t (q i) -> v t q i", i=4),
            gain_raw[:, 0:HALF].rearrange("v (q t i) -> v t q i", t=PACK, i=4),
        )
        gain_ps = psum.tile([P, P, PACK], F32, offset=4 * BANK * ROTATING_BANKS, name="gain_ps")
        for t in range(PACK):
            nc.tensor.transpose(gain_ps[:, :, t], gain_rows[:, t, :], ident[:])
        gain_sb = tile("gain_sb", [P, 4, PACK], F32)
        nc.scalar.copy(gain_sb[:], gain_ps[:, 0:4, :])
        load_wa("raw00", 0, (0, 256, HALF))
        for h in range(2):
            gather_scales(planes["b", HALF * h][0][:], list_b[:, 32 * h : 32 * (h + 1)])
        lift(nc.sync, ("b", 0))
        load_wa("raw10", 1, (0, HALF))
        load_wa("raw01", 0, (HALF, R))
        load_wa("raw11", 1, (HALF, R))
        lift(nc.sync, ("b", HALF))
        gather_words("b", 0, 256, at["words_0"])
        nc.vector.tensor_copy(
            wb_s[:].bitcast(I32).rearrange("p (u e) a q -> p u (a q) e", e=2),
            wb_raw_s[:].rearrange("p a (q u e) -> p u (a q) e", u=2, e=2),
        )
        part_words("b", 0, at["wb_scales"] + EDGE)
        gather_words("b", 256, 256, at["words_256"])
        gather_words("b", 512, 512, at["words_512"])
        part_words("b", 256, at["parted_256"])
        part_words("b", 512)
        round00 = tile("round00", [P, PACK, HALF], BF16)
        nc.scalar.copy(grouped_view(round00, 0, 256, "t q j i"), raw_view("raw00", 0, "t q j i"))
        layer(b0, at["act0"], True, 9 * SLAB)
        layer(b1, at["act1"])
        layer(b2, at["act2"])
        layer(b3, at["act3"])

        nc.gpsimd.memset(planes["a", 0][1][:].bitcast(I32), 0)
        gather_scales(planes["a", 0][0][:], list_a[:])
        lift(nc.sync, ("a", 0))
        gather_words("a", 0, 512, at["words_a"])
        nc.gpsimd.tensor_scalar(
            grouped_view(round00, 256, HALF, "q t i j"), raw_view("raw00", 256, "q t i j"), 1.0, 0.0, MULT, ADD
        )
        apply_gain(b1, at["rounded_first"])
        apply_gain(b0, at["raw00"] + EDGE, FIRST_SHARE)
        quantize_h(b1)
        round10 = tile("round10", [P, PACK, HALF], BF16, at["act0"] + 5120)
        nc.vector.tensor_copy(grouped_view(round10, 0, HALF, "t q j i"), raw_view("raw10", 0, "t q j i"))
        quantize_wa(0, 0, 0, round00, at["act0"] + 4096)
        quantize_wa(1, 0, 0, round10, None)
        part_words("a", 0, at["act0"] + 2048)
        quantize_h(b0)

        round01 = tile("round01", [P, PACK, HALF], BF16, at["parted_256"])
        nc.scalar.copy(grouped_view(round01, 0, HALF, "t q j i"), raw_view("raw01", 0, "t q j i"))
        layer(b4, at["raw01"])
        round11 = tile("round11", [P, PACK, HALF], BF16, at["round11"])
        nc.scalar.copy(grouped_view(round11, 0, HALF, "t q j i"), raw_view("raw11", 0, "t q j i"))
        for slab, place in ((b5, at["act5"]), (a0, at["act7"])):
            layer(slab, place)
        layer(a2, at["act9"], banks=(0,))

        apply_gain(b3, at["act0"])
        apply_gain(b2, at["words_a"], SHARE)
        quantize_h(b3)
        quantize_wa(0, 1, 0, round01, at["act2"] + 1024)
        quantize_wa(1, 1, 0, round11, at["act2"] + 1536)
        quantize_h(b2, 0, at["parted_256"] + 2048)
        layer(a1, at["act8"])
        layer(a2, at["act9"], banks=(1,))
        for slab, place in ((a3, at["act10"]), (b6, at["act6"]), (b7, at["act11"])):
            layer(slab, place)

        apply_gain(b5, at["parted_256"])
        apply_gain(b4, at["round11"], SHARE)
        quantize_h(b5)
        quantize_h(b4)
        apply_gain(a1, at["raw01"])
        apply_gain(a0, at["parted_256"], SHARE)
        quantize_h(a1)
        quantize_h(a0)
        for i in (0, 1):
            scores([i], [(0, 256), (256, 256)])
        scores([0, 1], [(512, 256)])
        apply_gain(a3, at["act7"])
        apply_gain(a2, at["raw01"], SHARE)
        quantize_h(a3)
        quantize_h(a2)
        for i in (2, 3):
            scores([i], [(0, 256), (256, 256)])
        scores([2, 3], [(512, 256)])
        apply_gain(b6, at["act9"])
        apply_gain(b6, at["act7"], LAST_SHARE, 1)
        quantize_h(b6)
        quantize_h(b6, 1)
        scores([0, 1, 2, 3], [(768, 128)], (0, 1))
        apply_gain(b7, at["act6"])
        apply_gain(b7, at["act9"], LAST_SHARE, 1)
        quantize_h(b7)
        quantize_h(b7, 1)
        scores([0, 1], [(896, 128)], (0, 1))
        scores([2, 3], [(896, 128)], (0, 1))
